import numpy as np
import ml_dtypes


def mxq(x, axis, fmt="e4m3"):
    dtype, down = {"e4m3": (ml_dtypes.float8_e4m3fn, 7), "e5m2": (ml_dtypes.float8_e5m2, 14)}[fmt]
    v = np.moveaxis(np.asarray(x, np.float32).astype(ml_dtypes.bfloat16).astype(np.float64), axis, -1)
    blocks = v.reshape(v.shape[:-1] + (-1, 32))
    amax = np.abs(blocks).max(-1, keepdims=True)
    byte = np.maximum(np.where(amax > 0, np.frexp(amax)[1] - 1 + 127, 0) - down, 1)
    scale = np.exp2(byte - 127.0)
    codes = (blocks / scale).astype(np.float32).astype(dtype).astype(np.float64)
    return np.moveaxis((codes * scale).reshape(v.shape), -1, axis)


WIDE = False


def mx_kscale(k):
    if not WIDE:
        return np.ones(k)
    levels = np.array([10, -10, 5, -5, 0])
    if k % 512:
        return np.exp2(np.random.permutation(np.resize(levels, k // 32))).repeat(32)
    a = np.empty((k // 512, 16))
    for p in range(k // 512):
        a[p, :8] = np.random.permutation(np.resize(levels, 8))
        for g in range(8):
            far = levels[np.abs(levels - a[p, g]) >= 10]
            a[p, g + 8] = far[np.random.randint(len(far))]
    return np.exp2(a.ravel()).repeat(32)


def f64(x):
    return np.asarray(x).astype(np.float64)


def striped(idx):
    return np.tile(idx.reshape(-1, 16).T, (8, 1)).astype(np.uint16)


def unstriped(offs):
    return offs[:16].T.reshape(-1).astype(np.int64)


E2M1 = np.array([0.0, 0.5, 1.0, 1.5, 2.0, 3.0, 4.0, 6.0, -0.0, -0.5, -1.0, -1.5, -2.0, -3.0, -4.0, -6.0])


def pack_weight(w, fmt):
    k, n = w.shape
    w = f64(np.asarray(w, np.float32).astype(ml_dtypes.bfloat16)).reshape(k // 32, 32, n)
    amax = np.abs(w).max(1)
    if fmt == "e4m3":
        byte = np.frexp(amax)[1] - 1 + 127 - 7
    else:
        mant, ex = np.frexp(amax / 6.0)
        byte = np.where(mant > 0.5, ex, ex - 1) + 127
    byte = np.clip(np.where(amax > 0, byte, 1), 1, 254)
    scaled = (w * np.exp2(127.0 - byte)[:, None, :]).reshape(k, n).astype(np.float32)
    by_word = np.ascontiguousarray(scaled.reshape(k // 512, 128, 4, n).transpose(0, 1, 3, 2))
    if fmt == "e4m3":
        words = by_word.astype(ml_dtypes.float8_e4m3fn).view(np.uint8)
    else:
        c = by_word.astype(ml_dtypes.float4_e2m1fn).view(np.uint8) & 0xF
        words = (c[..., 0::2] | (c[..., 1::2] << 4)).reshape(k // 512, 128, 2 * n)
    return np.ascontiguousarray(words), np.ascontiguousarray(byte.astype(np.uint8).reshape(k // 512, 16, n))


def unpack_weight(words, scales, fmt):
    g, _, n = scales.shape
    words = np.ascontiguousarray(words).reshape(g, 128, n, -1)
    if fmt == "e4m3":
        vals = words.view(ml_dtypes.float8_e4m3fn).astype(np.float64)
    else:
        nib = np.empty((g, 128, n, 4), np.uint8)
        nib[..., 0::2] = words & 0xF
        nib[..., 1::2] = words >> 4
        vals = E2M1[nib]
    vals = vals * np.repeat(np.exp2(scales.astype(np.float64) - 127.0), 8, axis=1)[..., None]
    return vals.transpose(0, 1, 3, 2).reshape(g * 512, n)


def gelu(v):
    return 0.5 * v * (1.0 + np.tanh(np.sqrt(2.0 / np.pi) * (v + 0.044715 * v**3)))


K, H, N, T, S, P, P2 = 1536, 1024, 512, 2048, 1024, 512, 256

def setup_inputs():
    n = np.random.standard_normal
    s = mx_kscale(K)[:, None]
    u = mx_kscale(H)[:, None]
    tab_words, tab_scales = pack_weight(n((K, T)) * s, "e4m3")
    wg_words, wg_scales = pack_weight(1.5 * n((H, N)) / np.sqrt(H) / u, "e2m1")
    old_new = np.random.permutation(S)
    linked = np.random.permutation(P)
    return {
        "tab_words": tab_words, "tab_scales": tab_scales,
        "offs": striped(np.random.permutation(T)[:S]),
        "pos1": striped(old_new[:P]),
        "pos2": striped(old_new[P:2 * P]),
        "pos3": striped(linked[:P2]),
        "pos4": striped(linked[P2:2 * P2]),
        "w1": (n((K, H)) / np.sqrt(K) / s * u.T).astype(np.float32),
        "b1": (0.5 * n(H) * u[:, 0]).astype(np.float32),
        "wg_words": wg_words, "wg_scales": wg_scales,
        "wu": (1.5 * n((H, N)) / np.sqrt(H) / u).astype(np.float32),
    }

def reference(tab_words, tab_scales, offs, pos1, pos2, pos3, pos4, w1, b1, wg_words, wg_scales, wu):
    v = unpack_weight(tab_words, tab_scales, "e4m3")[:, unstriped(offs)]
    h = mxq(f64(w1), 0, "e4m3").T @ v
    h = np.maximum(h + f64(b1)[:, None], 0.0)
    z = h[:, unstriped(pos2)] - h[:, unstriped(pos1)]
    zq = mxq(z, 0, "e4m3")
    gate = unpack_weight(wg_words, wg_scales, "e2m1").T @ zq
    lin = mxq(f64(wu), 0, "e4m3").T @ zq
    y = gate / (1.0 + np.exp(-gate)) * lin
    return y[:, unstriped(pos3)] + y[:, unstriped(pos4)]

@@ -1,0 +1,258 @@
+from contextlib import ExitStack
+
+import concourse.mybir as mybir
+
+K, H, N, T, S, M, M2 = 1536, 1024, 512, 2048, 1024, 512, 256
+FLOPS = 2 * K * H * S + 2 * 2 * H * N * M
+
+F32 = mybir.dt.float32
+BF16 = mybir.dt.bfloat16
+I32 = mybir.dt.int32
+U32 = mybir.dt.uint32
+U16 = mybir.dt.uint16
+U8 = mybir.dt.uint8
+FP8X4 = mybir.dt.float8_e4m3fn_x4
+FP4X4 = mybir.dt.float4_e2m1fn_x4
+ACT = mybir.ActivationFunctionType
+ALU = mybir.AluOpType
+
+P = 128
+PACK = 4
+KP = P * PACK
+BANK = 512
+
+
+def tile_list_redline_pair_features_kernel(
+    tc, tab_words, tab_scales, offs, pos1, pos2, pos3, pos4, w1, b1, wg_words, wg_scales, wu, out
+):
+    nc = tc.nc
+    k_passes = K // KP
+    r_passes = H // KP
+    n_tiles = N // P
+
+    with ExitStack() as ctx:
+        keep = ctx.enter_context(tc.tile_pool(name="keep", bufs=1))
+        raw = ctx.enter_context(tc.tile_pool(name="raw", bufs=6))
+        stage = ctx.enter_context(tc.tile_pool(name="stage", bufs=3))
+        psum = ctx.enter_context(tc.psum_pool(name="psum", bufs=1))
+
+        def load_list(src, name):
+            t = keep.tile(list(src.shape), U16, name=name)
+            nc.sync.dma_start(t[:], src)
+            return t
+
+        warm = keep.tile([P, 8], F32, name="warm")
+        warm_out = keep.tile([P, 8], F32, name="warm_out")
+        tab_planes = keep.tile([P, T], U8, name="tab_planes", align_bytes=64)
+        nc.vector.memset(tab_planes[:].bitcast(I32), 0)
+        nc.vector.memset(warm[:], 0.0)
+        nc.scalar.activation(warm_out[:], warm[:], ACT.Silu)
+        wg_planes = keep.tile([P, r_passes * N], U8, name="wg_planes", align_bytes=64)
+        nc.vector.memset(wg_planes[:].bitcast(I32), 0)
+
+        offs_t = load_list(offs, "offs_t")
+        for q in range(4):
+            nc.sync.dma_start(
+                tab_planes[32 * q : 32 * q + 4 * k_passes, :].bitcast(I32),
+                tab_scales[:, 4 * q : 4 * q + 4, :].bitcast(I32),
+            )
+
+        tab_t = []
+        w1_raw = {}
+
+        def load_tab(a):
+            t = keep.tile([P, T], I32, name="tab%d" % a, align_bytes=64)
+            nc.sync.dma_start(t[:], tab_words[a].rearrange("p t i -> p (t i)").bitcast(I32))
+            tab_t.append(t)
+
+        def load_w1(a, b):
+            t = raw.tile([P, PACK, KP], F32, name="raw", align_bytes=64)
+            nc.sync.dma_start(
+                t[:], w1[a * KP : (a + 1) * KP, b * KP : (b + 1) * KP].rearrange("(p j) c -> p j c", j=PACK)
+            )
+            w1_raw[a, b] = t
+
+        load_tab(0)
+        load_w1(0, 0)
+        load_tab(1)
+        load_w1(1, 0)
+        load_tab(2)
+        pos1_t = load_list(pos1, "pos1_t")
+        pos2_t = load_list(pos2, "pos2_t")
+        bias = keep.tile([P, r_passes, 8], F32, name="bias")
+        nc.sync.dma_start(bias[:, :, 0:PACK], b1.rearrange("(b p t) -> p b t", b=r_passes, t=PACK))
+        load_w1(2, 0)
+        for a in range(k_passes):
+            load_w1(a, 1)
+        wu_raw = []
+        for b in range(r_passes):
+            t = raw.tile([P, PACK, N], F32, name="raw", align_bytes=64)
+            nc.sync.dma_start(t[:], wu[b * KP : (b + 1) * KP, :].rearrange("(p j) c -> p j c", j=PACK))
+            wu_raw.append(t)
+        wg_t = keep.tile([P, r_passes, 2 * N], U8, name="wg_t", align_bytes=64)
+        nc.sync.dma_start(wg_t[:].bitcast(I32), wg_words.rearrange("b p c -> p b c").bitcast(I32))
+        for q in range(4):
+            nc.sync.dma_start(
+                wg_planes[32 * q : 32 * q + 4, :].bitcast(I32).rearrange("r (b c) -> r b c", b=r_passes),
+                wg_scales[:, 4 * q : 4 * q + 4, :].rearrange("b r c -> r b c").bitcast(I32),
+            )
+        pos3_t = load_list(pos3, "pos3_t")
+        pos4_t = load_list(pos4, "pos4_t")
+
+        v_planes = keep.tile([P, S], U8, name="v_planes", align_bytes=64)
+        nc.vector.tensor_copy(v_planes[:], tab_planes[:].indirect(offs_t[:]))
+        v_words = []
+        w1_codes = {}
+        w1_planes = {}
+
+        def gather_tab(a):
+            t = keep.tile([P, S], U32, name="v%d" % a, align_bytes=64)
+            nc.vector.tensor_copy(t[:], tab_t[a][:].bitcast(U32).indirect(offs_t[:]))
+            v_words.append(t)
+
+        def cast_w1(a, b, split):
+            g = stage.tile([P, PACK, P, PACK], BF16, name="grouped", align_bytes=64)
+            dst = g[:].rearrange("p t m j -> p m j t")
+            src = w1_raw[a, b][:].rearrange("p j (m t) -> p m j t", t=PACK)
+            if split:
+                nc.vector.tensor_copy(dst[:, 0:split], src[:, 0:split])
+            nc.scalar.copy(dst[:, split:P], src[:, split:P])
+            return g
+
+        def quant(g, name):
+            codes = keep.tile([P, KP], U32, name=name + "_codes", align_bytes=64)
+            planes = keep.tile([P, KP], U8, name=name + "_planes", align_bytes=64)
+            nc.vector.quantize_mx(out=codes[:].bitcast(FP8X4), scales=planes[:], in_=g)
+            return codes, planes
+
+        def quant_w1(a, b, g):
+            w1_codes[a, b], w1_planes[a, b] = quant(g[:].rearrange("p t m j -> p (t m j)"), "w1_%d_%d" % (a, b))
+
+        def bank(i):
+            return psum.tile([P, BANK], F32, name="bank%d" % (i % 8))
+
+        h_t = {}
+
+        def make_h(b, t):
+            h = keep.tile([P, S], F32, name="h%d_%d" % (b, t), align_bytes=64)
+            cols = slice(t * P, (t + 1) * P)
+            for u in range(S // BANK):
+                acc = bank(2 * (PACK * b + t) + u)
+                js = slice(u * BANK, (u + 1) * BANK)
+                for a in range(k_passes):
+                    nc.tensor.matmul_mx(
+                        out=acc[:],
+                        lhsT=w1_codes[a, b][:, cols].bitcast(FP8X4),
+                        lhsT_scale=w1_planes[a, b][:, cols],
+                        rhs=v_words[a][:, js].bitcast(FP8X4),
+                        rhs_scale=v_planes[4 * a : P, js],
+                        start=(a == 0),
+                        stop=(a == k_passes - 1),
+                    )
+                nc.scalar.activation(h[:, js], acc[:], ACT.Relu, bias=bias[:, b, t : t + 1])
+            h_t[b, t] = h
+
+        for a in range(k_passes):
+            gather_tab(a)
+            g = cast_w1(a, 0, 88 if a == k_passes - 1 else 0)
+            quant_w1(a, 0, g)
+        for t in range(PACK):
+            make_h(0, t)
+
+        z32 = [keep.tile([P, PACK, M], F32, name="z32_%d" % b, align_bytes=64) for b in range(r_passes)]
+        old = {}
+
+        def gather_old(b, t):
+            o = stage.tile([P, M], F32, name="old", align_bytes=64)
+            nc.vector.tensor_copy(o[:], h_t[b, t][:].indirect(pos1_t[:]))
+            old[b, t] = o
+
+        def gather_new(b, t):
+            nc.vector.tensor_tensor(z32[b][:, t, :], h_t[b, t][:].indirect(pos2_t[:]), old[b, t][:], ALU.subtract)
+
+        def cast_plain(src, split):
+            g = stage.tile([P, BANK, PACK], BF16, name="grouped", align_bytes=64)
+            dst = g[:].rearrange("p (c i) j -> p c j i", i=PACK)
+            s = src[:].rearrange("p j (c i) -> p c j i", i=PACK)
+            if split:
+                nc.vector.tensor_copy(dst[:, 0:split], s[:, 0:split])
+            nc.scalar.copy(dst[:, split:P], s[:, split:P])
+            return g[:].rearrange("p c j -> p (c j)")
+
+        gather_old(0, 0)
+        for t in range(PACK):
+            if t + 1 < PACK:
+                gather_old(0, t + 1)
+            gather_new(0, t)
+            if t < k_passes:
+                quant_w1(t, 1, cast_w1(t, 1, 0))
+        for t in range(PACK):
+            make_h(1, t)
+        zq = []
+        wq = []
+        gather_old(1, 0)
+        for t in range(PACK):
+            if t + 1 < PACK:
+                gather_old(1, t + 1)
+            gather_new(1, t)
+            if t == 0:
+                zq.append(quant(cast_plain(z32[0], 0), "z0"))
+            if t in (1, 2):
+                wq.append(quant(cast_plain(wu_raw[t - 1], 0), "wu%d" % (t - 1)))
+        zq.append(quant(cast_plain(z32[1], 88), "z1"))
+
+        gates = [bank(2 * i) for i in range(n_tiles)]
+        lins = [bank(2 * i + 1) for i in range(n_tiles)]
+
+        def second(b, i):
+            cols = slice(i * P, (i + 1) * P)
+            nc.tensor.matmul_mx(
+                out=gates[i][:],
+                lhsT=wg_t[:, b, 2 * i * P : 2 * (i + 1) * P].bitcast(FP4X4),
+                lhsT_scale=wg_planes[:, b * N + i * P : b * N + (i + 1) * P],
+                rhs=zq[b][0][:].bitcast(FP8X4),
+                rhs_scale=zq[b][1][:],
+                start=(b == 0),
+                stop=(b == r_passes - 1),
+            )
+            nc.tensor.matmul_mx(
+                out=lins[i][:],
+                lhsT=wq[b][0][:, cols].bitcast(FP8X4),
+                lhsT_scale=wq[b][1][:, cols],
+                rhs=zq[b][0][:].bitcast(FP8X4),
+                rhs_scale=zq[b][1][:],
+                start=(b == 0),
+                stop=(b == r_passes - 1),
+            )
+
+        for b in range(r_passes):
+            for i in range(n_tiles):
+                second(b, i)
+
+        y_t = []
+        first = []
+
+        def make_y(i):
+            s = stage.tile([P, M], F32, name="silu", align_bytes=64)
+            nc.scalar.activation(s[:], gates[i][:], ACT.Silu)
+            y = keep.tile([P, M], F32, name="y%d" % i, align_bytes=64)
+            nc.vector.tensor_tensor(y[:], lins[i][:], s[:], ALU.mult)
+            y_t.append(y)
+
+        def pick_first(i):
+            f = stage.tile([P, M2], F32, name="first", align_bytes=64)
+            nc.vector.tensor_copy(f[:], y_t[i][:].indirect(pos3_t[:]))
+            first.append(f)
+
+        def finish(i):
+            o = keep.tile([P, M2], F32, name="o%d" % i, align_bytes=64)
+            nc.vector.tensor_tensor(o[:], y_t[i][:].indirect(pos4_t[:]), first[i][:], ALU.add)
+            nc.sync.dma_start(out[i * P : (i + 1) * P, :], o[:])
+
+        for step in range(n_tiles + 2):
+            if step < n_tiles:
+                make_y(step)
+            if 1 <= step <= n_tiles:
+                pick_first(step - 1)
+            if step >= 2:
+                finish(step - 2)

@@ -32,7 +32,6 @@ def tile_list_redline_pair_features_kernel(
 
     with ExitStack() as ctx:
         keep = ctx.enter_context(tc.tile_pool(name="keep", bufs=1))
-        raw = ctx.enter_context(tc.tile_pool(name="raw", bufs=6))
         stage = ctx.enter_context(tc.tile_pool(name="stage", bufs=3))
         psum = ctx.enter_context(tc.psum_pool(name="psum", bufs=1))
 
@@ -46,16 +45,16 @@ def tile_list_redline_pair_features_kernel(
         tab_planes = keep.tile([P, T], U8, name="tab_planes", align_bytes=64)
         nc.vector.memset(tab_planes[:].bitcast(I32), 0)
         nc.vector.memset(warm[:], 0.0)
-        nc.scalar.activation(warm_out[:], warm[:], ACT.Silu)
         wg_planes = keep.tile([P, r_passes * N], U8, name="wg_planes", align_bytes=64)
         nc.vector.memset(wg_planes[:].bitcast(I32), 0)
 
         offs_t = load_list(offs, "offs_t")
         for q in range(4):
-            nc.sync.dma_start(
+            nc.scalar.dma_start(
                 tab_planes[32 * q : 32 * q + 4 * k_passes, :].bitcast(I32),
                 tab_scales[:, 4 * q : 4 * q + 4, :].bitcast(I32),
             )
+        nc.scalar.activation(warm_out[:], warm[:], ACT.Silu)
 
         tab_t = []
         w1_raw = {}
@@ -65,28 +64,34 @@ def tile_list_redline_pair_features_kernel(
             nc.sync.dma_start(t[:], tab_words[a].rearrange("p t i -> p (t i)").bitcast(I32))
             tab_t.append(t)
 
-        def load_w1(a, b):
-            t = raw.tile([P, PACK, KP], F32, name="raw", align_bytes=64)
+        def load_w1(a, c0, width, key):
+            t = keep.tile([P, PACK, width], F32, name="raw_%d_%d" % (a, key), align_bytes=64)
             nc.sync.dma_start(
-                t[:], w1[a * KP : (a + 1) * KP, b * KP : (b + 1) * KP].rearrange("(p j) c -> p j c", j=PACK)
+                t[:], w1[a * KP : (a + 1) * KP, c0 : c0 + width].rearrange("(p j) c -> p j c", j=PACK)
             )
-            w1_raw[a, b] = t
+            w1_raw[a, key] = t
 
         load_tab(0)
-        load_w1(0, 0)
-        load_tab(1)
-        load_w1(1, 0)
-        load_tab(2)
         pos1_t = load_list(pos1, "pos1_t")
         pos2_t = load_list(pos2, "pos2_t")
-        bias = keep.tile([P, r_passes, 8], F32, name="bias")
-        nc.sync.dma_start(bias[:, :, 0:PACK], b1.rearrange("(b p t) -> p b t", b=r_passes, t=PACK))
-        load_w1(2, 0)
+        bias0 = keep.tile([P, 2, 8], F32, name="bias0", align_bytes=64)
+        b1_early = b1[0:KP].rearrange("(g q t) -> q g t", g=2, t=PACK)
+        for e in range(2):
+            nc.sync.dma_start(bias0[64 * e : 64 * (e + 1), :, 0:3], b1_early[:, :, e : e + 3])
+        load_w1(0, 0, KP // 2, 0)
+        load_tab(1)
+        load_w1(1, 0, KP // 2, 0)
+        load_tab(2)
+        load_w1(2, 0, KP // 2, 0)
         for a in range(k_passes):
-            load_w1(a, 1)
+            load_w1(a, KP // 2, KP // 2, 1)
+        bias = keep.tile([P, PACK], F32, name="bias", align_bytes=64)
+        nc.sync.dma_start(bias[:], b1[KP : 2 * KP].rearrange("(p t) -> p t", t=PACK))
+        for a in range(k_passes):
+            load_w1(a, KP, KP, 2)
         wu_raw = []
         for b in range(r_passes):
-            t = raw.tile([P, PACK, N], F32, name="raw", align_bytes=64)
+            t = keep.tile([P, PACK, N], F32, name="tab%d" % b, align_bytes=64)
             nc.sync.dma_start(t[:], wu[b * KP : (b + 1) * KP, :].rearrange("(p j) c -> p j c", j=PACK))
             wu_raw.append(t)
         wg_t = keep.tile([P, r_passes, 2 * N], U8, name="wg_t", align_bytes=64)
@@ -107,152 +112,283 @@ def tile_list_redline_pair_features_kernel(
 
         def gather_tab(a):
             t = keep.tile([P, S], U32, name="v%d" % a, align_bytes=64)
-            nc.vector.tensor_copy(t[:], tab_t[a][:].bitcast(U32).indirect(offs_t[:]))
+            if a < k_passes - 1:
+                nc.vector.tensor_copy(t[:], tab_t[a][:].bitcast(U32).indirect(offs_t[:]))
+            else:
+                for u in range(2):
+                    nc.vector.tensor_copy(
+                        t[:, u * BANK : (u + 1) * BANK],
+                        tab_t[a][:].bitcast(U32).indirect(offs_t[:, 32 * u : 32 * (u + 1)]),
+                    )
             v_words.append(t)
 
-        def cast_w1(a, b, split):
-            g = stage.tile([P, PACK, P, PACK], BF16, name="grouped", align_bytes=64)
-            dst = g[:].rearrange("p t m j -> p m j t")
-            src = w1_raw[a, b][:].rearrange("p j (m t) -> p m j t", t=PACK)
-            if split:
-                nc.vector.tensor_copy(dst[:, 0:split], src[:, 0:split])
-            nc.scalar.copy(dst[:, split:P], src[:, split:P])
+        reuse = {(1, 0, 1): "w1_2_0_0_codes", (2, 0, 1): "w1_2_0_0_planes"}
+
+        def cast_w1(a, b, d):
+            if (a, b, d) in reuse:
+                g = keep.tile([P, 2 * P * PACK], BF16, name=reuse[a, b, d], align_bytes=64)
+            else:
+                g = stage.tile([P, 2 * P * PACK], BF16, name="grouped", align_bytes=64, bufs=4)
+            if b == 0:
+                dst = g[:].rearrange("p (t q j) -> p q j t", t=PACK, j=PACK)
+                src = w1_raw[a, d][:].rearrange("p j (q t) -> p q j t", t=PACK)
+                nc.scalar.copy(dst, src)
+            else:
+                dst = g[:].rearrange("p (t m j) -> p m j t", t=2, j=PACK)
+                src = w1_raw[a, 2][:].rearrange("p j (m t) -> p m j t", t=PACK)[:, :, :, 2 * d : 2 * d + 2]
+                nc.scalar.copy(dst, src)
             return g
 
-        def quant(g, name):
-            codes = keep.tile([P, KP], U32, name=name + "_codes", align_bytes=64)
-            planes = keep.tile([P, KP], U8, name=name + "_planes", align_bytes=64)
-            nc.vector.quantize_mx(out=codes[:].bitcast(FP8X4), scales=planes[:], in_=g)
-            return codes, planes
+        def quant_w1(a, b, d, g):
+            name = "w1_%d_%d_%d" % (a, b, d)
+            codes = keep.tile([P, 2 * P], U32, name=name + "_codes", align_bytes=64)
+            planes = keep.tile([P, 2 * P], U8, name=name + "_planes", align_bytes=64)
+            nc.vector.quantize_mx(
+                out=codes[:].bitcast(FP8X4), scales=planes[:], in_=g[:]
+            )
+            w1_codes[a, b, d], w1_planes[a, b, d] = codes, planes
 
-        def quant_w1(a, b, g):
-            w1_codes[a, b], w1_planes[a, b] = quant(g[:].rearrange("p t m j -> p (t m j)"), "w1_%d_%d" % (a, b))
+        def prep_w1(a, b, d):
+            quant_w1(a, b, d, cast_w1(a, b, d))
 
         def bank(i):
             return psum.tile([P, BANK], F32, name="bank%d" % (i % 8))
 
         h_t = {}
+        acc = {}
 
-        def make_h(b, t):
-            h = keep.tile([P, S], F32, name="h%d_%d" % (b, t), align_bytes=64)
-            cols = slice(t * P, (t + 1) * P)
+        def h_pass(a, b, t):
+            d = t // 2
+            cols = slice((t % 2) * P, (t % 2 + 1) * P)
             for u in range(S // BANK):
-                acc = bank(2 * (PACK * b + t) + u)
+                if a == 0:
+                    acc[b, t, u] = bank(2 * t + u)
                 js = slice(u * BANK, (u + 1) * BANK)
-                for a in range(k_passes):
-                    nc.tensor.matmul_mx(
-                        out=acc[:],
-                        lhsT=w1_codes[a, b][:, cols].bitcast(FP8X4),
-                        lhsT_scale=w1_planes[a, b][:, cols],
-                        rhs=v_words[a][:, js].bitcast(FP8X4),
-                        rhs_scale=v_planes[4 * a : P, js],
-                        start=(a == 0),
-                        stop=(a == k_passes - 1),
-                    )
-                nc.scalar.activation(h[:, js], acc[:], ACT.Relu, bias=bias[:, b, t : t + 1])
+                nc.tensor.matmul_mx(
+                    out=acc[b, t, u][:],
+                    lhsT=w1_codes[a, b, d][:, cols].bitcast(FP8X4),
+                    lhsT_scale=w1_planes[a, b, d][:, cols],
+                    rhs=v_words[a][:, js].bitcast(FP8X4),
+                    rhs_scale=v_planes[4 * a : P, js],
+                    start=(a == 0),
+                    stop=(a == k_passes - 1),
+                )
+
+        def relu(b, t):
+            h = keep.tile([P, S], F32, name="h%d_%d" % (b, t), align_bytes=64)
+            col = bias[:, t : t + 1] if b else bias0[:, t // 2, 2 * (t % 2) : 2 * (t % 2) + 1]
+            for u in range(S // BANK):
+                js = slice(u * BANK, (u + 1) * BANK)
+                if (b, t, u) == (0, 0, 1):
+                    nc.vector.tensor_scalar(h[:, js], acc[b, t, u][:], col, 0.0, ALU.add, ALU.max)
+                else:
+                    nc.scalar.activation(h[:, js], acc[b, t, u][:], ACT.Relu, bias=col)
             h_t[b, t] = h
+
+        MH = M // 2
+        z32 = {}
+        z_early = keep.tile([P, PACK, M], F32, name="z32_0", align_bytes=64)
+        for e in range(2):
+            z32[0, e] = z_early[:, :, e * MH : (e + 1) * MH]
+        z_tile = {}
+        z_late = keep.tile([P, 2 * PACK - 1, MH], F32, name="z32_1", align_bytes=64)
+        z32[1, 0] = z_late[:, PACK - 1 : 2 * PACK - 1, :]
+        z32[1, 1] = z_late[:, 0:PACK, :]
+
+        def pick_old(b, t, e, o):
+            nc.vector.tensor_copy(o, h_t[b, t][:].indirect(pos1_t[:, 16 * e : 16 * (e + 1)]))
+
+        def pick_new(b, t, e, o):
+            dst = z32[b, e][:, t, :] if b else z_tile[t][:, e * MH : (e + 1) * MH]
+            nc.vector.tensor_tensor(
+                dst, h_t[b, t][:].indirect(pos2_t[:, 16 * e : 16 * (e + 1)]), o, ALU.subtract
+            )
+
+        def diff(b, t):
+            if b == 0:
+                z_tile[t] = keep.tile([P, M], F32, name="z_tile%d" % t if t else "raw_1_1", align_bytes=64)
+            old = []
+            for e in range(2):
+                o = stage.tile([P, MH], F32, name="old", align_bytes=64)
+                pick_old(b, t, e, o[:])
+                old.append(o)
+            for e in range(2):
+                pick_new(b, t, e, old[e][:])
+            if b == 0:
+                g, u = divmod(t, 2)
+                for e in range(2):
+                    nc.sync.dma_start(
+                        z_early[64 * g : 64 * (g + 1), 2 * u + e, :], z_tile[t][64 * e : 64 * (e + 1), :]
+                    )
+
+        def cast_plain(src, eng, tag):
+            if tag:
+                g = keep.tile([P, MH * PACK], BF16, name=tag, align_bytes=64)
+            else:
+                g = stage.tile([P, MH * PACK], BF16, name="grouped", align_bytes=64, bufs=4)
+            dst = g[:].rearrange("p (c i j) -> p c j i", i=PACK, j=PACK)
+            s = src.rearrange("p j (c i) -> p c j i", i=PACK)
+            if eng == "v":
+                nc.vector.tensor_copy(dst, s)
+            else:
+                nc.scalar.copy(dst, s)
+            return g[:]
+
+        def codes_planes(name):
+            codes = keep.tile([P, KP], U32, name=name + "_codes", align_bytes=64)
+            planes = keep.tile([P, KP], U8, name=name + "_planes", align_bytes=64)
+            return codes, planes
+
+        def quant_half(g, dst, e):
+            cols = slice(e * MH, (e + 1) * MH)
+            nc.vector.quantize_mx(out=dst[0][:, cols].bitcast(FP8X4), scales=dst[1][:, cols], in_=g)
+
+        zq = [codes_planes("z%d" % b) for b in range(r_passes)]
+        wq = [codes_planes("wu%d" % b) for b in range(r_passes)]
+
+        def prep_wu(b, e):
+            quant_half(cast_plain(wu_raw[b][:, :, e * MH : (e + 1) * MH], "s", ""), wq[b], e)
 
         for a in range(k_passes):
             gather_tab(a)
-            g = cast_w1(a, 0, 88 if a == k_passes - 1 else 0)
-            quant_w1(a, 0, g)
-        for t in range(PACK):
-            make_h(0, t)
+            prep_w1(a, 0, 0)
+            h_pass(a, 0, 0)
+            h_pass(a, 0, 1)
+        prep_w1(0, 0, 1)
+        relu(0, 0)
+        prep_w1(1, 0, 1)
+        diff(0, 0)
+        prep_w1(2, 0, 1)
+        for a in range(k_passes):
+            h_pass(a, 0, 2)
+            h_pass(a, 0, 3)
+        relu(0, 1)
+        diff(0, 1)
+        prep_w1(0, 1, 0)
+        prep_w1(1, 1, 0)
+        relu(0, 2)
+        diff(0, 2)
+        prep_w1(2, 1, 0)
+        for a in range(k_passes):
+            h_pass(a, 1, 0)
+            h_pass(a, 1, 1)
+        prep_w1(0, 1, 1)
+        relu(0, 3)
+        diff(0, 3)
+        prep_w1(1, 1, 1)
+        prep_w1(2, 1, 1)
+        for a in range(k_passes):
+            h_pass(a, 1, 2)
+            h_pass(a, 1, 3)
+        relu(1, 0)
+        diff(1, 0)
+        prep_wu(0, 0)
+        relu(1, 1)
+        diff(1, 1)
+        prep_wu(0, 1)
+        quant_half(cast_plain(z32[0, 0], "s", "v2"), zq[0], 0)
+        relu(1, 2)
+        relu(1, 3)
+        late_old = keep.tile([P, MH], F32, name="bias", align_bytes=64)
+        last_old = keep.tile([P, MH], F32, name="last_old", align_bytes=64)
+        pick_old(1, 2, 0, late_old[:])
+        pick_old(1, 3, 0, last_old[:])
+        pick_new(1, 2, 0, late_old[:])
+        pick_new(1, 3, 0, last_old[:])
+        quant_half(cast_plain(z32[0, 1], "s", "v1"), zq[0], 1)
+        end_old = keep.tile([P, 2, MH], F32, name="z32_0", align_bytes=64)
 
-        z32 = [keep.tile([P, PACK, M], F32, name="z32_%d" % b, align_bytes=64) for b in range(r_passes)]
-        old = {}
+        gates = {}
+        lins = {}
 
-        def gather_old(b, t):
-            o = stage.tile([P, M], F32, name="old", align_bytes=64)
-            nc.vector.tensor_copy(o[:], h_t[b, t][:].indirect(pos1_t[:]))
-            old[b, t] = o
+        def second(b, e, pair):
+            if b == 0:
+                gates[e, pair] = bank(4 * e + 2 * pair)
+                lins[e, pair] = bank(4 * e + 2 * pair + 1)
+            for ii in range(2):
+                i = 2 * pair + ii
+                for q in range(2):
+                    ms = slice(e * MH + q * P, e * MH + (q + 1) * P)
+                    nc.tensor.matmul_mx(
+                        out=gates[e, pair][:, ii * MH + q * P : ii * MH + (q + 1) * P],
+                        lhsT=wg_t[:, b, 2 * i * P : 2 * (i + 1) * P].bitcast(FP4X4),
+                        lhsT_scale=wg_planes[:, b * N + i * P : b * N + (i + 1) * P],
+                        rhs=zq[b][0][:, ms].bitcast(FP8X4),
+                        rhs_scale=zq[b][1][:, ms],
+                        start=(b == 0 and ii == 0 and q == 0),
+                        stop=(b == r_passes - 1 and ii == 1 and q == 1),
+                    )
+            for ii in range(2):
+                i = 2 * pair + ii
+                cols = slice(i * P, (i + 1) * P)
+                ms = slice(e * MH, (e + 1) * MH)
+                nc.tensor.matmul_mx(
+                    out=lins[e, pair][:, ii * MH : (ii + 1) * MH],
+                    lhsT=wq[b][0][:, cols].bitcast(FP8X4),
+                    lhsT_scale=wq[b][1][:, cols],
+                    rhs=zq[b][0][:, ms].bitcast(FP8X4),
+                    rhs_scale=zq[b][1][:, ms],
+                    start=(b == 0 and ii == 0),
+                    stop=(b == r_passes - 1 and ii == 1),
+                )
 
-        def gather_new(b, t):
-            nc.vector.tensor_tensor(z32[b][:, t, :], h_t[b, t][:].indirect(pos2_t[:]), old[b, t][:], ALU.subtract)
+        for e in range(2):
+            for pair in range(2):
+                second(0, e, pair)
 
-        def cast_plain(src, split):
-            g = stage.tile([P, BANK, PACK], BF16, name="grouped", align_bytes=64)
-            dst = g[:].rearrange("p (c i) j -> p c j i", i=PACK)
-            s = src[:].rearrange("p j (c i) -> p c j i", i=PACK)
-            if split:
-                nc.vector.tensor_copy(dst[:, 0:split], s[:, 0:split])
-            nc.scalar.copy(dst[:, split:P], s[:, split:P])
-            return g[:].rearrange("p c j -> p (c j)")
+        pick_old(1, 2, 1, end_old[:, 0, :])
+        pick_old(1, 3, 1, end_old[:, 1, :])
+        pick_new(1, 2, 1, end_old[:, 0, :])
+        prep_wu(1, 0)
+        prep_wu(1, 1)
+        quant_half(cast_plain(z32[1, 0], "s", ""), zq[1], 0)
+        pick_new(1, 3, 1, end_old[:, 1, :])
+        for pair in range(2):
+            second(1, 0, pair)
+        gb = keep.tile([P, MH, PACK], BF16, name="z1_grouped1", align_bytes=64)
+        dst = gb[:].rearrange("p (c i) j -> p c j i", i=PACK)
+        src = z32[1, 1].rearrange("p j (c i) -> p c j i", i=PACK)
+        nc.vector.tensor_copy(dst[:, 0:44], src[:, 0:44])
+        nc.scalar.copy(dst[:, 44:64], src[:, 44:64])
+        quant_half(gb[:].rearrange("p c j -> p (c j)"), zq[1], 1)
+        for pair in range(2):
+            second(1, 1, pair)
 
-        gather_old(0, 0)
-        for t in range(PACK):
-            if t + 1 < PACK:
-                gather_old(0, t + 1)
-            gather_new(0, t)
-            if t < k_passes:
-                quant_w1(t, 1, cast_w1(t, 1, 0))
-        for t in range(PACK):
-            make_h(1, t)
-        zq = []
-        wq = []
-        gather_old(1, 0)
-        for t in range(PACK):
-            if t + 1 < PACK:
-                gather_old(1, t + 1)
-            gather_new(1, t)
-            if t == 0:
-                zq.append(quant(cast_plain(z32[0], 0), "z0"))
-            if t in (1, 2):
-                wq.append(quant(cast_plain(wu_raw[t - 1], 0), "wu%d" % (t - 1)))
-        zq.append(quant(cast_plain(z32[1], 88), "z1"))
+        y_t = [keep.tile([P, M], F32, name="y%d" % i, align_bytes=64) for i in range(n_tiles)]
+        silu = {}
+        first = {}
 
-        gates = [bank(2 * i) for i in range(n_tiles)]
-        lins = [bank(2 * i + 1) for i in range(n_tiles)]
+        def make_silu(e, pair):
+            s = keep.tile([P, M], F32, name="silu%d_%d" % (e, pair), align_bytes=64)
+            nc.scalar.activation(s[:], gates[e, pair][:], ACT.Silu)
+            silu[e, pair] = s
 
-        def second(b, i):
-            cols = slice(i * P, (i + 1) * P)
-            nc.tensor.matmul_mx(
-                out=gates[i][:],
-                lhsT=wg_t[:, b, 2 * i * P : 2 * (i + 1) * P].bitcast(FP4X4),
-                lhsT_scale=wg_planes[:, b * N + i * P : b * N + (i + 1) * P],
-                rhs=zq[b][0][:].bitcast(FP8X4),
-                rhs_scale=zq[b][1][:],
-                start=(b == 0),
-                stop=(b == r_passes - 1),
+        def make_y(e, i):
+            cs = slice((i % 2) * MH, (i % 2 + 1) * MH)
+            nc.vector.tensor_tensor(
+                y_t[i][:, e * MH : (e + 1) * MH], lins[e, i // 2][:, cs], silu[e, i // 2][:, cs], ALU.mult
             )
-            nc.tensor.matmul_mx(
-                out=lins[i][:],
-                lhsT=wq[b][0][:, cols].bitcast(FP8X4),
-                lhsT_scale=wq[b][1][:, cols],
-                rhs=zq[b][0][:].bitcast(FP8X4),
-                rhs_scale=zq[b][1][:],
-                start=(b == 0),
-                stop=(b == r_passes - 1),
-            )
-
-        for b in range(r_passes):
-            for i in range(n_tiles):
-                second(b, i)
-
-        y_t = []
-        first = []
-
-        def make_y(i):
-            s = stage.tile([P, M], F32, name="silu", align_bytes=64)
-            nc.scalar.activation(s[:], gates[i][:], ACT.Silu)
-            y = keep.tile([P, M], F32, name="y%d" % i, align_bytes=64)
-            nc.vector.tensor_tensor(y[:], lins[i][:], s[:], ALU.mult)
-            y_t.append(y)
 
         def pick_first(i):
             f = stage.tile([P, M2], F32, name="first", align_bytes=64)
             nc.vector.tensor_copy(f[:], y_t[i][:].indirect(pos3_t[:]))
-            first.append(f)
+            first[i] = f
 
         def finish(i):
             o = keep.tile([P, M2], F32, name="o%d" % i, align_bytes=64)
             nc.vector.tensor_tensor(o[:], y_t[i][:].indirect(pos4_t[:]), first[i][:], ALU.add)
             nc.sync.dma_start(out[i * P : (i + 1) * P, :], o[:])
 
-        for step in range(n_tiles + 2):
+        for e in range(2):
+            for pair in range(2):
+                make_silu(e, pair)
+        for i in range(n_tiles):
+            make_y(0, i)
+        make_y(1, 0)
+        for step in range(1, n_tiles + 2):
             if step < n_tiles:
-                make_y(step)
-            if 1 <= step <= n_tiles:
+                make_y(1, step)
+            if step <= n_tiles:
                 pick_first(step - 1)
             if step >= 2:
                 finish(step - 2)

@@ -48,16 +48,9 @@ def tile_list_redline_pair_features_kernel(
         wg_planes = keep.tile([P, r_passes * N], U8, name="wg_planes", align_bytes=64)
         nc.vector.memset(wg_planes[:].bitcast(I32), 0)
 
-        offs_t = load_list(offs, "offs_t")
-        for q in range(4):
-            nc.scalar.dma_start(
-                tab_planes[32 * q : 32 * q + 4 * k_passes, :].bitcast(I32),
-                tab_scales[:, 4 * q : 4 * q + 4, :].bitcast(I32),
-            )
-        nc.scalar.activation(warm_out[:], warm[:], ACT.Silu)
-
         tab_t = []
         w1_raw = {}
+        wu_raw = []
 
         def load_tab(a):
             t = keep.tile([P, T], I32, name="tab%d" % a, align_bytes=64)
@@ -71,41 +64,67 @@ def tile_list_redline_pair_features_kernel(
             )
             w1_raw[a, key] = t
 
+        def load_wu(b):
+            t = keep.tile([P, PACK, N], F32, name="tab%d" % b, align_bytes=64)
+            nc.sync.dma_start(t[:], wu[b * KP : (b + 1) * KP, :].rearrange("(p j) c -> p j c", j=PACK))
+            wu_raw.append(t)
+
+        def load_wg_planes(q):
+            nc.sync.dma_start(
+                wg_planes[32 * q : 32 * q + 4, :].bitcast(I32).rearrange("r (b c) -> r b c", b=r_passes),
+                wg_scales[:, 4 * q : 4 * q + 4, :].rearrange("b r c -> r b c").bitcast(I32),
+            )
+
+        b1_early = b1[0:KP].rearrange("(g q t) -> q g t", g=2, t=PACK)
+        bias_first = keep.tile([P, 8], F32, name="bias_first", align_bytes=64)
+        bias_cols = {(0, 0): bias_first[:, 0:1], (0, 1): bias_first[:, 2:3]}
+
+        def load_bias_first(e):
+            nc.sync.dma_start(bias_first[64 * e : 64 * (e + 1), 0:3], b1_early[:, 0, e : e + 3])
+
+        def load_bias_tile(u):
+            col = keep.tile([P, 1], F32, name="bias_tile%d" % u, align_bytes=64)
+            for e in range(2):
+                nc.sync.dma_start(col[64 * e : 64 * (e + 1), :], b1_early[:, 1, 2 * u + e : 2 * u + e + 1])
+            bias_cols[0, 2 + u] = col[:]
+
+        for q in range(4):
+            nc.scalar.dma_start(
+                tab_planes[32 * q : 32 * q + 4 * k_passes, :].bitcast(I32),
+                tab_scales[:, 4 * q : 4 * q + 4, :].bitcast(I32),
+            )
+        nc.scalar.activation(warm_out[:], warm[:], ACT.Silu)
+        offs_t = load_list(offs, "offs_t")
         load_tab(0)
         pos1_t = load_list(pos1, "pos1_t")
         pos2_t = load_list(pos2, "pos2_t")
-        bias0 = keep.tile([P, 2, 8], F32, name="bias0", align_bytes=64)
-        b1_early = b1[0:KP].rearrange("(g q t) -> q g t", g=2, t=PACK)
-        for e in range(2):
-            nc.sync.dma_start(bias0[64 * e : 64 * (e + 1), :, 0:3], b1_early[:, :, e : e + 3])
+        load_bias_first(0)
         load_w1(0, 0, KP // 2, 0)
         load_tab(1)
+        load_bias_first(1)
         load_w1(1, 0, KP // 2, 0)
         load_tab(2)
         load_w1(2, 0, KP // 2, 0)
         for a in range(k_passes):
             load_w1(a, KP // 2, KP // 2, 1)
+            load_wg_planes(a)
+        load_w1(0, KP, KP, 2)
         bias = keep.tile([P, PACK], F32, name="bias", align_bytes=64)
         nc.sync.dma_start(bias[:], b1[KP : 2 * KP].rearrange("(p t) -> p t", t=PACK))
-        for a in range(k_passes):
-            load_w1(a, KP, KP, 2)
-        wu_raw = []
-        for b in range(r_passes):
-            t = keep.tile([P, PACK, N], F32, name="tab%d" % b, align_bytes=64)
-            nc.sync.dma_start(t[:], wu[b * KP : (b + 1) * KP, :].rearrange("(p j) c -> p j c", j=PACK))
-            wu_raw.append(t)
+        for t in range(PACK):
+            bias_cols[1, t] = bias[:, t : t + 1]
+        load_w1(1, KP, KP, 2)
+        load_bias_tile(0)
+        load_w1(2, KP, KP, 2)
+        load_bias_tile(1)
+        load_wu(0)
+        load_wg_planes(3)
+        pos3_t = load_list(pos3, "pos3_t")
+        load_wu(1)
+        pos4_t = load_list(pos4, "pos4_t")
         wg_t = keep.tile([P, r_passes, 2 * N], U8, name="wg_t", align_bytes=64)
         nc.sync.dma_start(wg_t[:].bitcast(I32), wg_words.rearrange("b p c -> p b c").bitcast(I32))
-        for q in range(4):
-            nc.sync.dma_start(
-                wg_planes[32 * q : 32 * q + 4, :].bitcast(I32).rearrange("r (b c) -> r b c", b=r_passes),
-                wg_scales[:, 4 * q : 4 * q + 4, :].rearrange("b r c -> r b c").bitcast(I32),
-            )
-        pos3_t = load_list(pos3, "pos3_t")
-        pos4_t = load_list(pos4, "pos4_t")
 
-        v_planes = keep.tile([P, S], U8, name="v_planes", align_bytes=64)
-        nc.vector.tensor_copy(v_planes[:], tab_planes[:].indirect(offs_t[:]))
         v_words = []
         w1_codes = {}
         w1_planes = {}
@@ -176,7 +195,7 @@ def tile_list_redline_pair_features_kernel(
 
         def relu(b, t):
             h = keep.tile([P, S], F32, name="h%d_%d" % (b, t), align_bytes=64)
-            col = bias[:, t : t + 1] if b else bias0[:, t // 2, 2 * (t % 2) : 2 * (t % 2) + 1]
+            col = bias_cols[b, t]
             for u in range(S // BANK):
                 js = slice(u * BANK, (u + 1) * BANK)
                 if (b, t, u) == (0, 0, 1):
@@ -246,11 +265,19 @@ def tile_list_redline_pair_features_kernel(
         zq = [codes_planes("z%d" % b) for b in range(r_passes)]
         wq = [codes_planes("wu%d" % b) for b in range(r_passes)]
 
-        def prep_wu(b, e):
-            quant_half(cast_plain(wu_raw[b][:, :, e * MH : (e + 1) * MH], "s", ""), wq[b], e)
+        def prep_wu(b, tag):
+            g = keep.tile([P, N * PACK], BF16, name=tag, align_bytes=64)
+            nc.scalar.copy(
+                g[:].rearrange("p (c i j) -> p c j i", i=PACK, j=PACK),
+                wu_raw[b][:].rearrange("p j (c i) -> p c j i", i=PACK),
+            )
+            nc.vector.quantize_mx(out=wq[b][0][:].bitcast(FP8X4), scales=wq[b][1][:], in_=g[:])
 
         for a in range(k_passes):
             gather_tab(a)
+            if a == 0:
+                v_planes = keep.tile([P, S], U8, name="v_planes", align_bytes=64)
+                nc.vector.tensor_copy(v_planes[:], tab_planes[:].indirect(offs_t[:]))
             prep_w1(a, 0, 0)
             h_pass(a, 0, 0)
             h_pass(a, 0, 1)
@@ -265,28 +292,26 @@ def tile_list_redline_pair_features_kernel(
         relu(0, 1)
         diff(0, 1)
         prep_w1(0, 1, 0)
+        prep_w1(0, 1, 1)
         prep_w1(1, 1, 0)
         relu(0, 2)
         diff(0, 2)
+        prep_w1(1, 1, 1)
         prep_w1(2, 1, 0)
         for a in range(k_passes):
             h_pass(a, 1, 0)
             h_pass(a, 1, 1)
-        prep_w1(0, 1, 1)
         relu(0, 3)
         diff(0, 3)
-        prep_w1(1, 1, 1)
         prep_w1(2, 1, 1)
         for a in range(k_passes):
             h_pass(a, 1, 2)
             h_pass(a, 1, 3)
         relu(1, 0)
         diff(1, 0)
-        prep_wu(0, 0)
         relu(1, 1)
         diff(1, 1)
-        prep_wu(0, 1)
-        quant_half(cast_plain(z32[0, 0], "s", "v2"), zq[0], 0)
+        prep_wu(0, "w1_2_1_0_planes")
         relu(1, 2)
         relu(1, 3)
         late_old = keep.tile([P, MH], F32, name="bias", align_bytes=64)
@@ -295,8 +320,8 @@ def tile_list_redline_pair_features_kernel(
         pick_old(1, 3, 0, last_old[:])
         pick_new(1, 2, 0, late_old[:])
         pick_new(1, 3, 0, last_old[:])
-        quant_half(cast_plain(z32[0, 1], "s", "v1"), zq[0], 1)
-        end_old = keep.tile([P, 2, MH], F32, name="z32_0", align_bytes=64)
+        quant_half(cast_plain(z32[0, 0], "s", "v2"), zq[0], 0)
+        end_old = keep.tile([P, 2, MH], F32, name="v2", align_bytes=64)
 
         gates = {}
         lins = {}
@@ -332,19 +357,20 @@ def tile_list_redline_pair_features_kernel(
                     stop=(b == r_passes - 1 and ii == 1),
                 )
 
-        for e in range(2):
-            for pair in range(2):
-                second(0, e, pair)
+        for pair in range(2):
+            second(0, 0, pair)
 
         pick_old(1, 2, 1, end_old[:, 0, :])
         pick_old(1, 3, 1, end_old[:, 1, :])
+        prep_wu(1, "w1_2_1_1_planes")
         pick_new(1, 2, 1, end_old[:, 0, :])
-        prep_wu(1, 0)
-        prep_wu(1, 1)
         quant_half(cast_plain(z32[1, 0], "s", ""), zq[1], 0)
         pick_new(1, 3, 1, end_old[:, 1, :])
         for pair in range(2):
             second(1, 0, pair)
+        quant_half(cast_plain(z32[0, 1], "s", "w1_2_1_1_planes"), zq[0], 1)
+        for pair in range(2):
+            second(0, 1, pair)
         gb = keep.tile([P, MH, PACK], BF16, name="z1_grouped1", align_bytes=64)
         dst = gb[:].rearrange("p (c i) j -> p c j i", i=PACK)
         src = z32[1, 1].rearrange("p j (c i) -> p c j i", i=PACK)

@@ -17,404 +17,360 @@ ACT = mybir.ActivationFunctionType
 ALU = mybir.AluOpType
 
 P = 128
+SIDE = P // 2
+QUADRANT = 32
+PLANE_ROWS = 4
 PACK = 4
-KP = P * PACK
+PASS = P * PACK
 BANK = 512
+LIST_ROWS = 16
+ALIGN = 64
+K_PASSES = K // PASS
+R_PASSES = H // PASS
+LAST = K_PASSES - 1
+PAIR_COLS = 2 * P
+MH = M // 2
+N_TILES = N // P
 
 
 def tile_list_redline_pair_features_kernel(
     tc, tab_words, tab_scales, offs, pos1, pos2, pos3, pos4, w1, b1, wg_words, wg_scales, wu, out
 ):
     nc = tc.nc
-    k_passes = K // KP
-    r_passes = H // KP
-    n_tiles = N // P
 
     with ExitStack() as ctx:
         keep = ctx.enter_context(tc.tile_pool(name="keep", bufs=1))
         stage = ctx.enter_context(tc.tile_pool(name="stage", bufs=3))
         psum = ctx.enter_context(tc.psum_pool(name="psum", bufs=1))
 
-        def load_list(src, name):
-            t = keep.tile(list(src.shape), U16, name=name)
-            nc.sync.dma_start(t[:], src)
-            return t
+        def held(shape, dtype, slot):
+            return keep.tile(shape, dtype, name=slot, align_bytes=ALIGN)
 
-        warm = keep.tile([P, 8], F32, name="warm")
-        warm_out = keep.tile([P, 8], F32, name="warm_out")
-        tab_planes = keep.tile([P, T], U8, name="tab_planes", align_bytes=64)
+        def bank(index):
+            return psum.tile([P, BANK], F32, name="bank%d" % index)
+
+        tab_planes = held([P, T], U8, "tab_planes")
         nc.vector.memset(tab_planes[:].bitcast(I32), 0)
-        nc.vector.memset(warm[:], 0.0)
-        wg_planes = keep.tile([P, r_passes * N], U8, name="wg_planes", align_bytes=64)
+        wg_planes = held([P, R_PASSES * N], U8, "wg_planes")
         nc.vector.memset(wg_planes[:].bitcast(I32), 0)
 
-        tab_t = []
-        w1_raw = {}
-        wu_raw = []
+        tab, w1_raw, wu_raw, bias_col = {}, {}, {}, {}
+
+        def load_list(src, name):
+            offsets = keep.tile(list(src.shape), U16, name=name)
+            nc.sync.dma_start(offsets[:], src)
+            return offsets
 
         def load_tab(a):
-            t = keep.tile([P, T], I32, name="tab%d" % a, align_bytes=64)
-            nc.sync.dma_start(t[:], tab_words[a].rearrange("p t i -> p (t i)").bitcast(I32))
-            tab_t.append(t)
+            tab[a] = held([P, T], I32, "tab%d" % a)
+            nc.sync.dma_start(tab[a][:], tab_words[a].rearrange("p c j -> p (c j)").bitcast(I32))
 
-        def load_w1(a, c0, width, key):
-            t = keep.tile([P, PACK, width], F32, name="raw_%d_%d" % (a, key), align_bytes=64)
-            nc.sync.dma_start(
-                t[:], w1[a * KP : (a + 1) * KP, c0 : c0 + width].rearrange("(p j) c -> p j c", j=PACK)
-            )
-            w1_raw[a, key] = t
+        def load_w1(a, first_col, width):
+            raw = held([P, PACK, width], F32, "w1_raw_%d_%d" % (a, first_col))
+            rows = w1[a * PASS : (a + 1) * PASS, first_col : first_col + width]
+            nc.sync.dma_start(raw[:], rows.rearrange("(p j) c -> p j c", j=PACK))
+            w1_raw[a, first_col] = raw
 
         def load_wu(b):
-            t = keep.tile([P, PACK, N], F32, name="tab%d" % b, align_bytes=64)
-            nc.sync.dma_start(t[:], wu[b * KP : (b + 1) * KP, :].rearrange("(p j) c -> p j c", j=PACK))
-            wu_raw.append(t)
+            wu_raw[b] = held([P, PACK, N], F32, "tab%d" % b)
+            nc.sync.dma_start(wu_raw[b][:], wu[b * PASS : (b + 1) * PASS, :].rearrange("(p j) c -> p j c", j=PACK))
 
-        def load_wg_planes(q):
+        def load_wg_planes(quad):
+            rows = wg_planes[QUADRANT * quad : QUADRANT * quad + PLANE_ROWS, :]
             nc.sync.dma_start(
-                wg_planes[32 * q : 32 * q + 4, :].bitcast(I32).rearrange("r (b c) -> r b c", b=r_passes),
-                wg_scales[:, 4 * q : 4 * q + 4, :].rearrange("b r c -> r b c").bitcast(I32),
+                rows.bitcast(I32).rearrange("s (b c) -> s b c", b=R_PASSES),
+                wg_scales[:, PLANE_ROWS * quad : PLANE_ROWS * (quad + 1), :].rearrange("b s c -> s b c").bitcast(I32),
             )
 
-        b1_early = b1[0:KP].rearrange("(g q t) -> q g t", g=2, t=PACK)
-        bias_first = keep.tile([P, 8], F32, name="bias_first", align_bytes=64)
-        bias_cols = {(0, 0): bias_first[:, 0:1], (0, 1): bias_first[:, 2:3]}
+        b1_early = b1[0:PASS].rearrange("(d w u side) -> w d u side", d=2, u=2, side=2)
+        bias_first = held([P, 2], F32, "bias_first")
+        for u in range(2):
+            bias_col[0, u] = bias_first[:, u : u + 1]
 
-        def load_bias_first(e):
-            nc.sync.dma_start(bias_first[64 * e : 64 * (e + 1), 0:3], b1_early[:, 0, e : e + 3])
+        def load_bias_first(side):
+            with nc.allow_non_contiguous_dma(reason="one bias value for each partition and tile"):
+                nc.sync.dma_start(bias_first[SIDE * side : SIDE * (side + 1), :], b1_early[:, 0, :, side])
 
-        def load_bias_tile(u):
-            col = keep.tile([P, 1], F32, name="bias_tile%d" % u, align_bytes=64)
-            for e in range(2):
-                nc.sync.dma_start(col[64 * e : 64 * (e + 1), :], b1_early[:, 1, 2 * u + e : 2 * u + e + 1])
-            bias_cols[0, 2 + u] = col[:]
+        def load_bias_of_tile(t):
+            col = held([P, 1], F32, "bias_tile%d" % t)
+            for side in range(2):
+                nc.sync.dma_start(col[SIDE * side : SIDE * (side + 1), :], b1_early[:, t // 2, t % 2, side : side + 1])
+            bias_col[0, t] = col[:]
 
-        for q in range(4):
+        for quad in range(P // QUADRANT):
             nc.scalar.dma_start(
-                tab_planes[32 * q : 32 * q + 4 * k_passes, :].bitcast(I32),
-                tab_scales[:, 4 * q : 4 * q + 4, :].bitcast(I32),
+                tab_planes[QUADRANT * quad : QUADRANT * quad + PLANE_ROWS * K_PASSES, :].bitcast(I32),
+                tab_scales[:, PLANE_ROWS * quad : PLANE_ROWS * (quad + 1), :].bitcast(I32),
             )
-        nc.scalar.activation(warm_out[:], warm[:], ACT.Silu)
+
         offs_t = load_list(offs, "offs_t")
         load_tab(0)
         pos1_t = load_list(pos1, "pos1_t")
         pos2_t = load_list(pos2, "pos2_t")
         load_bias_first(0)
-        load_w1(0, 0, KP // 2, 0)
+        load_w1(0, 0, PAIR_COLS)
         load_tab(1)
         load_bias_first(1)
-        load_w1(1, 0, KP // 2, 0)
+        load_w1(1, 0, PAIR_COLS)
         load_tab(2)
-        load_w1(2, 0, KP // 2, 0)
-        for a in range(k_passes):
-            load_w1(a, KP // 2, KP // 2, 1)
+        load_w1(2, 0, PAIR_COLS)
+        for a in range(K_PASSES):
+            load_w1(a, PAIR_COLS, PAIR_COLS)
             load_wg_planes(a)
-        load_w1(0, KP, KP, 2)
-        bias = keep.tile([P, PACK], F32, name="bias", align_bytes=64)
-        nc.sync.dma_start(bias[:], b1[KP : 2 * KP].rearrange("(p t) -> p t", t=PACK))
+        load_w1(0, PASS, PASS)
+        bias_late = held([P, PACK], F32, "bias_late")
+        nc.sync.dma_start(bias_late[:], b1[PASS : 2 * PASS].rearrange("(p t) -> p t", t=PACK))
         for t in range(PACK):
-            bias_cols[1, t] = bias[:, t : t + 1]
-        load_w1(1, KP, KP, 2)
-        load_bias_tile(0)
-        load_w1(2, KP, KP, 2)
-        load_bias_tile(1)
+            bias_col[1, t] = bias_late[:, t : t + 1]
+        load_w1(1, PASS, PASS)
+        load_bias_of_tile(2)
+        load_w1(2, PASS, PASS)
+        load_bias_of_tile(3)
         load_wu(0)
-        load_wg_planes(3)
+        load_wg_planes(P // QUADRANT - 1)
         pos3_t = load_list(pos3, "pos3_t")
         load_wu(1)
         pos4_t = load_list(pos4, "pos4_t")
-        wg_t = keep.tile([P, r_passes, 2 * N], U8, name="wg_t", align_bytes=64)
+        wg_t = held([P, R_PASSES, 2 * N], U8, "wg_t")
         nc.sync.dma_start(wg_t[:].bitcast(I32), wg_words.rearrange("b p c -> p b c").bitcast(I32))
 
-        v_words = []
-        w1_codes = {}
-        w1_planes = {}
+        v_words, w1_codes, w1_planes, h_acc, h = {}, {}, {}, {}, {}
 
-        def gather_tab(a):
-            t = keep.tile([P, S], U32, name="v%d" % a, align_bytes=64)
-            if a < k_passes - 1:
-                nc.vector.tensor_copy(t[:], tab_t[a][:].bitcast(U32).indirect(offs_t[:]))
+        def gather_words(a):
+            v_words[a] = held([P, S], U32, "v%d" % a)
+            width = BANK if a == LAST else S
+            for c0 in range(0, S, width):
+                entries = offs_t[:, c0 // LIST_ROWS : (c0 + width) // LIST_ROWS]
+                nc.vector.tensor_copy(v_words[a][:, c0 : c0 + width], tab[a][:].bitcast(U32).indirect(entries))
+
+        def codes_slot(a, b, d):
+            return "w1_codes_%d_%d_%d" % (a, b, d)
+
+        def planes_slot(a, b, d):
+            return "w1_planes_%d_%d_%d" % (a, b, d)
+
+        def quantise_w1(a, b, d, slot=None, copy=nc.scalar.copy):
+            if slot:
+                grouped = held([P, PAIR_COLS * PACK], BF16, slot)
             else:
-                for u in range(2):
-                    nc.vector.tensor_copy(
-                        t[:, u * BANK : (u + 1) * BANK],
-                        tab_t[a][:].bitcast(U32).indirect(offs_t[:, 32 * u : 32 * (u + 1)]),
-                    )
-            v_words.append(t)
-
-        reuse = {(1, 0, 1): "w1_2_0_0_codes", (2, 0, 1): "w1_2_0_0_planes"}
-
-        def cast_w1(a, b, d):
-            if (a, b, d) in reuse:
-                g = keep.tile([P, 2 * P * PACK], BF16, name=reuse[a, b, d], align_bytes=64)
-            else:
-                g = stage.tile([P, 2 * P * PACK], BF16, name="grouped", align_bytes=64, bufs=4)
+                grouped = stage.tile([P, PAIR_COLS * PACK], BF16, name="grouped", align_bytes=ALIGN, bufs=4)
             if b == 0:
-                dst = g[:].rearrange("p (t q j) -> p q j t", t=PACK, j=PACK)
-                src = w1_raw[a, d][:].rearrange("p j (q t) -> p q j t", t=PACK)
-                nc.scalar.copy(dst, src)
+                copy(
+                    grouped[:].rearrange("p (place w j) -> p w j place", place=PACK, j=PACK),
+                    w1_raw[a, d * PAIR_COLS][:].rearrange("p j (w place) -> p w j place", place=PACK),
+                )
             else:
-                dst = g[:].rearrange("p (t m j) -> p m j t", t=2, j=PACK)
-                src = w1_raw[a, 2][:].rearrange("p j (m t) -> p m j t", t=PACK)[:, :, :, 2 * d : 2 * d + 2]
-                nc.scalar.copy(dst, src)
-            return g
+                copy(
+                    grouped[:].rearrange("p (t w j) -> p w j t", t=2, j=PACK),
+                    w1_raw[a, PASS][:].rearrange("p j (w t) -> p w j t", t=PACK)[:, :, :, 2 * d : 2 * d + 2],
+                )
+            w1_codes[a, b, d] = held([P, PAIR_COLS], U32, codes_slot(a, b, d))
+            w1_planes[a, b, d] = held([P, PAIR_COLS], U8, planes_slot(a, b, d))
+            nc.vector.quantize_mx(out=w1_codes[a, b, d][:].bitcast(FP8X4), scales=w1_planes[a, b, d][:], in_=grouped[:])
 
-        def quant_w1(a, b, d, g):
-            name = "w1_%d_%d_%d" % (a, b, d)
-            codes = keep.tile([P, 2 * P], U32, name=name + "_codes", align_bytes=64)
-            planes = keep.tile([P, 2 * P], U8, name=name + "_planes", align_bytes=64)
-            nc.vector.quantize_mx(
-                out=codes[:].bitcast(FP8X4), scales=planes[:], in_=g[:]
-            )
-            w1_codes[a, b, d], w1_planes[a, b, d] = codes, planes
+        def h_pass(a, b, d):
+            for t in (2 * d, 2 * d + 1):
+                cols = slice((t % 2) * P, (t % 2 + 1) * P)
+                for part in range(S // BANK):
+                    if a == 0:
+                        h_acc[b, t, part] = bank(2 * t + part)
+                    entries = slice(part * BANK, (part + 1) * BANK)
+                    nc.tensor.matmul_mx(
+                        out=h_acc[b, t, part][:],
+                        lhsT=w1_codes[a, b, d][:, cols].bitcast(FP8X4),
+                        lhsT_scale=w1_planes[a, b, d][:, cols],
+                        rhs=v_words[a][:, entries].bitcast(FP8X4),
+                        rhs_scale=v_planes[PLANE_ROWS * a : P, entries],
+                        start=(a == 0),
+                        stop=(a == LAST),
+                    )
 
-        def prep_w1(a, b, d):
-            quant_w1(a, b, d, cast_w1(a, b, d))
+        def h_passes(b, d):
+            for a in range(K_PASSES):
+                h_pass(a, b, d)
 
-        def bank(i):
-            return psum.tile([P, BANK], F32, name="bank%d" % (i % 8))
+        def relu(b, t, share_with_vector=False):
+            h[b, t] = held([P, S], F32, "h%d_%d" % (b, t))
+            for part in range(S // BANK):
+                dst = h[b, t][:, part * BANK : (part + 1) * BANK]
+                if share_with_vector and part == 1:
+                    nc.vector.tensor_scalar(dst, h_acc[b, t, part][:], bias_col[b, t], 0.0, ALU.add, ALU.max)
+                else:
+                    nc.scalar.activation(dst, h_acc[b, t, part][:], ACT.Relu, bias=bias_col[b, t])
 
-        h_t = {}
-        acc = {}
+        z_early = held([P, PACK, M], F32, "z_early")
+        z_late = [held([P, PACK, MH], F32, "z_late%d" % e) for e in range(2)]
 
-        def h_pass(a, b, t):
-            d = t // 2
-            cols = slice((t % 2) * P, (t % 2 + 1) * P)
-            for u in range(S // BANK):
-                if a == 0:
-                    acc[b, t, u] = bank(2 * t + u)
-                js = slice(u * BANK, (u + 1) * BANK)
-                nc.tensor.matmul_mx(
-                    out=acc[b, t, u][:],
-                    lhsT=w1_codes[a, b, d][:, cols].bitcast(FP8X4),
-                    lhsT_scale=w1_planes[a, b, d][:, cols],
-                    rhs=v_words[a][:, js].bitcast(FP8X4),
-                    rhs_scale=v_planes[4 * a : P, js],
-                    start=(a == 0),
-                    stop=(a == k_passes - 1),
+        def half_list(offsets, e):
+            return offsets[:, e * MH // LIST_ROWS : (e + 1) * MH // LIST_ROWS]
+
+        def pick_old(b, t, e, old):
+            nc.vector.tensor_copy(old, h[b, t][:].indirect(half_list(pos1_t, e)))
+
+        def pick_new(b, t, e, old, dst):
+            nc.vector.tensor_tensor(dst, h[b, t][:].indirect(half_list(pos2_t, e)), old, ALU.subtract)
+
+        def differences(b, t, dst):
+            old = [stage.tile([P, MH], F32, name="old", align_bytes=ALIGN) for e in range(2)]
+            for e in range(2):
+                pick_old(b, t, e, old[e][:])
+            for e in range(2):
+                pick_new(b, t, e, old[e][:], dst[e])
+
+        def early_differences(t, slot):
+            z_tile = held([P, M], F32, slot)
+            differences(0, t, [z_tile[:, e * MH : (e + 1) * MH] for e in range(2)])
+            d, u = divmod(t, 2)
+            for side in range(2):
+                nc.sync.dma_start(
+                    z_early[SIDE * d : SIDE * (d + 1), 2 * u + side, :], z_tile[SIDE * side : SIDE * (side + 1), :]
                 )
 
-        def relu(b, t):
-            h = keep.tile([P, S], F32, name="h%d_%d" % (b, t), align_bytes=64)
-            col = bias_cols[b, t]
-            for u in range(S // BANK):
-                js = slice(u * BANK, (u + 1) * BANK)
-                if (b, t, u) == (0, 0, 1):
-                    nc.vector.tensor_scalar(h[:, js], acc[b, t, u][:], col, 0.0, ALU.add, ALU.max)
-                else:
-                    nc.scalar.activation(h[:, js], acc[b, t, u][:], ACT.Relu, bias=col)
-            h_t[b, t] = h
+        def late_differences(t):
+            differences(1, t, [z_late[e][:, t, :] for e in range(2)])
 
-        MH = M // 2
-        z32 = {}
-        z_early = keep.tile([P, PACK, M], F32, name="z32_0", align_bytes=64)
-        for e in range(2):
-            z32[0, e] = z_early[:, :, e * MH : (e + 1) * MH]
-        z_tile = {}
-        z_late = keep.tile([P, 2 * PACK - 1, MH], F32, name="z32_1", align_bytes=64)
-        z32[1, 0] = z_late[:, PACK - 1 : 2 * PACK - 1, :]
-        z32[1, 1] = z_late[:, 0:PACK, :]
-
-        def pick_old(b, t, e, o):
-            nc.vector.tensor_copy(o, h_t[b, t][:].indirect(pos1_t[:, 16 * e : 16 * (e + 1)]))
-
-        def pick_new(b, t, e, o):
-            dst = z32[b, e][:, t, :] if b else z_tile[t][:, e * MH : (e + 1) * MH]
-            nc.vector.tensor_tensor(
-                dst, h_t[b, t][:].indirect(pos2_t[:, 16 * e : 16 * (e + 1)]), o, ALU.subtract
+        def round_and_group(src, slot, copy):
+            grouped = held([P, src.shape[2] * PACK], BF16, slot)
+            copy(
+                grouped[:].rearrange("p (c x j) -> p c j x", x=PACK, j=PACK),
+                src.rearrange("p j (c x) -> p c j x", x=PACK),
             )
+            return grouped[:]
 
-        def diff(b, t):
-            if b == 0:
-                z_tile[t] = keep.tile([P, M], F32, name="z_tile%d" % t if t else "raw_1_1", align_bytes=64)
-            old = []
-            for e in range(2):
-                o = stage.tile([P, MH], F32, name="old", align_bytes=64)
-                pick_old(b, t, e, o[:])
-                old.append(o)
-            for e in range(2):
-                pick_new(b, t, e, old[e][:])
-            if b == 0:
-                g, u = divmod(t, 2)
-                for e in range(2):
-                    nc.sync.dma_start(
-                        z_early[64 * g : 64 * (g + 1), 2 * u + e, :], z_tile[t][64 * e : 64 * (e + 1), :]
-                    )
+        z_codes, z_planes, wu_codes, wu_planes = {}, {}, {}, {}
+        for b in range(R_PASSES):
+            z_codes[b] = held([P, M], U32, "z_codes%d" % b)
+            z_planes[b] = held([P, M], U8, "z_planes%d" % b)
+        for b in range(R_PASSES):
+            wu_codes[b] = held([P, N], U32, "wu_codes%d" % b)
+            wu_planes[b] = held([P, N], U8, "wu_planes%d" % b)
 
-        def cast_plain(src, eng, tag):
-            if tag:
-                g = keep.tile([P, MH * PACK], BF16, name=tag, align_bytes=64)
-            else:
-                g = stage.tile([P, MH * PACK], BF16, name="grouped", align_bytes=64, bufs=4)
-            dst = g[:].rearrange("p (c i j) -> p c j i", i=PACK, j=PACK)
-            s = src.rearrange("p j (c i) -> p c j i", i=PACK)
-            if eng == "v":
-                nc.vector.tensor_copy(dst, s)
-            else:
-                nc.scalar.copy(dst, s)
-            return g[:]
+        def quantise_z(b, changes, grouped):
+            nc.vector.quantize_mx(out=z_codes[b][:, changes].bitcast(FP8X4), scales=z_planes[b][:, changes], in_=grouped)
 
-        def codes_planes(name):
-            codes = keep.tile([P, KP], U32, name=name + "_codes", align_bytes=64)
-            planes = keep.tile([P, KP], U8, name=name + "_planes", align_bytes=64)
-            return codes, planes
+        def quantise_wu(b, slot):
+            grouped = round_and_group(wu_raw[b][:], slot, nc.scalar.copy)
+            nc.vector.quantize_mx(out=wu_codes[b][:].bitcast(FP8X4), scales=wu_planes[b][:], in_=grouped)
 
-        def quant_half(g, dst, e):
-            cols = slice(e * MH, (e + 1) * MH)
-            nc.vector.quantize_mx(out=dst[0][:, cols].bitcast(FP8X4), scales=dst[1][:, cols], in_=g)
-
-        zq = [codes_planes("z%d" % b) for b in range(r_passes)]
-        wq = [codes_planes("wu%d" % b) for b in range(r_passes)]
-
-        def prep_wu(b, tag):
-            g = keep.tile([P, N * PACK], BF16, name=tag, align_bytes=64)
-            nc.scalar.copy(
-                g[:].rearrange("p (c i j) -> p c j i", i=PACK, j=PACK),
-                wu_raw[b][:].rearrange("p j (c i) -> p c j i", i=PACK),
-            )
-            nc.vector.quantize_mx(out=wq[b][0][:].bitcast(FP8X4), scales=wq[b][1][:], in_=g[:])
-
-        for a in range(k_passes):
-            gather_tab(a)
+        for a in range(K_PASSES):
+            gather_words(a)
             if a == 0:
-                v_planes = keep.tile([P, S], U8, name="v_planes", align_bytes=64)
+                v_planes = held([P, S], U8, "v_planes")
                 nc.vector.tensor_copy(v_planes[:], tab_planes[:].indirect(offs_t[:]))
-            prep_w1(a, 0, 0)
+            quantise_w1(a, 0, 0)
             h_pass(a, 0, 0)
-            h_pass(a, 0, 1)
-        prep_w1(0, 0, 1)
-        relu(0, 0)
-        prep_w1(1, 0, 1)
-        diff(0, 0)
-        prep_w1(2, 0, 1)
-        for a in range(k_passes):
-            h_pass(a, 0, 2)
-            h_pass(a, 0, 3)
+
+        quantise_w1(0, 0, 1)
+        relu(0, 0, share_with_vector=True)
+        quantise_w1(1, 0, 1, slot=codes_slot(LAST, 0, 0))
+        early_differences(0, "w1_raw_%d_%d" % (1, PAIR_COLS))
+        quantise_w1(2, 0, 1, slot=planes_slot(LAST, 0, 0))
+        h_passes(0, 1)
         relu(0, 1)
-        diff(0, 1)
-        prep_w1(0, 1, 0)
-        prep_w1(0, 1, 1)
-        prep_w1(1, 1, 0)
+        early_differences(1, "z_tile1")
+        quantise_w1(0, 1, 0)
+        quantise_w1(0, 1, 1, copy=nc.vector.tensor_copy)
+        quantise_w1(1, 1, 0)
         relu(0, 2)
-        diff(0, 2)
-        prep_w1(1, 1, 1)
-        prep_w1(2, 1, 0)
-        for a in range(k_passes):
-            h_pass(a, 1, 0)
-            h_pass(a, 1, 1)
+        early_differences(2, "z_tile2")
+        quantise_w1(1, 1, 1)
+        quantise_w1(2, 1, 0)
+        h_passes(1, 0)
         relu(0, 3)
-        diff(0, 3)
-        prep_w1(2, 1, 1)
-        for a in range(k_passes):
-            h_pass(a, 1, 2)
-            h_pass(a, 1, 3)
-        relu(1, 0)
-        diff(1, 0)
-        relu(1, 1)
-        diff(1, 1)
-        prep_wu(0, "w1_2_1_0_planes")
+        early_differences(3, "z_tile3")
+        quantise_w1(2, 1, 1)
+        h_passes(1, 1)
+        for t in range(2):
+            relu(1, t)
+            late_differences(t)
         relu(1, 2)
         relu(1, 3)
-        late_old = keep.tile([P, MH], F32, name="bias", align_bytes=64)
-        last_old = keep.tile([P, MH], F32, name="last_old", align_bytes=64)
-        pick_old(1, 2, 0, late_old[:])
-        pick_old(1, 3, 0, last_old[:])
-        pick_new(1, 2, 0, late_old[:])
-        pick_new(1, 3, 0, last_old[:])
-        quant_half(cast_plain(z32[0, 0], "s", "v2"), zq[0], 0)
-        end_old = keep.tile([P, 2, MH], F32, name="v2", align_bytes=64)
 
-        gates = {}
-        lins = {}
+        last_pair = (PACK - 2, PACK - 1)
+        old_first = [held([P, MH], F32, slot) for slot in ("bias_late", "old_last")]
+        for t, old in zip(last_pair, old_first):
+            pick_old(1, t, 0, old[:])
+        for t, old in zip(last_pair, old_first):
+            pick_new(1, t, 0, old[:], z_late[0][:, t, :])
 
-        def second(b, e, pair):
-            if b == 0:
-                gates[e, pair] = bank(4 * e + 2 * pair)
-                lins[e, pair] = bank(4 * e + 2 * pair + 1)
-            for ii in range(2):
-                i = 2 * pair + ii
-                for q in range(2):
-                    ms = slice(e * MH + q * P, e * MH + (q + 1) * P)
+        gate, lin = {}, {}
+
+        def second_pass(b, e, opens):
+            for pair in range(N_TILES // 2):
+                if opens:
+                    gate[e, pair] = bank(4 * e + 2 * pair)
+                    lin[e, pair] = bank(4 * e + 2 * pair + 1)
+                for x in range(2):
+                    i = 2 * pair + x
+                    for c0 in range(0, MH, P):
+                        changes = slice(e * MH + c0, e * MH + c0 + P)
+                        nc.tensor.matmul_mx(
+                            out=gate[e, pair][:, x * MH + c0 : x * MH + c0 + P],
+                            lhsT=wg_t[:, b, 2 * i * P : 2 * (i + 1) * P].bitcast(FP4X4),
+                            lhsT_scale=wg_planes[:, b * N + i * P : b * N + (i + 1) * P],
+                            rhs=z_codes[b][:, changes].bitcast(FP8X4),
+                            rhs_scale=z_planes[b][:, changes],
+                            start=(opens and x == 0 and c0 == 0),
+                            stop=(not opens and x == 1 and c0 == MH - P),
+                        )
+                for x in range(2):
+                    cols = slice((2 * pair + x) * P, (2 * pair + x + 1) * P)
+                    changes = slice(e * MH, (e + 1) * MH)
                     nc.tensor.matmul_mx(
-                        out=gates[e, pair][:, ii * MH + q * P : ii * MH + (q + 1) * P],
-                        lhsT=wg_t[:, b, 2 * i * P : 2 * (i + 1) * P].bitcast(FP4X4),
-                        lhsT_scale=wg_planes[:, b * N + i * P : b * N + (i + 1) * P],
-                        rhs=zq[b][0][:, ms].bitcast(FP8X4),
-                        rhs_scale=zq[b][1][:, ms],
-                        start=(b == 0 and ii == 0 and q == 0),
-                        stop=(b == r_passes - 1 and ii == 1 and q == 1),
+                        out=lin[e, pair][:, x * MH : (x + 1) * MH],
+                        lhsT=wu_codes[b][:, cols].bitcast(FP8X4),
+                        lhsT_scale=wu_planes[b][:, cols],
+                        rhs=z_codes[b][:, changes].bitcast(FP8X4),
+                        rhs_scale=z_planes[b][:, changes],
+                        start=(opens and x == 0),
+                        stop=(not opens and x == 1),
                     )
-            for ii in range(2):
-                i = 2 * pair + ii
-                cols = slice(i * P, (i + 1) * P)
-                ms = slice(e * MH, (e + 1) * MH)
-                nc.tensor.matmul_mx(
-                    out=lins[e, pair][:, ii * MH : (ii + 1) * MH],
-                    lhsT=wq[b][0][:, cols].bitcast(FP8X4),
-                    lhsT_scale=wq[b][1][:, cols],
-                    rhs=zq[b][0][:, ms].bitcast(FP8X4),
-                    rhs_scale=zq[b][1][:, ms],
-                    start=(b == 0 and ii == 0),
-                    stop=(b == r_passes - 1 and ii == 1),
-                )
 
-        for pair in range(2):
-            second(0, 0, pair)
+        quantise_wu(0, planes_slot(LAST, 1, 1))
+        quantise_wu(1, codes_slot(LAST, 1, 1))
+        quantise_z(1, slice(0, MH), round_and_group(z_late[0][:], "tab1", nc.scalar.copy))
+        second_pass(1, 0, opens=True)
 
-        pick_old(1, 2, 1, end_old[:, 0, :])
-        pick_old(1, 3, 1, end_old[:, 1, :])
-        prep_wu(1, "w1_2_1_1_planes")
-        pick_new(1, 2, 1, end_old[:, 0, :])
-        quant_half(cast_plain(z32[1, 0], "s", ""), zq[1], 0)
-        pick_new(1, 3, 1, end_old[:, 1, :])
-        for pair in range(2):
-            second(1, 0, pair)
-        quant_half(cast_plain(z32[0, 1], "s", "w1_2_1_1_planes"), zq[0], 1)
-        for pair in range(2):
-            second(0, 1, pair)
-        gb = keep.tile([P, MH, PACK], BF16, name="z1_grouped1", align_bytes=64)
-        dst = gb[:].rearrange("p (c i) j -> p c j i", i=PACK)
-        src = z32[1, 1].rearrange("p j (c i) -> p c j i", i=PACK)
-        nc.vector.tensor_copy(dst[:, 0:44], src[:, 0:44])
-        nc.scalar.copy(dst[:, 44:64], src[:, 44:64])
-        quant_half(gb[:].rearrange("p c j -> p (c j)"), zq[1], 1)
-        for pair in range(2):
-            second(1, 1, pair)
+        z_early_grouped = round_and_group(z_early[:], "bias_late", nc.vector.tensor_copy)
+        old_second = held([P, 2, MH], F32, "z_early")
+        for x, t in enumerate(last_pair):
+            pick_old(1, t, 1, old_second[:, x, :])
+        quantise_z(0, slice(0, M), z_early_grouped)
+        second_pass(0, 0, opens=False)
+        second_pass(0, 1, opens=True)
+        for x, t in enumerate(last_pair):
+            pick_new(1, t, 1, old_second[:, x, :], z_late[1][:, t, :])
+        quantise_z(1, slice(MH, M), round_and_group(z_late[1][:], "z_last_grouped", nc.vector.tensor_copy))
+        second_pass(1, 1, opens=False)
 
-        y_t = [keep.tile([P, M], F32, name="y%d" % i, align_bytes=64) for i in range(n_tiles)]
-        silu = {}
-        first = {}
-
-        def make_silu(e, pair):
-            s = keep.tile([P, M], F32, name="silu%d_%d" % (e, pair), align_bytes=64)
-            nc.scalar.activation(s[:], gates[e, pair][:], ACT.Silu)
-            silu[e, pair] = s
+        y = [held([P, M], F32, "y%d" % i) for i in range(N_TILES)]
+        silu, first = {}, {}
 
         def make_y(e, i):
-            cs = slice((i % 2) * MH, (i % 2 + 1) * MH)
+            cols = slice((i % 2) * MH, (i % 2 + 1) * MH)
             nc.vector.tensor_tensor(
-                y_t[i][:, e * MH : (e + 1) * MH], lins[e, i // 2][:, cs], silu[e, i // 2][:, cs], ALU.mult
+                y[i][:, e * MH : (e + 1) * MH], lin[e, i // 2][:, cols], silu[e, i // 2][:, cols], ALU.mult
             )
 
         def pick_first(i):
-            f = stage.tile([P, M2], F32, name="first", align_bytes=64)
-            nc.vector.tensor_copy(f[:], y_t[i][:].indirect(pos3_t[:]))
-            first[i] = f
+            first[i] = stage.tile([P, M2], F32, name="first", align_bytes=ALIGN)
+            nc.vector.tensor_copy(first[i][:], y[i][:].indirect(pos3_t[:]))
 
-        def finish(i):
-            o = keep.tile([P, M2], F32, name="o%d" % i, align_bytes=64)
-            nc.vector.tensor_tensor(o[:], y_t[i][:].indirect(pos4_t[:]), first[i][:], ALU.add)
-            nc.sync.dma_start(out[i * P : (i + 1) * P, :], o[:])
+        def add_second_and_store(i):
+            result = held([P, M2], F32, "result%d" % i)
+            nc.vector.tensor_tensor(result[:], y[i][:].indirect(pos4_t[:]), first[i][:], ALU.add)
+            nc.sync.dma_start(out[i * P : (i + 1) * P, :], result[:])
 
         for e in range(2):
-            for pair in range(2):
-                make_silu(e, pair)
-        for i in range(n_tiles):
+            for pair in range(N_TILES // 2):
+                silu[e, pair] = held([P, BANK], F32, "silu%d_%d" % (e, pair))
+                nc.scalar.activation(silu[e, pair][:], gate[e, pair][:], ACT.Silu)
+        for i in range(N_TILES):
             make_y(0, i)
-        make_y(1, 0)
-        for step in range(1, n_tiles + 2):
-            if step < n_tiles:
+        for step in range(N_TILES + 2):
+            if step < N_TILES:
                 make_y(1, step)
-            if step <= n_tiles:
+            if 1 <= step <= N_TILES:
                 pick_first(step - 1)
             if step >= 2:
-                finish(step - 2)
+                add_second_and_store(step - 2)

@@ -71,8 +71,8 @@ def tile_list_redline_pair_features_kernel(
             nc.sync.dma_start(raw[:], rows.rearrange("(p j) c -> p j c", j=PACK))
             w1_raw[a, first_col] = raw
 
-        def load_wu(b):
-            wu_raw[b] = held([P, PACK, N], F32, "tab%d" % b)
+        def load_wu(b, slot):
+            wu_raw[b] = held([P, PACK, N], F32, slot)
             nc.sync.dma_start(wu_raw[b][:], wu[b * PASS : (b + 1) * PASS, :].rearrange("(p j) c -> p j c", j=PACK))
 
         def load_wg_planes(quad):
@@ -82,20 +82,13 @@ def tile_list_redline_pair_features_kernel(
                 wg_scales[:, PLANE_ROWS * quad : PLANE_ROWS * (quad + 1), :].rearrange("b s c -> s b c").bitcast(I32),
             )
 
-        b1_early = b1[0:PASS].rearrange("(d w u side) -> w d u side", d=2, u=2, side=2)
-        bias_first = held([P, 2], F32, "bias_first")
-        for u in range(2):
-            bias_col[0, u] = bias_first[:, u : u + 1]
-
-        def load_bias_first(side):
-            with nc.allow_non_contiguous_dma(reason="one bias value for each partition and tile"):
-                nc.sync.dma_start(bias_first[SIDE * side : SIDE * (side + 1), :], b1_early[:, 0, :, side])
-
-        def load_bias_of_tile(t):
-            col = held([P, 1], F32, "bias_tile%d" % t)
+        b1_early = b1[0:PASS].rearrange("(d w x) -> w d x", d=2, x=PACK)
+        def load_bias_early(d):
+            cols = held([P, 3], F32, "bias_early%d" % d)
             for side in range(2):
-                nc.sync.dma_start(col[SIDE * side : SIDE * (side + 1), :], b1_early[:, t // 2, t % 2, side : side + 1])
-            bias_col[0, t] = col[:]
+                nc.sync.dma_start(cols[SIDE * side : SIDE * (side + 1), :], b1_early[:, d, side : side + 3])
+            for u in range(2):
+                bias_col[0, 2 * d + u] = cols[:, 2 * u : 2 * u + 1]
 
         for quad in range(P // QUADRANT):
             nc.scalar.dma_start(
@@ -103,36 +96,31 @@ def tile_list_redline_pair_features_kernel(
                 tab_scales[:, PLANE_ROWS * quad : PLANE_ROWS * (quad + 1), :].bitcast(I32),
             )
 
+        warm_in = held([P, 1], F32, "warm_in")
+        nc.vector.memset(warm_in[:], 0.0)
+        warm_out = held([P, 1], F32, "warm_out")
+        nc.scalar.activation(warm_out[:], warm_in[:], ACT.Silu)
+
         offs_t = load_list(offs, "offs_t")
         load_tab(0)
         pos1_t = load_list(pos1, "pos1_t")
         pos2_t = load_list(pos2, "pos2_t")
-        load_bias_first(0)
+        load_bias_early(0)
         load_w1(0, 0, PAIR_COLS)
-        load_tab(1)
-        load_bias_first(1)
-        load_w1(1, 0, PAIR_COLS)
-        load_tab(2)
-        load_w1(2, 0, PAIR_COLS)
+        for a in range(1, K_PASSES):
+            load_tab(a)
+            load_w1(a, 0, PAIR_COLS)
         for a in range(K_PASSES):
             load_w1(a, PAIR_COLS, PAIR_COLS)
-            load_wg_planes(a)
         load_w1(0, PASS, PASS)
+        load_bias_early(1)
+        load_w1(1, PASS, PASS)
+        load_w1(2, PASS, PASS)
         bias_late = held([P, PACK], F32, "bias_late")
         nc.sync.dma_start(bias_late[:], b1[PASS : 2 * PASS].rearrange("(p t) -> p t", t=PACK))
         for t in range(PACK):
             bias_col[1, t] = bias_late[:, t : t + 1]
-        load_w1(1, PASS, PASS)
-        load_bias_of_tile(2)
-        load_w1(2, PASS, PASS)
-        load_bias_of_tile(3)
-        load_wu(0)
-        load_wg_planes(P // QUADRANT - 1)
-        pos3_t = load_list(pos3, "pos3_t")
-        load_wu(1)
-        pos4_t = load_list(pos4, "pos4_t")
-        wg_t = held([P, R_PASSES, 2 * N], U8, "wg_t")
-        nc.sync.dma_start(wg_t[:].bitcast(I32), wg_words.rearrange("b p c -> p b c").bitcast(I32))
+        load_wu(0, "tab0")
 
         v_words, w1_codes, w1_planes, h_acc, h = {}, {}, {}, {}, {}
 
@@ -156,8 +144,8 @@ def tile_list_redline_pair_features_kernel(
                 grouped = stage.tile([P, PAIR_COLS * PACK], BF16, name="grouped", align_bytes=ALIGN, bufs=4)
             if b == 0:
                 copy(
-                    grouped[:].rearrange("p (place w j) -> p w j place", place=PACK, j=PACK),
-                    w1_raw[a, d * PAIR_COLS][:].rearrange("p j (w place) -> p w j place", place=PACK),
+                    grouped[:].rearrange("p (u side w j) -> p u w j side", u=2, side=2, j=PACK),
+                    w1_raw[a, d * PAIR_COLS][:].rearrange("p j (w u side) -> p u w j side", u=2, side=2),
                 )
             else:
                 copy(
@@ -189,8 +177,8 @@ def tile_list_redline_pair_features_kernel(
             for a in range(K_PASSES):
                 h_pass(a, b, d)
 
-        def relu(b, t, share_with_vector=False):
-            h[b, t] = held([P, S], F32, "h%d_%d" % (b, t))
+        def relu(b, t, share_with_vector=False, slot=None):
+            h[b, t] = held([P, S], F32, slot or "h%d_%d" % (b, t))
             for part in range(S // BANK):
                 dst = h[b, t][:, part * BANK : (part + 1) * BANK]
                 if share_with_vector and part == 1:
@@ -210,16 +198,16 @@ def tile_list_redline_pair_features_kernel(
         def pick_new(b, t, e, old, dst):
             nc.vector.tensor_tensor(dst, h[b, t][:].indirect(half_list(pos2_t, e)), old, ALU.subtract)
 
-        def differences(b, t, dst):
-            old = [stage.tile([P, MH], F32, name="old", align_bytes=ALIGN) for e in range(2)]
+        def differences(b, t, dst, slot):
+            old = [held([P, MH], F32, slot[e]) for e in range(2)]
             for e in range(2):
                 pick_old(b, t, e, old[e][:])
             for e in range(2):
                 pick_new(b, t, e, old[e][:], dst[e])
 
-        def early_differences(t, slot):
-            z_tile = held([P, M], F32, slot)
-            differences(0, t, [z_tile[:, e * MH : (e + 1) * MH] for e in range(2)])
+        def early_differences(t, slot, z_slot=None):
+            z_tile = held([P, M], F32, z_slot or "z_tile%d" % t)
+            differences(0, t, [z_tile[:, e * MH : (e + 1) * MH] for e in range(2)], slot)
             d, u = divmod(t, 2)
             for side in range(2):
                 nc.sync.dma_start(
@@ -227,13 +215,13 @@ def tile_list_redline_pair_features_kernel(
                 )
 
         def late_differences(t):
-            differences(1, t, [z_late[e][:, t, :] for e in range(2)])
+            differences(1, t, [z_late[e][:, t, :] for e in range(2)], ["old_late%d_%d" % (t, e) for e in range(2)])
 
         def round_and_group(src, slot, copy):
             grouped = held([P, src.shape[2] * PACK], BF16, slot)
             copy(
-                grouped[:].rearrange("p (c x j) -> p c j x", x=PACK, j=PACK),
-                src.rearrange("p j (c x) -> p c j x", x=PACK),
+                grouped[:].rearrange("p (c x j) -> p c j x", x=2, j=PACK),
+                src.rearrange("p j (c x) -> p c j x", x=2),
             )
             return grouped[:]
 
@@ -260,29 +248,40 @@ def tile_list_redline_pair_features_kernel(
             quantise_w1(a, 0, 0)
             h_pass(a, 0, 0)
 
-        quantise_w1(0, 0, 1)
-        relu(0, 0, share_with_vector=True)
+        quantise_w1(0, 0, 1, slot="grouped_first", copy=nc.vector.tensor_copy)
+        relu(0, 0)
         quantise_w1(1, 0, 1, slot=codes_slot(LAST, 0, 0))
-        early_differences(0, "w1_raw_%d_%d" % (1, PAIR_COLS))
+        early_differences(0, ["w1_raw_%d_%d" % (0, PAIR_COLS), "grouped_first"], z_slot="w1_raw_%d_%d" % (1, PAIR_COLS))
         quantise_w1(2, 0, 1, slot=planes_slot(LAST, 0, 0))
         h_passes(0, 1)
-        relu(0, 1)
-        early_differences(1, "z_tile1")
+        relu(0, 1, slot="w1_raw_%d_%d" % (LAST, PAIR_COLS))
+        early_differences(1, ["old1_0", "old1_1"])
         quantise_w1(0, 1, 0)
-        quantise_w1(0, 1, 1, copy=nc.vector.tensor_copy)
-        quantise_w1(1, 1, 0)
         relu(0, 2)
-        early_differences(2, "z_tile2")
-        quantise_w1(1, 1, 1)
-        quantise_w1(2, 1, 0)
-        h_passes(1, 0)
+        early_differences(2, ["old2_0", "old2_1"])
         relu(0, 3)
-        early_differences(3, "z_tile3")
-        quantise_w1(2, 1, 1)
+        quantise_w1(1, 1, 0)
+        quantise_w1(2, 1, 0, slot="grouped_last")
+        h_passes(1, 0)
+        early_differences(3, ["old3_0", "old3_1"], z_slot="grouped_last")
+        load_wu(1, "z_tile1")
+        wg_t = held([P, R_PASSES, 2 * N], U8, "wg_t")
+        nc.sync.dma_start(wg_t[:].bitcast(I32), wg_words.rearrange("b p c -> p b c").bitcast(I32))
+        for quad in range(P // QUADRANT):
+            load_wg_planes(quad)
+        pos3_t = load_list(pos3, "pos3_t")
+        pos4_t = load_list(pos4, "pos4_t")
+        quantise_w1(0, 1, 1, slot="old3_0", copy=nc.vector.tensor_copy)
+        quantise_w1(1, 1, 1)
+        relu(1, 0, share_with_vector=True)
+        late_differences(0)
+        quantise_w1(2, 1, 1, slot=planes_slot(LAST, 1, 0))
         h_passes(1, 1)
-        for t in range(2):
-            relu(1, t)
-            late_differences(t)
+        relu(1, 1)
+        late_differences(1)
+        halves = [slice(e * MH, (e + 1) * MH) for e in range(2)]
+        quantise_wu(0, codes_slot(LAST, 1, 0))
+        quantise_z(0, halves[0], round_and_group(z_early[:, :, halves[0]], "tab0", nc.vector.tensor_copy))
         relu(1, 2)
         relu(1, 3)
 
@@ -326,21 +325,19 @@ def tile_list_redline_pair_features_kernel(
                         stop=(not opens and x == 1),
                     )
 
-        quantise_wu(0, planes_slot(LAST, 1, 1))
+        second_pass(0, 0, opens=True)
         quantise_wu(1, codes_slot(LAST, 1, 1))
-        quantise_z(1, slice(0, MH), round_and_group(z_late[0][:], "tab1", nc.scalar.copy))
-        second_pass(1, 0, opens=True)
-
-        z_early_grouped = round_and_group(z_early[:], "bias_late", nc.vector.tensor_copy)
-        old_second = held([P, 2, MH], F32, "z_early")
-        for x, t in enumerate(last_pair):
-            pick_old(1, t, 1, old_second[:, x, :])
-        quantise_z(0, slice(0, M), z_early_grouped)
-        second_pass(0, 0, opens=False)
+        z_first_grouped = round_and_group(z_late[0][:], "z_tile1", nc.vector.tensor_copy)
+        old_second = [held([P, MH], F32, slot) for slot in (codes_slot(LAST, 1, 1), "z_late0")]
+        pick_old(1, last_pair[0], 1, old_second[0][:])
+        quantise_z(1, halves[0], z_first_grouped)
+        second_pass(1, 0, opens=False)
+        pick_old(1, last_pair[1], 1, old_second[1][:])
+        quantise_z(0, halves[1], round_and_group(z_early[:, :, halves[1]], planes_slot(LAST, 1, 1), nc.scalar.copy))
         second_pass(0, 1, opens=True)
-        for x, t in enumerate(last_pair):
-            pick_new(1, t, 1, old_second[:, x, :], z_late[1][:, t, :])
-        quantise_z(1, slice(MH, M), round_and_group(z_late[1][:], "z_last_grouped", nc.vector.tensor_copy))
+        for t, old in zip(last_pair, old_second):
+            pick_new(1, t, 1, old[:], z_late[1][:, t, :])
+        quantise_z(1, halves[1], round_and_group(z_late[1][:], "z_last_grouped", nc.vector.tensor_copy))
         second_pass(1, 1, opens=False)
 
         y = [held([P, M], F32, "y%d" % i) for i in range(N_TILES)]

@@ -41,9 +41,12 @@ def tile_list_redline_pair_features_kernel(
     with ExitStack() as ctx:
         keep = ctx.enter_context(tc.tile_pool(name="keep", bufs=1))
         stage = ctx.enter_context(tc.tile_pool(name="stage", bufs=3))
+        placed = ctx.enter_context(tc.tile_pool(name="placed", bufs=1))
         psum = ctx.enter_context(tc.psum_pool(name="psum", bufs=1))
 
         def held(shape, dtype, slot):
+            if isinstance(slot, int):
+                return placed.tile(shape, dtype, name="placed%d" % slot, align_bytes=ALIGN, offset=slot)
             return keep.tile(shape, dtype, name=slot, align_bytes=ALIGN)
 
         def bank(index):
@@ -138,7 +141,7 @@ def tile_list_redline_pair_features_kernel(
             return "w1_planes_%d_%d_%d" % (a, b, d)
 
         def quantise_w1(a, b, d, slot=None, copy=nc.scalar.copy):
-            if slot:
+            if slot is not None:
                 grouped = held([P, PAIR_COLS * PACK], BF16, slot)
             else:
                 grouped = stage.tile([P, PAIR_COLS * PACK], BF16, name="grouped", align_bytes=ALIGN, bufs=4)
@@ -187,7 +190,8 @@ def tile_list_redline_pair_features_kernel(
                     nc.scalar.activation(dst, h_acc[b, t, part][:], ACT.Relu, bias=bias_col[b, t])
 
         z_early = held([P, PACK, M], F32, "z_early")
-        z_late = [held([P, PACK, MH], F32, "z_late%d" % e) for e in range(2)]
+        old_late = held([P, PACK, M], F32, "tab1")
+        new_late = [held([P, PACK, MH], F32, slot) for slot in ("tab2", "new_late1")]
 
         def half_list(offsets, e):
             return offsets[:, e * MH // LIST_ROWS : (e + 1) * MH // LIST_ROWS]
@@ -206,7 +210,7 @@ def tile_list_redline_pair_features_kernel(
                 pick_new(b, t, e, old[e][:], dst[e])
 
         def early_differences(t, slot, z_slot=None):
-            z_tile = held([P, M], F32, z_slot or "z_tile%d" % t)
+            z_tile = held([P, M], F32, "z_tile%d" % t if z_slot is None else z_slot)
             differences(0, t, [z_tile[:, e * MH : (e + 1) * MH] for e in range(2)], slot)
             d, u = divmod(t, 2)
             for side in range(2):
@@ -214,8 +218,23 @@ def tile_list_redline_pair_features_kernel(
                     z_early[SIDE * d : SIDE * (d + 1), 2 * u + side, :], z_tile[SIDE * side : SIDE * (side + 1), :]
                 )
 
-        def late_differences(t):
-            differences(1, t, [z_late[e][:, t, :] for e in range(2)], ["old_late%d_%d" % (t, e) for e in range(2)])
+        def pick_old_late(t, changes):
+            entries = pos1_t[:, changes.start // LIST_ROWS : changes.stop // LIST_ROWS]
+            nc.vector.tensor_copy(old_late[:, t, changes], h[1, t][:].indirect(entries))
+
+        def pick_new_late(t, e):
+            nc.vector.tensor_copy(new_late[e][:, t, :], h[1, t][:].indirect(half_list(pos2_t, e)))
+
+        def subtract_and_group(e, slot):
+            changes = slice(e * MH, (e + 1) * MH)
+            grouped = held([P, MH * PACK], BF16, slot)
+            nc.vector.tensor_tensor(
+                grouped[:].rearrange("p (c x j) -> p c j x", x=2, j=PACK),
+                new_late[e][:].rearrange("p j (c x) -> p c j x", x=2),
+                old_late[:, :, changes].rearrange("p j (c x) -> p c j x", x=2),
+                ALU.subtract,
+            )
+            return grouped[:]
 
         def round_and_group(src, slot, copy):
             grouped = held([P, src.shape[2] * PACK], BF16, slot)
@@ -257,13 +276,14 @@ def tile_list_redline_pair_features_kernel(
         relu(0, 1, slot="w1_raw_%d_%d" % (LAST, PAIR_COLS))
         early_differences(1, ["old1_0", "old1_1"])
         quantise_w1(0, 1, 0)
+        quantise_w1(0, 1, 1, slot=codes_slot(1, 0, 1))
         relu(0, 2)
         early_differences(2, ["old2_0", "old2_1"])
         relu(0, 3)
         quantise_w1(1, 1, 0)
-        quantise_w1(2, 1, 0, slot="grouped_last")
+        quantise_w1(2, 1, 0, slot=1024)
         h_passes(1, 0)
-        early_differences(3, ["old3_0", "old3_1"], z_slot="grouped_last")
+        early_differences(3, ["old3_0", "old3_1"], z_slot=0)
         load_wu(1, "z_tile1")
         wg_t = held([P, R_PASSES, 2 * N], U8, "wg_t")
         nc.sync.dma_start(wg_t[:].bitcast(I32), wg_words.rearrange("b p c -> p b c").bitcast(I32))
@@ -271,26 +291,27 @@ def tile_list_redline_pair_features_kernel(
             load_wg_planes(quad)
         pos3_t = load_list(pos3, "pos3_t")
         pos4_t = load_list(pos4, "pos4_t")
-        quantise_w1(0, 1, 1, slot="old3_0", copy=nc.vector.tensor_copy)
-        quantise_w1(1, 1, 1)
-        relu(1, 0, share_with_vector=True)
-        late_differences(0)
+        quantise_w1(1, 1, 1, slot=2048)
+        relu(1, 0)
+        whole = slice(0, M)
+        halves = [slice(e * MH, (e + 1) * MH) for e in range(2)]
+        pick_old_late(0, whole)
+        pick_new_late(0, 0)
+        pick_new_late(0, 1)
         quantise_w1(2, 1, 1, slot=planes_slot(LAST, 1, 0))
         h_passes(1, 1)
         relu(1, 1)
-        late_differences(1)
-        halves = [slice(e * MH, (e + 1) * MH) for e in range(2)]
+        pick_old_late(1, whole)
+        pick_new_late(1, 0)
+        pick_new_late(1, 1)
         quantise_wu(0, codes_slot(LAST, 1, 0))
-        quantise_z(0, halves[0], round_and_group(z_early[:, :, halves[0]], "tab0", nc.vector.tensor_copy))
         relu(1, 2)
+        pick_new_late(2, 0)
+        pick_old_late(2, whole)
+        quantise_z(0, halves[0], round_and_group(z_early[:, :, halves[0]], planes_slot(LAST, 1, 1), nc.scalar.copy))
         relu(1, 3)
-
-        last_pair = (PACK - 2, PACK - 1)
-        old_first = [held([P, MH], F32, slot) for slot in ("bias_late", "old_last")]
-        for t, old in zip(last_pair, old_first):
-            pick_old(1, t, 0, old[:])
-        for t, old in zip(last_pair, old_first):
-            pick_new(1, t, 0, old[:], z_late[0][:, t, :])
+        pick_new_late(3, 0)
+        pick_old_late(3, halves[0])
 
         gate, lin = {}, {}
 
@@ -326,18 +347,27 @@ def tile_list_redline_pair_features_kernel(
                     )
 
         second_pass(0, 0, opens=True)
-        quantise_wu(1, codes_slot(LAST, 1, 1))
-        z_first_grouped = round_and_group(z_late[0][:], "z_tile1", nc.vector.tensor_copy)
-        old_second = [held([P, MH], F32, slot) for slot in (codes_slot(LAST, 1, 1), "z_late0")]
-        pick_old(1, last_pair[0], 1, old_second[0][:])
+        z_first_grouped = subtract_and_group(0, "z_first_grouped")
+        pick_old_late(3, halves[1])
         quantise_z(1, halves[0], z_first_grouped)
+        def quantise_wu_half(x, slot):
+            cols = slice(x * N // 2, (x + 1) * N // 2)
+            grouped = round_and_group(wu_raw[1][:, :, cols], slot, nc.scalar.copy)
+            nc.vector.quantize_mx(out=wu_codes[1][:, cols].bitcast(FP8X4), scales=wu_planes[1][:, cols], in_=grouped)
+
+        quantise_wu_half(0, codes_slot(LAST, 1, 1))
+        z_part = new_late[1][:, 2:PACK, :].rearrange("p t m -> p (t m)").bitcast(BF16)
+        nc.scalar.copy(
+            z_part.rearrange("p (c x j) -> p c j x", x=2, j=PACK),
+            z_early[:, :, halves[1]].rearrange("p j (c x) -> p c j x", x=2),
+        )
+        quantise_z(0, halves[1], z_part)
+        quantise_wu_half(1, "v2")
         second_pass(1, 0, opens=False)
-        pick_old(1, last_pair[1], 1, old_second[1][:])
-        quantise_z(0, halves[1], round_and_group(z_early[:, :, halves[1]], planes_slot(LAST, 1, 1), nc.scalar.copy))
         second_pass(0, 1, opens=True)
-        for t, old in zip(last_pair, old_second):
-            pick_new(1, t, 1, old[:], z_late[1][:, t, :])
-        quantise_z(1, halves[1], round_and_group(z_late[1][:], "z_last_grouped", nc.vector.tensor_copy))
+        for t in (2, 3):
+            pick_new_late(t, 1)
+        quantise_z(1, halves[1], subtract_and_group(1, "z_last_grouped"))
         second_pass(1, 1, opens=False)
 
         y = [held([P, M], F32, "y%d" % i) for i in range(N_TILES)]

@@ -31,6 +31,10 @@ LAST = K_PASSES - 1
 PAIR_COLS = 2 * P
 MH = M // 2
 N_TILES = N // P
+NH = N // 2
+BIAS_RUN = 3
+GROUPED_BYTES = PAIR_COLS * PACK * 2
+AT_PASS1, AT_H3, AT_PASS2, AT_NEXT_WEIGHTS = 0, GROUPED_BYTES, 3 * GROUPED_BYTES, 4 * GROUPED_BYTES
 
 
 def tile_list_redline_pair_features_kernel(
@@ -46,7 +50,7 @@ def tile_list_redline_pair_features_kernel(
 
         def held(shape, dtype, slot):
             if isinstance(slot, int):
-                return placed.tile(shape, dtype, name="placed%d" % slot, align_bytes=ALIGN, offset=slot)
+                return placed.tile(shape, dtype, name="placed%d_%d" % (slot, shape[1]), align_bytes=ALIGN, offset=slot)
             return keep.tile(shape, dtype, name=slot, align_bytes=ALIGN)
 
         def bank(index):
@@ -68,8 +72,11 @@ def tile_list_redline_pair_features_kernel(
             tab[a] = held([P, T], I32, "tab%d" % a)
             nc.sync.dma_start(tab[a][:], tab_words[a].rearrange("p c j -> p (c j)").bitcast(I32))
 
+        def raw_slot(a, first_col):
+            return "w1_raw_%d_%d" % (a, first_col)
+
         def load_w1(a, first_col, width):
-            raw = held([P, PACK, width], F32, "w1_raw_%d_%d" % (a, first_col))
+            raw = held([P, PACK, width], F32, raw_slot(a, first_col))
             rows = w1[a * PASS : (a + 1) * PASS, first_col : first_col + width]
             nc.sync.dma_start(raw[:], rows.rearrange("(p j) c -> p j c", j=PACK))
             w1_raw[a, first_col] = raw
@@ -86,15 +93,17 @@ def tile_list_redline_pair_features_kernel(
             )
 
         b1_early = b1[0:PASS].rearrange("(d w x) -> w d x", d=2, x=PACK)
+
         def load_bias_early(d):
-            cols = held([P, 3], F32, "bias_early%d" % d)
+            cols = held([P, BIAS_RUN], F32, "bias_early%d" % d)
             for side in range(2):
-                nc.sync.dma_start(cols[SIDE * side : SIDE * (side + 1), :], b1_early[:, d, side : side + 3])
+                nc.sync.dma_start(cols[SIDE * side : SIDE * (side + 1), :], b1_early[:, d, side : side + BIAS_RUN])
             for u in range(2):
                 bias_col[0, 2 * d + u] = cols[:, 2 * u : 2 * u + 1]
 
         for quad in range(P // QUADRANT):
-            nc.scalar.dma_start(
+            queue = nc.sync if quad % 2 == 0 else nc.scalar
+            queue.dma_start(
                 tab_planes[QUADRANT * quad : QUADRANT * quad + PLANE_ROWS * K_PASSES, :].bitcast(I32),
                 tab_scales[:, PLANE_ROWS * quad : PLANE_ROWS * (quad + 1), :].bitcast(I32),
             )
@@ -108,27 +117,28 @@ def tile_list_redline_pair_features_kernel(
         load_tab(0)
         pos1_t = load_list(pos1, "pos1_t")
         pos2_t = load_list(pos2, "pos2_t")
-        load_bias_early(0)
         load_w1(0, 0, PAIR_COLS)
         for a in range(1, K_PASSES):
             load_tab(a)
             load_w1(a, 0, PAIR_COLS)
+        load_bias_early(0)
         for a in range(K_PASSES):
             load_w1(a, PAIR_COLS, PAIR_COLS)
         load_w1(0, PASS, PASS)
         load_bias_early(1)
         load_w1(1, PASS, PASS)
         load_w1(2, PASS, PASS)
-        bias_late = held([P, PACK], F32, "bias_late")
-        nc.sync.dma_start(bias_late[:], b1[PASS : 2 * PASS].rearrange("(p t) -> p t", t=PACK))
-        for t in range(PACK):
+        b1_late = b1[PASS : 2 * PASS].rearrange("(p t) -> p t", t=PACK)
+        bias_late = held([P, PACK - 1], F32, "bias_late")
+        nc.sync.dma_start(bias_late[:], b1_late[:, 0 : PACK - 1])
+        for t in range(PACK - 1):
             bias_col[1, t] = bias_late[:, t : t + 1]
         load_wu(0, "tab0")
 
         v_words, w1_codes, w1_planes, h_acc, h = {}, {}, {}, {}, {}
 
         def gather_words(a):
-            v_words[a] = held([P, S], U32, "v%d" % a)
+            v_words[a] = held([P, S], U32, "tab_planes" if a == 1 else "v%d" % a)
             width = BANK if a == LAST else S
             for c0 in range(0, S, width):
                 entries = offs_t[:, c0 // LIST_ROWS : (c0 + width) // LIST_ROWS]
@@ -140,24 +150,38 @@ def tile_list_redline_pair_features_kernel(
         def planes_slot(a, b, d):
             return "w1_planes_%d_%d_%d" % (a, b, d)
 
-        def quantise_w1(a, b, d, slot=None, copy=nc.scalar.copy):
+        def quantise_w1(a, b, d, slot=None, copy=nc.scalar.copy, room=1):
             if slot is not None:
-                grouped = held([P, PAIR_COLS * PACK], BF16, slot)
+                grouped = held([P, room * PAIR_COLS * PACK], BF16, slot)[:, 0 : PAIR_COLS * PACK]
             else:
-                grouped = stage.tile([P, PAIR_COLS * PACK], BF16, name="grouped", align_bytes=ALIGN, bufs=4)
+                grouped = stage.tile([P, PAIR_COLS * PACK], BF16, name="grouped", align_bytes=ALIGN, bufs=4)[:]
             if b == 0:
                 copy(
-                    grouped[:].rearrange("p (u side w j) -> p u w j side", u=2, side=2, j=PACK),
+                    grouped.rearrange("p (u side w j) -> p u w j side", u=2, side=2, j=PACK),
                     w1_raw[a, d * PAIR_COLS][:].rearrange("p j (w u side) -> p u w j side", u=2, side=2),
                 )
             else:
                 copy(
-                    grouped[:].rearrange("p (t w j) -> p w j t", t=2, j=PACK),
+                    grouped.rearrange("p (t w j) -> p w j t", t=2, j=PACK),
                     w1_raw[a, PASS][:].rearrange("p j (w t) -> p w j t", t=PACK)[:, :, :, 2 * d : 2 * d + 2],
                 )
             w1_codes[a, b, d] = held([P, PAIR_COLS], U32, codes_slot(a, b, d))
             w1_planes[a, b, d] = held([P, PAIR_COLS], U8, planes_slot(a, b, d))
-            nc.vector.quantize_mx(out=w1_codes[a, b, d][:].bitcast(FP8X4), scales=w1_planes[a, b, d][:], in_=grouped[:])
+            nc.vector.quantize_mx(out=w1_codes[a, b, d][:].bitcast(FP8X4), scales=w1_planes[a, b, d][:], in_=grouped)
+
+        def quantise_first_tiles():
+            w1_codes[LAST, 0, 0] = held([P, PAIR_COLS], U32, codes_slot(LAST, 0, 0))
+            w1_planes[LAST, 0, 0] = held([P, PAIR_COLS], U8, planes_slot(LAST, 0, 0))
+            for u in range(2):
+                grouped = held([P, P * PACK], BF16, "grouped_tile%d" % u)
+                nc.scalar.copy(
+                    grouped[:].rearrange("p (side w j) -> p w j side", side=2, j=PACK),
+                    w1_raw[LAST, 0][:].rearrange("p j (w u side) -> p u w j side", u=2, side=2)[:, u, :, :, :],
+                )
+                cols = slice(u * P, (u + 1) * P)
+                nc.vector.quantize_mx(
+                    out=w1_codes[LAST, 0, 0][:, cols].bitcast(FP8X4), scales=w1_planes[LAST, 0, 0][:, cols], in_=grouped[:]
+                )
 
         def h_pass(a, b, d):
             for t in (2 * d, 2 * d + 1):
@@ -181,7 +205,7 @@ def tile_list_redline_pair_features_kernel(
                 h_pass(a, b, d)
 
         def relu(b, t, share_with_vector=False, slot=None):
-            h[b, t] = held([P, S], F32, slot or "h%d_%d" % (b, t))
+            h[b, t] = held([P, S], F32, "h%d_%d" % (b, t) if slot is None else slot)
             for part in range(S // BANK):
                 dst = h[b, t][:, part * BANK : (part + 1) * BANK]
                 if share_with_vector and part == 1:
@@ -189,12 +213,17 @@ def tile_list_redline_pair_features_kernel(
                 else:
                     nc.scalar.activation(dst, h_acc[b, t, part][:], ACT.Relu, bias=bias_col[b, t])
 
-        z_early = held([P, PACK, M], F32, "z_early")
-        old_late = held([P, PACK, M], F32, "tab1")
-        new_late = [held([P, PACK, MH], F32, slot) for slot in ("tab2", "new_late1")]
+        z_early_slot = raw_slot(1, PAIR_COLS)
+        z_early = held([P, PACK, M], F32, z_early_slot)
+        z_late_slots = ("tab1", "tab2")
+        z_late = [held([P, PACK, MH], F32, slot) for slot in z_late_slots]
+        halves = [slice(e * MH, (e + 1) * MH) for e in range(2)]
 
         def half_list(offsets, e):
             return offsets[:, e * MH // LIST_ROWS : (e + 1) * MH // LIST_ROWS]
+
+        def old_slot(b, t, e):
+            return ("old%d_%d" if b == 0 else "old_late%d_%d") % (t, e)
 
         def pick_old(b, t, e, old):
             nc.vector.tensor_copy(old, h[b, t][:].indirect(half_list(pos1_t, e)))
@@ -202,39 +231,33 @@ def tile_list_redline_pair_features_kernel(
         def pick_new(b, t, e, old, dst):
             nc.vector.tensor_tensor(dst, h[b, t][:].indirect(half_list(pos2_t, e)), old, ALU.subtract)
 
-        def differences(b, t, dst, slot):
-            old = [held([P, MH], F32, slot[e]) for e in range(2)]
+        def differences_by_halves(b, t, dst):
+            old = [held([P, MH], F32, old_slot(b, t, e)) for e in range(2)]
             for e in range(2):
                 pick_old(b, t, e, old[e][:])
             for e in range(2):
                 pick_new(b, t, e, old[e][:], dst[e])
 
-        def early_differences(t, slot, z_slot=None):
-            z_tile = held([P, M], F32, "z_tile%d" % t if z_slot is None else z_slot)
-            differences(0, t, [z_tile[:, e * MH : (e + 1) * MH] for e in range(2)], slot)
+        def move_early(t, z_tile):
             d, u = divmod(t, 2)
-            for side in range(2):
+            for side in range(1 - d, 2):
                 nc.sync.dma_start(
                     z_early[SIDE * d : SIDE * (d + 1), 2 * u + side, :], z_tile[SIDE * side : SIDE * (side + 1), :]
                 )
 
-        def pick_old_late(t, changes):
-            entries = pos1_t[:, changes.start // LIST_ROWS : changes.stop // LIST_ROWS]
-            nc.vector.tensor_copy(old_late[:, t, changes], h[1, t][:].indirect(entries))
+        def early_differences(t, z_tile):
+            old = held([P, M], F32, "old%d" % t)
+            nc.vector.tensor_copy(old[:], h[0, t][:].indirect(pos1_t[:]))
+            nc.vector.tensor_tensor(z_tile, h[0, t][:].indirect(pos2_t[:]), old[:], ALU.subtract)
+            move_early(t, z_tile)
 
-        def pick_new_late(t, e):
-            nc.vector.tensor_copy(new_late[e][:, t, :], h[1, t][:].indirect(half_list(pos2_t, e)))
+        def late_differences(t):
+            differences_by_halves(1, t, [z_late[e][:, t, :] for e in range(2)])
 
-        def subtract_and_group(e, slot):
-            changes = slice(e * MH, (e + 1) * MH)
-            grouped = held([P, MH * PACK], BF16, slot)
-            nc.vector.tensor_tensor(
-                grouped[:].rearrange("p (c x j) -> p c j x", x=2, j=PACK),
-                new_late[e][:].rearrange("p j (c x) -> p c j x", x=2),
-                old_late[:, :, changes].rearrange("p j (c x) -> p c j x", x=2),
-                ALU.subtract,
-            )
-            return grouped[:]
+        def first_half_difference(t, slot):
+            old = held([P, MH], F32, slot)
+            pick_old(1, t, 0, old[:])
+            pick_new(1, t, 0, old[:], z_late[0][:, t, :])
 
         def round_and_group(src, slot, copy):
             grouped = held([P, src.shape[2] * PACK], BF16, slot)
@@ -255,63 +278,69 @@ def tile_list_redline_pair_features_kernel(
         def quantise_z(b, changes, grouped):
             nc.vector.quantize_mx(out=z_codes[b][:, changes].bitcast(FP8X4), scales=z_planes[b][:, changes], in_=grouped)
 
-        def quantise_wu(b, slot):
-            grouped = round_and_group(wu_raw[b][:], slot, nc.scalar.copy)
-            nc.vector.quantize_mx(out=wu_codes[b][:].bitcast(FP8X4), scales=wu_planes[b][:], in_=grouped)
+        def quantise_wu(b, x, slot):
+            cols = slice(x * NH, (x + 1) * NH)
+            grouped = round_and_group(wu_raw[b][:, :, cols], slot, nc.scalar.copy)
+            nc.vector.quantize_mx(out=wu_codes[b][:, cols].bitcast(FP8X4), scales=wu_planes[b][:, cols], in_=grouped)
 
         for a in range(K_PASSES):
             gather_words(a)
             if a == 0:
                 v_planes = held([P, S], U8, "v_planes")
                 nc.vector.tensor_copy(v_planes[:], tab_planes[:].indirect(offs_t[:]))
-            quantise_w1(a, 0, 0)
+            if a < LAST:
+                quantise_w1(a, 0, 0)
+            else:
+                quantise_first_tiles()
             h_pass(a, 0, 0)
 
         quantise_w1(0, 0, 1, slot="grouped_first", copy=nc.vector.tensor_copy)
-        relu(0, 0)
+        relu(0, 0, share_with_vector=True, slot=raw_slot(0, PAIR_COLS))
         quantise_w1(1, 0, 1, slot=codes_slot(LAST, 0, 0))
-        early_differences(0, ["w1_raw_%d_%d" % (0, PAIR_COLS), "grouped_first"], z_slot="w1_raw_%d_%d" % (1, PAIR_COLS))
+        early_differences(0, z_early[:, 0, :])
         quantise_w1(2, 0, 1, slot=planes_slot(LAST, 0, 0))
         h_passes(0, 1)
-        relu(0, 1, slot="w1_raw_%d_%d" % (LAST, PAIR_COLS))
-        early_differences(1, ["old1_0", "old1_1"])
+        relu(0, 1, slot=raw_slot(LAST, PAIR_COLS))
+        differences_by_halves(0, 1, [z_early[:, 2, changes] for changes in halves])
+        move_early(1, z_early[:, 2, :])
         quantise_w1(0, 1, 0)
         quantise_w1(0, 1, 1, slot=codes_slot(1, 0, 1))
         relu(0, 2)
-        early_differences(2, ["old2_0", "old2_1"])
-        relu(0, 3)
-        quantise_w1(1, 1, 0)
-        quantise_w1(2, 1, 0, slot=1024)
+        quantise_w1(1, 1, 0, slot=AT_PASS1, room=3)
+        early_differences(2, held([P, M], F32, AT_PASS1)[:])
+        relu(0, 3, slot=AT_H3)
+        quantise_w1(2, 1, 0, slot=AT_PASS2, room=2)
         h_passes(1, 0)
-        early_differences(3, ["old3_0", "old3_1"], z_slot=0)
-        load_wu(1, "z_tile1")
-        wg_t = held([P, R_PASSES, 2 * N], U8, "wg_t")
+        early_differences(3, held([P, M], F32, AT_PASS2)[:])
+
+        bias_last = held([P, 1], F32, AT_H3 + GROUPED_BYTES)
+        nc.sync.dma_start(bias_last[:], b1_late[:, PACK - 1 : PACK])
+        bias_col[1, PACK - 1] = bias_last[:]
+
+        load_wu(1, "old%d" % (PACK - 1))
+        wg_t = held([P, R_PASSES, 2 * N], U8, AT_H3)
         nc.sync.dma_start(wg_t[:].bitcast(I32), wg_words.rearrange("b p c -> p b c").bitcast(I32))
         for quad in range(P // QUADRANT):
             load_wg_planes(quad)
         pos3_t = load_list(pos3, "pos3_t")
         pos4_t = load_list(pos4, "pos4_t")
-        quantise_w1(1, 1, 1, slot=2048)
-        relu(1, 0)
-        whole = slice(0, M)
-        halves = [slice(e * MH, (e + 1) * MH) for e in range(2)]
-        pick_old_late(0, whole)
-        pick_new_late(0, 0)
-        pick_new_late(0, 1)
+
+        quantise_wu(0, 0, "wu_first")
+        quantise_w1(1, 1, 1, slot=AT_NEXT_WEIGHTS)
+        relu(1, 0, share_with_vector=True)
+        late_differences(0)
         quantise_w1(2, 1, 1, slot=planes_slot(LAST, 1, 0))
         h_passes(1, 1)
         relu(1, 1)
-        pick_old_late(1, whole)
-        pick_new_late(1, 0)
-        pick_new_late(1, 1)
-        quantise_wu(0, codes_slot(LAST, 1, 0))
-        relu(1, 2)
-        pick_new_late(2, 0)
-        pick_old_late(2, whole)
+        late_differences(1)
+        quantise_wu(0, 1, codes_slot(LAST, 1, 0))
+
+        last_pair = (PACK - 2, PACK - 1)
+        relu(1, last_pair[0])
+        first_half_difference(last_pair[0], old_slot(1, 0, 0))
         quantise_z(0, halves[0], round_and_group(z_early[:, :, halves[0]], planes_slot(LAST, 1, 1), nc.scalar.copy))
-        relu(1, 3)
-        pick_new_late(3, 0)
-        pick_old_late(3, halves[0])
+        relu(1, last_pair[1])
+        first_half_difference(last_pair[1], old_slot(1, 0, 1))
 
         gate, lin = {}, {}
 
@@ -347,27 +376,19 @@ def tile_list_redline_pair_features_kernel(
                     )
 
         second_pass(0, 0, opens=True)
-        z_first_grouped = subtract_and_group(0, "z_first_grouped")
-        pick_old_late(3, halves[1])
-        quantise_z(1, halves[0], z_first_grouped)
-        def quantise_wu_half(x, slot):
-            cols = slice(x * N // 2, (x + 1) * N // 2)
-            grouped = round_and_group(wu_raw[1][:, :, cols], slot, nc.scalar.copy)
-            nc.vector.quantize_mx(out=wu_codes[1][:, cols].bitcast(FP8X4), scales=wu_planes[1][:, cols], in_=grouped)
-
-        quantise_wu_half(0, codes_slot(LAST, 1, 1))
-        z_part = new_late[1][:, 2:PACK, :].rearrange("p t m -> p (t m)").bitcast(BF16)
-        nc.scalar.copy(
-            z_part.rearrange("p (c x j) -> p c j x", x=2, j=PACK),
-            z_early[:, :, halves[1]].rearrange("p j (c x) -> p c j x", x=2),
-        )
-        quantise_z(0, halves[1], z_part)
-        quantise_wu_half(1, "v2")
-        second_pass(1, 0, opens=False)
+        quantise_z(0, halves[1], round_and_group(z_early[:, :, halves[1]], "v%d" % LAST, nc.scalar.copy))
         second_pass(0, 1, opens=True)
-        for t in (2, 3):
-            pick_new_late(t, 1)
-        quantise_z(1, halves[1], subtract_and_group(1, "z_last_grouped"))
+        old_second = held([P, 2, MH], F32, z_early_slot)
+        for x, t in enumerate(last_pair):
+            pick_old(1, t, 1, old_second[:, x, :])
+        for x, t in enumerate(last_pair):
+            pick_new(1, t, 1, old_second[:, x, :], z_late[1][:, t, :])
+        quantise_wu(1, 0, codes_slot(LAST, 1, 1))
+        quantise_z(1, halves[0], round_and_group(z_late[0][:], "z_first_grouped", nc.scalar.copy))
+        z_last_grouped = round_and_group(z_late[1][:], z_late_slots[0], nc.vector.tensor_copy)
+        quantise_wu(1, 1, "v_planes")
+        second_pass(1, 0, opens=False)
+        quantise_z(1, halves[1], z_last_grouped)
         second_pass(1, 1, opens=False)
 
         y = [held([P, M], F32, "y%d" % i) for i in range(N_TILES)]

@@ -32,9 +32,17 @@ PAIR_COLS = 2 * P
 MH = M // 2
 N_TILES = N // P
 NH = N // 2
+LAST_CUT = 3 * S // 4
 BIAS_RUN = 3
 GROUPED_BYTES = PAIR_COLS * PACK * 2
-AT_PASS1, AT_H3, AT_PASS2, AT_NEXT_WEIGHTS = 0, GROUPED_BYTES, 3 * GROUPED_BYTES, 4 * GROUPED_BYTES
+H_BYTES = S * 4
+RAW_BYTES = PACK * PASS * 4
+AT_THIRD_PASS1 = 0
+AT_FOURTH = AT_THIRD_PASS1 + GROUPED_BYTES
+AT_H4 = AT_FOURTH + 2 * GROUPED_BYTES
+AT_BIAS3 = AT_H4 - ALIGN
+AT_RAW1 = AT_H4 + H_BYTES
+AT_RAW2 = AT_RAW1 + RAW_BYTES
 
 
 def tile_list_redline_pair_features_kernel(
@@ -75,8 +83,8 @@ def tile_list_redline_pair_features_kernel(
         def raw_slot(a, first_col):
             return "w1_raw_%d_%d" % (a, first_col)
 
-        def load_w1(a, first_col, width):
-            raw = held([P, PACK, width], F32, raw_slot(a, first_col))
+        def load_w1(a, first_col, width, slot=None):
+            raw = held([P, PACK, width], F32, raw_slot(a, first_col) if slot is None else slot)
             rows = w1[a * PASS : (a + 1) * PASS, first_col : first_col + width]
             nc.sync.dma_start(raw[:], rows.rearrange("(p j) c -> p j c", j=PACK))
             w1_raw[a, first_col] = raw
@@ -100,6 +108,14 @@ def tile_list_redline_pair_features_kernel(
                 nc.sync.dma_start(cols[SIDE * side : SIDE * (side + 1), :], b1_early[:, d, side : side + BIAS_RUN])
             for u in range(2):
                 bias_col[0, 2 * d + u] = cols[:, 2 * u : 2 * u + 1]
+
+        def load_bias_of_tile(t, slot, width):
+            d, u = divmod(t, 2)
+            cols = held([P, width], F32, slot)
+            for side in range(2):
+                x = 2 * u + side
+                nc.sync.dma_start(cols[SIDE * side : SIDE * (side + 1), 0:1], b1_early[:, d, x : x + 1])
+            bias_col[0, t] = cols[:, 0:1]
 
         for quad in range(P // QUADRANT):
             queue = nc.sync if quad % 2 == 0 else nc.scalar
@@ -125,24 +141,32 @@ def tile_list_redline_pair_features_kernel(
         for a in range(K_PASSES):
             load_w1(a, PAIR_COLS, PAIR_COLS)
         load_w1(0, PASS, PASS)
-        load_bias_early(1)
-        load_w1(1, PASS, PASS)
-        load_w1(2, PASS, PASS)
+        load_bias_of_tile(2, "bias2", 1)
+        load_w1(1, PASS, PASS, slot=AT_RAW1)
+        load_w1(2, PASS, PASS, slot=AT_RAW2)
+        load_bias_of_tile(3, AT_BIAS3, 2 * ALIGN // 4)
         b1_late = b1[PASS : 2 * PASS].rearrange("(p t) -> p t", t=PACK)
-        bias_late = held([P, PACK - 1], F32, "bias_late")
-        nc.sync.dma_start(bias_late[:], b1_late[:, 0 : PACK - 1])
-        for t in range(PACK - 1):
+        bias_late = held([P, PACK], F32, "bias_late")
+        nc.sync.dma_start(bias_late[:], b1_late)
+        for t in range(PACK):
             bias_col[1, t] = bias_late[:, t : t + 1]
         load_wu(0, "tab0")
 
         v_words, w1_codes, w1_planes, h_acc, h = {}, {}, {}, {}, {}
 
-        def gather_words(a):
-            v_words[a] = held([P, S], U32, "tab_planes" if a == 1 else "v%d" % a)
-            width = BANK if a == LAST else S
-            for c0 in range(0, S, width):
-                entries = offs_t[:, c0 // LIST_ROWS : (c0 + width) // LIST_ROWS]
-                nc.vector.tensor_copy(v_words[a][:, c0 : c0 + width], tab[a][:].bitcast(U32).indirect(entries))
+        def gather_words(a, first, end, slot):
+            words = held([P, end - first], U32, slot)
+            entries = offs_t[:, first // LIST_ROWS : end // LIST_ROWS]
+            nc.vector.tensor_copy(words[:], tab[a][:].bitcast(U32).indirect(entries))
+            v_words.setdefault(a, []).append((first, end, words))
+
+        def runs_of_bank(a, part):
+            for_bank = []
+            for first, end, words in v_words[a]:
+                lo, hi = max(first, part * BANK), min(end, (part + 1) * BANK)
+                if lo < hi:
+                    for_bank.append((lo, hi, words[:, lo - first : hi - first]))
+            return for_bank
 
         def codes_slot(a, b, d):
             return "w1_codes_%d_%d_%d" % (a, b, d)
@@ -173,6 +197,8 @@ def tile_list_redline_pair_features_kernel(
             w1_codes[LAST, 0, 0] = held([P, PAIR_COLS], U32, codes_slot(LAST, 0, 0))
             w1_planes[LAST, 0, 0] = held([P, PAIR_COLS], U8, planes_slot(LAST, 0, 0))
             for u in range(2):
+                if u == 1:
+                    gather_words(LAST, LAST_CUT, S, "grouped_tile0")
                 grouped = held([P, P * PACK], BF16, "grouped_tile%d" % u)
                 nc.scalar.copy(
                     grouped[:].rearrange("p (side w j) -> p w j side", side=2, j=PACK),
@@ -189,16 +215,16 @@ def tile_list_redline_pair_features_kernel(
                 for part in range(S // BANK):
                     if a == 0:
                         h_acc[b, t, part] = bank(2 * t + part)
-                    entries = slice(part * BANK, (part + 1) * BANK)
-                    nc.tensor.matmul_mx(
-                        out=h_acc[b, t, part][:],
-                        lhsT=w1_codes[a, b, d][:, cols].bitcast(FP8X4),
-                        lhsT_scale=w1_planes[a, b, d][:, cols],
-                        rhs=v_words[a][:, entries].bitcast(FP8X4),
-                        rhs_scale=v_planes[PLANE_ROWS * a : P, entries],
-                        start=(a == 0),
-                        stop=(a == LAST),
-                    )
+                    for lo, hi, words in runs_of_bank(a, part):
+                        nc.tensor.matmul_mx(
+                            out=h_acc[b, t, part][:, lo - part * BANK : hi - part * BANK],
+                            lhsT=w1_codes[a, b, d][:, cols].bitcast(FP8X4),
+                            lhsT_scale=w1_planes[a, b, d][:, cols],
+                            rhs=words.bitcast(FP8X4),
+                            rhs_scale=v_planes[PLANE_ROWS * a : P, lo:hi],
+                            start=(a == 0),
+                            stop=(a == LAST and hi == (part + 1) * BANK),
+                        )
 
         def h_passes(b, d):
             for a in range(K_PASSES):
@@ -215,8 +241,9 @@ def tile_list_redline_pair_features_kernel(
 
         z_early_slot = raw_slot(1, PAIR_COLS)
         z_early = held([P, PACK, M], F32, z_early_slot)
-        z_late_slots = ("tab1", "tab2")
-        z_late = [held([P, PACK, MH], F32, slot) for slot in z_late_slots]
+        z_late_slots = (AT_RAW1, "tab2")
+        z_late_flat = [held([P, PACK * MH], F32, slot) for slot in z_late_slots]
+        z_late = [flat[:].rearrange("p (j m) -> p j m", j=PACK) for flat in z_late_flat]
         halves = [slice(e * MH, (e + 1) * MH) for e in range(2)]
 
         def half_list(offsets, e):
@@ -254,18 +281,15 @@ def tile_list_redline_pair_features_kernel(
         def late_differences(t):
             differences_by_halves(1, t, [z_late[e][:, t, :] for e in range(2)])
 
-        def first_half_difference(t, slot):
-            old = held([P, MH], F32, slot)
-            pick_old(1, t, 0, old[:])
-            pick_new(1, t, 0, old[:], z_late[0][:, t, :])
-
-        def round_and_group(src, slot, copy):
-            grouped = held([P, src.shape[2] * PACK], BF16, slot)
+        def round_into(grouped, src, copy):
             copy(
-                grouped[:].rearrange("p (c x j) -> p c j x", x=2, j=PACK),
+                grouped.rearrange("p (c x j) -> p c j x", x=2, j=PACK),
                 src.rearrange("p j (c x) -> p c j x", x=2),
             )
-            return grouped[:]
+            return grouped
+
+        def round_and_group(src, slot, copy):
+            return round_into(held([P, src.shape[2] * PACK], BF16, slot)[:], src, copy)
 
         z_codes, z_planes, wu_codes, wu_planes = {}, {}, {}, {}
         for b in range(R_PASSES):
@@ -284,7 +308,7 @@ def tile_list_redline_pair_features_kernel(
             nc.vector.quantize_mx(out=wu_codes[b][:, cols].bitcast(FP8X4), scales=wu_planes[b][:, cols], in_=grouped)
 
         for a in range(K_PASSES):
-            gather_words(a)
+            gather_words(a, 0, LAST_CUT if a == LAST else S, "tab_planes" if a == 1 else "v%d" % a)
             if a == 0:
                 v_planes = held([P, S], U8, "v_planes")
                 nc.vector.tensor_copy(v_planes[:], tab_planes[:].indirect(offs_t[:]))
@@ -295,7 +319,7 @@ def tile_list_redline_pair_features_kernel(
             h_pass(a, 0, 0)
 
         quantise_w1(0, 0, 1, slot="grouped_first", copy=nc.vector.tensor_copy)
-        relu(0, 0, share_with_vector=True, slot=raw_slot(0, PAIR_COLS))
+        relu(0, 0)
         quantise_w1(1, 0, 1, slot=codes_slot(LAST, 0, 0))
         early_differences(0, z_early[:, 0, :])
         quantise_w1(2, 0, 1, slot=planes_slot(LAST, 0, 0))
@@ -304,88 +328,84 @@ def tile_list_redline_pair_features_kernel(
         differences_by_halves(0, 1, [z_early[:, 2, changes] for changes in halves])
         move_early(1, z_early[:, 2, :])
         quantise_w1(0, 1, 0)
-        quantise_w1(0, 1, 1, slot=codes_slot(1, 0, 1))
         relu(0, 2)
-        quantise_w1(1, 1, 0, slot=AT_PASS1, room=3)
-        early_differences(2, held([P, M], F32, AT_PASS1)[:])
-        relu(0, 3, slot=AT_H3)
-        quantise_w1(2, 1, 0, slot=AT_PASS2, room=2)
+        quantise_w1(1, 1, 0, slot=AT_THIRD_PASS1)
+        early_differences(2, held([P, M], F32, AT_THIRD_PASS1)[:])
+        quantise_w1(2, 1, 0)
         h_passes(1, 0)
-        early_differences(3, held([P, M], F32, AT_PASS2)[:])
-
-        bias_last = held([P, 1], F32, AT_H3 + GROUPED_BYTES)
-        nc.sync.dma_start(bias_last[:], b1_late[:, PACK - 1 : PACK])
-        bias_col[1, PACK - 1] = bias_last[:]
+        relu(0, 3)
+        quantise_w1(0, 1, 1, slot=AT_FOURTH, room=2)
+        early_differences(3, held([P, M], F32, raw_slot(0, PASS))[:])
 
         load_wu(1, "old%d" % (PACK - 1))
-        wg_t = held([P, R_PASSES, 2 * N], U8, AT_H3)
+        wg_t = held([P, R_PASSES, 2 * N], U8, "h0_%d" % (PACK - 1))
         nc.sync.dma_start(wg_t[:].bitcast(I32), wg_words.rearrange("b p c -> p b c").bitcast(I32))
         for quad in range(P // QUADRANT):
             load_wg_planes(quad)
         pos3_t = load_list(pos3, "pos3_t")
         pos4_t = load_list(pos4, "pos4_t")
 
-        quantise_wu(0, 0, "wu_first")
-        quantise_w1(1, 1, 1, slot=AT_NEXT_WEIGHTS)
-        relu(1, 0, share_with_vector=True)
-        late_differences(0)
-        quantise_w1(2, 1, 1, slot=planes_slot(LAST, 1, 0))
+        relu(1, 0, slot=AT_H4)
+        quantise_w1(1, 1, 1, slot=AT_FOURTH)
+        old = held([P, M], F32, "old_late0")
+        nc.vector.tensor_copy(old[:], h[1, 0][:].indirect(pos1_t[:]))
+        for e in range(2):
+            pick_new(1, 0, e, old[:, halves[e]], z_late[e][:, 0, :])
+        quantise_w1(2, 1, 1, slot=AT_FOURTH + GROUPED_BYTES)
         h_passes(1, 1)
-        relu(1, 1)
+        relu(1, 1, slot=AT_RAW1 + H_BYTES)
         late_differences(1)
-        quantise_wu(0, 1, codes_slot(LAST, 1, 0))
+        for x in range(2):
+            quantise_wu(0, x, AT_RAW2 + x * GROUPED_BYTES)
 
         last_pair = (PACK - 2, PACK - 1)
-        relu(1, last_pair[0])
-        first_half_difference(last_pair[0], old_slot(1, 0, 0))
-        quantise_z(0, halves[0], round_and_group(z_early[:, :, halves[0]], planes_slot(LAST, 1, 1), nc.scalar.copy))
-        relu(1, last_pair[1])
-        first_half_difference(last_pair[1], old_slot(1, 0, 1))
+        old_last = {}
+        for t in last_pair:
+            relu(1, t)
+            old_last[t] = held([P, M], F32, "old_last%d" % t)
+            nc.vector.tensor_copy(old_last[t][:], h[1, t][:].indirect(pos1_t[:]))
 
-        gate, lin = {}, {}
+        def early_half_then_last_differences(e):
+            grouped = z_late_flat[e][:, last_pair[0] * MH : PACK * MH].bitcast(BF16)
+            quantise_z(0, halves[e], round_into(grouped, z_early[:, :, halves[e]], nc.scalar.copy))
+            second_pass(0, e, opens=True)
+            for t in last_pair:
+                pick_new(1, t, e, old_last[t][:, halves[e]], z_late[e][:, t, :])
+
+        acc = {}
+        gate_cols, lin_cols = slice(0, MH), slice(MH, 2 * MH)
 
         def second_pass(b, e, opens):
-            for pair in range(N_TILES // 2):
+            for i in range(N_TILES):
                 if opens:
-                    gate[e, pair] = bank(4 * e + 2 * pair)
-                    lin[e, pair] = bank(4 * e + 2 * pair + 1)
-                for x in range(2):
-                    i = 2 * pair + x
-                    for c0 in range(0, MH, P):
-                        changes = slice(e * MH + c0, e * MH + c0 + P)
-                        nc.tensor.matmul_mx(
-                            out=gate[e, pair][:, x * MH + c0 : x * MH + c0 + P],
-                            lhsT=wg_t[:, b, 2 * i * P : 2 * (i + 1) * P].bitcast(FP4X4),
-                            lhsT_scale=wg_planes[:, b * N + i * P : b * N + (i + 1) * P],
-                            rhs=z_codes[b][:, changes].bitcast(FP8X4),
-                            rhs_scale=z_planes[b][:, changes],
-                            start=(opens and x == 0 and c0 == 0),
-                            stop=(not opens and x == 1 and c0 == MH - P),
-                        )
-                for x in range(2):
-                    cols = slice((2 * pair + x) * P, (2 * pair + x + 1) * P)
-                    changes = slice(e * MH, (e + 1) * MH)
+                    acc[e, i] = bank(N_TILES * e + i)
+                for c0 in range(0, MH, P):
+                    changes = slice(e * MH + c0, e * MH + c0 + P)
                     nc.tensor.matmul_mx(
-                        out=lin[e, pair][:, x * MH : (x + 1) * MH],
-                        lhsT=wu_codes[b][:, cols].bitcast(FP8X4),
-                        lhsT_scale=wu_planes[b][:, cols],
+                        out=acc[e, i][:, c0 : c0 + P],
+                        lhsT=wg_t[:, b, 2 * i * P : 2 * (i + 1) * P].bitcast(FP4X4),
+                        lhsT_scale=wg_planes[:, b * N + i * P : b * N + (i + 1) * P],
                         rhs=z_codes[b][:, changes].bitcast(FP8X4),
                         rhs_scale=z_planes[b][:, changes],
-                        start=(opens and x == 0),
-                        stop=(not opens and x == 1),
+                        start=(opens and c0 == 0),
+                        stop=False,
                     )
+                cols = slice(i * P, (i + 1) * P)
+                nc.tensor.matmul_mx(
+                    out=acc[e, i][:, lin_cols],
+                    lhsT=wu_codes[b][:, cols].bitcast(FP8X4),
+                    lhsT_scale=wu_planes[b][:, cols],
+                    rhs=z_codes[b][:, halves[e]].bitcast(FP8X4),
+                    rhs_scale=z_planes[b][:, halves[e]],
+                    start=False,
+                    stop=not opens,
+                )
 
-        second_pass(0, 0, opens=True)
-        quantise_z(0, halves[1], round_and_group(z_early[:, :, halves[1]], "v%d" % LAST, nc.scalar.copy))
-        second_pass(0, 1, opens=True)
-        old_second = held([P, 2, MH], F32, z_early_slot)
-        for x, t in enumerate(last_pair):
-            pick_old(1, t, 1, old_second[:, x, :])
-        for x, t in enumerate(last_pair):
-            pick_new(1, t, 1, old_second[:, x, :], z_late[1][:, t, :])
+        for e in range(2):
+            early_half_then_last_differences(e)
         quantise_wu(1, 0, codes_slot(LAST, 1, 1))
-        quantise_z(1, halves[0], round_and_group(z_late[0][:], "z_first_grouped", nc.scalar.copy))
-        z_last_grouped = round_and_group(z_late[1][:], z_late_slots[0], nc.vector.tensor_copy)
+        quantise_z(1, halves[0], round_and_group(z_late[0], "z_first_grouped", nc.scalar.copy))
+        z_last_grouped = round_and_group(z_late[1], z_late_slots[0], nc.vector.tensor_copy)
         quantise_wu(1, 1, "v_planes")
         second_pass(1, 0, opens=False)
         quantise_z(1, halves[1], z_last_grouped)
@@ -394,11 +414,12 @@ def tile_list_redline_pair_features_kernel(
         y = [held([P, M], F32, "y%d" % i) for i in range(N_TILES)]
         silu, first = {}, {}
 
+        def make_silu(e, i):
+            silu[e, i] = held([P, MH], F32, "silu%d_%d" % (e, i))
+            nc.scalar.activation(silu[e, i][:], acc[e, i][:, gate_cols], ACT.Silu)
+
         def make_y(e, i):
-            cols = slice((i % 2) * MH, (i % 2 + 1) * MH)
-            nc.vector.tensor_tensor(
-                y[i][:, e * MH : (e + 1) * MH], lin[e, i // 2][:, cols], silu[e, i // 2][:, cols], ALU.mult
-            )
+            nc.vector.tensor_tensor(y[i][:, halves[e]], acc[e, i][:, lin_cols], silu[e, i][:], ALU.mult)
 
         def pick_first(i):
             first[i] = stage.tile([P, M2], F32, name="first", align_bytes=ALIGN)
@@ -410,9 +431,8 @@ def tile_list_redline_pair_features_kernel(
             nc.sync.dma_start(out[i * P : (i + 1) * P, :], result[:])
 
         for e in range(2):
-            for pair in range(N_TILES // 2):
-                silu[e, pair] = held([P, BANK], F32, "silu%d_%d" % (e, pair))
-                nc.scalar.activation(silu[e, pair][:], gate[e, pair][:], ACT.Silu)
+            for i in range(N_TILES):
+                make_silu(e, i)
         for i in range(N_TILES):
             make_y(0, i)
         for step in range(N_TILES + 2):

@@ -131,15 +131,16 @@ def tile_list_redline_pair_features_kernel(
 
         offs_t = load_list(offs, "offs_t")
         load_tab(0)
-        pos1_t = load_list(pos1, "pos1_t")
-        pos2_t = load_list(pos2, "pos2_t")
         load_w1(0, 0, PAIR_COLS)
         for a in range(1, K_PASSES):
             load_tab(a)
             load_w1(a, 0, PAIR_COLS)
         load_bias_early(0)
-        for a in range(K_PASSES):
-            load_w1(a, PAIR_COLS, PAIR_COLS)
+        load_w1(0, PAIR_COLS, PAIR_COLS)
+        pos1_t = load_list(pos1, "pos1_t")
+        load_w1(1, PAIR_COLS, PAIR_COLS)
+        pos2_t = load_list(pos2, "pos2_t")
+        load_w1(2, PAIR_COLS, PAIR_COLS)
         load_w1(0, PASS, PASS)
         load_bias_of_tile(2, "bias2", 1)
         load_w1(1, PASS, PASS, slot=AT_RAW1)

@@ -135,8 +135,8 @@ def tile_list_redline_pair_features_kernel(
         for a in range(1, K_PASSES):
             load_tab(a)
             load_w1(a, 0, PAIR_COLS)
-        load_bias_early(0)
         load_w1(0, PAIR_COLS, PAIR_COLS)
+        load_bias_early(0)
         pos1_t = load_list(pos1, "pos1_t")
         load_w1(1, PAIR_COLS, PAIR_COLS)
         pos2_t = load_list(pos2, "pos2_t")
@@ -161,10 +161,15 @@ def tile_list_redline_pair_features_kernel(
             nc.vector.tensor_copy(words[:], tab[a][:].bitcast(U32).indirect(entries))
             v_words.setdefault(a, []).append((first, end, words))
 
-        def runs_of_bank(a, part):
+        def parts_of_tile(b, t):
+            if (b, t) == (0, 0):
+                return [(0, BANK, 0), (BANK, LAST_CUT, 1), (LAST_CUT, S, 2 * PACK - 1)]
+            return [(0, BANK, 2 * t), (BANK, S, 2 * t + 1)]
+
+        def runs_of_part(a, part_first, part_end):
             for_bank = []
             for first, end, words in v_words[a]:
-                lo, hi = max(first, part * BANK), min(end, (part + 1) * BANK)
+                lo, hi = max(first, part_first), min(end, part_end)
                 if lo < hi:
                     for_bank.append((lo, hi, words[:, lo - first : hi - first]))
             return for_bank
@@ -198,13 +203,13 @@ def tile_list_redline_pair_features_kernel(
             w1_codes[LAST, 0, 0] = held([P, PAIR_COLS], U32, codes_slot(LAST, 0, 0))
             w1_planes[LAST, 0, 0] = held([P, PAIR_COLS], U8, planes_slot(LAST, 0, 0))
             for u in range(2):
-                if u == 1:
-                    gather_words(LAST, LAST_CUT, S, "grouped_tile0")
                 grouped = held([P, P * PACK], BF16, "grouped_tile%d" % u)
                 nc.scalar.copy(
                     grouped[:].rearrange("p (side w j) -> p w j side", side=2, j=PACK),
                     w1_raw[LAST, 0][:].rearrange("p j (w u side) -> p u w j side", u=2, side=2)[:, u, :, :, :],
                 )
+                if u == 1:
+                    gather_words(LAST, LAST_CUT, S, raw_slot(LAST, 0))
                 cols = slice(u * P, (u + 1) * P)
                 nc.vector.quantize_mx(
                     out=w1_codes[LAST, 0, 0][:, cols].bitcast(FP8X4), scales=w1_planes[LAST, 0, 0][:, cols], in_=grouped[:]
@@ -213,32 +218,29 @@ def tile_list_redline_pair_features_kernel(
         def h_pass(a, b, d):
             for t in (2 * d, 2 * d + 1):
                 cols = slice((t % 2) * P, (t % 2 + 1) * P)
-                for part in range(S // BANK):
+                for first, end, index in parts_of_tile(b, t):
                     if a == 0:
-                        h_acc[b, t, part] = bank(2 * t + part)
-                    for lo, hi, words in runs_of_bank(a, part):
+                        h_acc[b, t, first] = bank(index)
+                    for lo, hi, words in runs_of_part(a, first, end):
                         nc.tensor.matmul_mx(
-                            out=h_acc[b, t, part][:, lo - part * BANK : hi - part * BANK],
+                            out=h_acc[b, t, first][:, lo - first : hi - first],
                             lhsT=w1_codes[a, b, d][:, cols].bitcast(FP8X4),
                             lhsT_scale=w1_planes[a, b, d][:, cols],
                             rhs=words.bitcast(FP8X4),
                             rhs_scale=v_planes[PLANE_ROWS * a : P, lo:hi],
                             start=(a == 0),
-                            stop=(a == LAST and hi == (part + 1) * BANK),
+                            stop=(a == LAST and hi == end),
                         )
 
         def h_passes(b, d):
             for a in range(K_PASSES):
                 h_pass(a, b, d)
 
-        def relu(b, t, share_with_vector=False, slot=None):
+        def relu(b, t, slot=None):
             h[b, t] = held([P, S], F32, "h%d_%d" % (b, t) if slot is None else slot)
-            for part in range(S // BANK):
-                dst = h[b, t][:, part * BANK : (part + 1) * BANK]
-                if share_with_vector and part == 1:
-                    nc.vector.tensor_scalar(dst, h_acc[b, t, part][:], bias_col[b, t], 0.0, ALU.add, ALU.max)
-                else:
-                    nc.scalar.activation(dst, h_acc[b, t, part][:], ACT.Relu, bias=bias_col[b, t])
+            for first, end, index in parts_of_tile(b, t):
+                acc_part = h_acc[b, t, first][:, 0 : end - first]
+                nc.scalar.activation(h[b, t][:, first:end], acc_part, ACT.Relu, bias=bias_col[b, t])
 
         z_early_slot = raw_slot(1, PAIR_COLS)
         z_early = held([P, PACK, M], F32, z_early_slot)
@@ -319,9 +321,9 @@ def tile_list_redline_pair_features_kernel(
                 quantise_first_tiles()
             h_pass(a, 0, 0)
 
-        quantise_w1(0, 0, 1, slot="grouped_first", copy=nc.vector.tensor_copy)
+        quantise_w1(0, 0, 1)
         relu(0, 0)
-        quantise_w1(1, 0, 1, slot=codes_slot(LAST, 0, 0))
+        quantise_w1(1, 0, 1, slot="grouped_second")
         early_differences(0, z_early[:, 0, :])
         quantise_w1(2, 0, 1, slot=planes_slot(LAST, 0, 0))
         h_passes(0, 1)

@@ -43,6 +43,7 @@ AT_H4 = AT_FOURTH + 2 * GROUPED_BYTES
 AT_BIAS3 = AT_H4 - ALIGN
 AT_RAW1 = AT_H4 + H_BYTES
 AT_RAW2 = AT_RAW1 + RAW_BYTES
+AT_H3 = AT_RAW2 + RAW_BYTES
 
 
 def tile_list_redline_pair_features_kernel(
@@ -299,15 +300,23 @@ def tile_list_redline_pair_features_kernel(
             z_codes[b] = held([P, M], U32, "z_codes%d" % b)
             z_planes[b] = held([P, M], U8, "z_planes%d" % b)
         for b in range(R_PASSES):
-            wu_codes[b] = held([P, N], U32, "wu_codes%d" % b)
+            wu_codes[b] = held([P, N], U32, old_slot(1, 1, 0) if b == 0 else z_late_slots[0])
             wu_planes[b] = held([P, N], U8, "wu_planes%d" % b)
 
         def quantise_z(b, changes, grouped):
             nc.vector.quantize_mx(out=z_codes[b][:, changes].bitcast(FP8X4), scales=z_planes[b][:, changes], in_=grouped)
 
-        def quantise_wu(b, x, slot):
-            cols = slice(x * NH, (x + 1) * NH)
-            grouped = round_and_group(wu_raw[b][:, :, cols], slot, nc.scalar.copy)
+        def round_on_gpsimd(src, slot):
+            grouped = held([P, src.shape[2] * PACK], BF16, slot)[:]
+            by_column = grouped.rearrange("p (c j) -> p c j", j=PACK)
+            nc.gpsimd.tensor_scalar(by_column, src.rearrange("p j c -> p c j"), 1.0, 0.0, ALU.mult, ALU.add)
+            return grouped
+
+        def round_on_scalar(src, slot):
+            return round_and_group(src, slot, nc.scalar.copy)
+
+        def quantise_wu(b, cols, slot, rounding):
+            grouped = rounding(wu_raw[b][:, :, cols], slot)
             nc.vector.quantize_mx(out=wu_codes[b][:, cols].bitcast(FP8X4), scales=wu_planes[b][:, cols], in_=grouped)
 
         for a in range(K_PASSES):
@@ -336,12 +345,12 @@ def tile_list_redline_pair_features_kernel(
         early_differences(2, held([P, M], F32, AT_THIRD_PASS1)[:])
         quantise_w1(2, 1, 0)
         h_passes(1, 0)
-        relu(0, 3)
+        relu(0, 3, slot=AT_H3)
         quantise_w1(0, 1, 1, slot=AT_FOURTH, room=2)
         early_differences(3, held([P, M], F32, raw_slot(0, PASS))[:])
 
         load_wu(1, "old%d" % (PACK - 1))
-        wg_t = held([P, R_PASSES, 2 * N], U8, "h0_%d" % (PACK - 1))
+        wg_t = held([P, R_PASSES, 2 * N], U8, AT_H3)
         nc.sync.dma_start(wg_t[:].bitcast(I32), wg_words.rearrange("b p c -> p b c").bitcast(I32))
         for quad in range(P // QUADRANT):
             load_wg_planes(quad)
@@ -358,8 +367,9 @@ def tile_list_redline_pair_features_kernel(
         h_passes(1, 1)
         relu(1, 1, slot=AT_RAW1 + H_BYTES)
         late_differences(1)
-        for x in range(2):
-            quantise_wu(0, x, AT_RAW2 + x * GROUPED_BYTES)
+        quantise_wu(0, slice(0, P), AT_H3 + GROUPED_BYTES, round_on_gpsimd)
+        quantise_wu(0, slice(P, NH), AT_FOURTH + GROUPED_BYTES, round_on_gpsimd)
+        quantise_wu(0, slice(NH, N), AT_RAW2, round_on_scalar)
 
         last_pair = (PACK - 2, PACK - 1)
         old_last = {}
@@ -406,10 +416,12 @@ def tile_list_redline_pair_features_kernel(
 
         for e in range(2):
             early_half_then_last_differences(e)
-        quantise_wu(1, 0, codes_slot(LAST, 1, 1))
-        quantise_z(1, halves[0], round_and_group(z_late[0], "z_first_grouped", nc.scalar.copy))
-        z_last_grouped = round_and_group(z_late[1], z_late_slots[0], nc.vector.tensor_copy)
-        quantise_wu(1, 1, "v_planes")
+        wu_first = round_on_gpsimd(wu_raw[1][:, :, 0:NH], AT_RAW2)
+        wu_last = round_on_scalar(wu_raw[1][:, :, NH:N], "v_planes")
+        quantise_z(1, halves[0], round_on_scalar(z_late[0], "z_first_grouped"))
+        z_last_grouped = round_on_scalar(z_late[1], "z_last_grouped")
+        for cols, grouped in ((slice(0, NH), wu_first), (slice(NH, N), wu_last)):
+            nc.vector.quantize_mx(out=wu_codes[1][:, cols].bitcast(FP8X4), scales=wu_planes[1][:, cols], in_=grouped)
         second_pass(1, 0, opens=False)
         quantise_z(1, halves[1], z_last_grouped)
         second_pass(1, 1, opens=False)
@@ -424,24 +436,32 @@ def tile_list_redline_pair_features_kernel(
         def make_y(e, i):
             nc.vector.tensor_tensor(y[i][:, halves[e]], acc[e, i][:, lin_cols], silu[e, i][:], ALU.mult)
 
+        def make_y_on_gpsimd(e, i):
+            lin = held([P, MH], F32, "lin%d_%d" % (e, i))
+            nc.scalar.copy(lin[:], acc[e, i][:, lin_cols])
+            nc.gpsimd.tensor_tensor(y[i][:, halves[e]], lin[:], silu[e, i][:], ALU.mult)
+
         def pick_first(i):
-            first[i] = stage.tile([P, M2], F32, name="first", align_bytes=ALIGN)
+            first[i] = held([P, M2], F32, "first%d" % i)
             nc.vector.tensor_copy(first[i][:], y[i][:].indirect(pos3_t[:]))
 
-        def add_second_and_store(i):
-            result = held([P, M2], F32, "result%d" % i)
+        def add_second_and_store(i, slot):
+            result = held([P, M2], F32, slot)
             nc.vector.tensor_tensor(result[:], y[i][:].indirect(pos4_t[:]), first[i][:], ALU.add)
             nc.sync.dma_start(out[i * P : (i + 1) * P, :], result[:])
 
-        for e in range(2):
-            for i in range(N_TILES):
-                make_silu(e, i)
         for i in range(N_TILES):
+            make_silu(0, i)
             make_y(0, i)
-        for step in range(N_TILES + 2):
-            if step < N_TILES:
-                make_y(1, step)
-            if 1 <= step <= N_TILES:
-                pick_first(step - 1)
-            if step >= 2:
-                add_second_and_store(step - 2)
+        for i in range(N_TILES):
+            make_silu(1, i)
+            if i < N_TILES // 2:
+                make_y(1, i)
+            else:
+                make_y_on_gpsimd(1, i)
+        for i in range(N_TILES):
+            pick_first(i)
+        last = N_TILES - 1
+        result_slots = ("silu1_%d" % last, "lin1_%d" % last, "result2", "result3")
+        for i in range(N_TILES):
+            add_second_and_store(i, result_slots[i])

@@ -32,18 +32,16 @@ PAIR_COLS = 2 * P
 MH = M // 2
 N_TILES = N // P
 NH = N // 2
-LAST_CUT = 3 * S // 4
-BIAS_RUN = 3
 GROUPED_BYTES = PAIR_COLS * PACK * 2
 H_BYTES = S * 4
 RAW_BYTES = PACK * PASS * 4
-AT_THIRD_PASS1 = 0
-AT_FOURTH = AT_THIRD_PASS1 + GROUPED_BYTES
-AT_H4 = AT_FOURTH + 2 * GROUPED_BYTES
-AT_BIAS3 = AT_H4 - ALIGN
-AT_RAW1 = AT_H4 + H_BYTES
+AT_RAW1 = 0
 AT_RAW2 = AT_RAW1 + RAW_BYTES
 AT_H3 = AT_RAW2 + RAW_BYTES
+AT_Z3 = AT_H3 + H_BYTES
+AT_THIRD2 = AT_Z3 + GROUPED_BYTES // 2
+AT_FOURTH0 = AT_THIRD2 + GROUPED_BYTES // 2
+AT_LAST_LIN = AT_FOURTH0 + 2 * GROUPED_BYTES
 
 
 def tile_list_redline_pair_features_kernel(
@@ -59,7 +57,7 @@ def tile_list_redline_pair_features_kernel(
 
         def held(shape, dtype, slot):
             if isinstance(slot, int):
-                return placed.tile(shape, dtype, name="placed%d_%d" % (slot, shape[1]), align_bytes=ALIGN, offset=slot)
+                return placed.tile(shape, dtype, name="placed%d_%d_%d" % (slot, shape[1], len(shape)), align_bytes=ALIGN, offset=slot)
             return keep.tile(shape, dtype, name=slot, align_bytes=ALIGN)
 
         def bank(index):
@@ -103,19 +101,15 @@ def tile_list_redline_pair_features_kernel(
 
         b1_early = b1[0:PASS].rearrange("(d w x) -> w d x", d=2, x=PACK)
 
-        def load_bias_early(d):
-            cols = held([P, BIAS_RUN], F32, "bias_early%d" % d)
-            for side in range(2):
-                nc.sync.dma_start(cols[SIDE * side : SIDE * (side + 1), :], b1_early[:, d, side : side + BIAS_RUN])
-            for u in range(2):
-                bias_col[0, 2 * d + u] = cols[:, 2 * u : 2 * u + 1]
-
         def load_bias_of_tile(t, slot, width):
             d, u = divmod(t, 2)
             cols = held([P, width], F32, slot)
-            for side in range(2):
-                x = 2 * u + side
-                nc.sync.dma_start(cols[SIDE * side : SIDE * (side + 1), 0:1], b1_early[:, d, x : x + 1])
+            if d == 0:
+                for side in range(2):
+                    x = 2 * u + side
+                    nc.sync.dma_start(cols[SIDE * side : SIDE * (side + 1), 0:1], b1_early[:, d, x : x + 1])
+            else:
+                nc.sync.dma_start(cols[:, 0:1], b1_early[:, d, 2 * u : 2 * u + 2])
             bias_col[0, t] = cols[:, 0:1]
 
         for quad in range(P // QUADRANT):
@@ -131,13 +125,13 @@ def tile_list_redline_pair_features_kernel(
         nc.scalar.activation(warm_out[:], warm_in[:], ACT.Silu)
 
         offs_t = load_list(offs, "offs_t")
-        load_tab(0)
-        load_w1(0, 0, PAIR_COLS)
-        for a in range(1, K_PASSES):
+        for a in range(K_PASSES):
             load_tab(a)
             load_w1(a, 0, PAIR_COLS)
+            if a == 1:
+                load_bias_of_tile(0, "bias0", 1)
+                load_bias_of_tile(1, "bias1", 1)
         load_w1(0, PAIR_COLS, PAIR_COLS)
-        load_bias_early(0)
         pos1_t = load_list(pos1, "pos1_t")
         load_w1(1, PAIR_COLS, PAIR_COLS)
         pos2_t = load_list(pos2, "pos2_t")
@@ -145,8 +139,8 @@ def tile_list_redline_pair_features_kernel(
         load_w1(0, PASS, PASS)
         load_bias_of_tile(2, "bias2", 1)
         load_w1(1, PASS, PASS, slot=AT_RAW1)
+        load_bias_of_tile(3, "bias3", 1)
         load_w1(2, PASS, PASS, slot=AT_RAW2)
-        load_bias_of_tile(3, AT_BIAS3, 2 * ALIGN // 4)
         b1_late = b1[PASS : 2 * PASS].rearrange("(p t) -> p t", t=PACK)
         bias_late = held([P, PACK], F32, "bias_late")
         nc.sync.dma_start(bias_late[:], b1_late)
@@ -156,96 +150,91 @@ def tile_list_redline_pair_features_kernel(
 
         v_words, w1_codes, w1_planes, h_acc, h = {}, {}, {}, {}, {}
 
-        def gather_words(a, first, end, slot):
-            words = held([P, end - first], U32, slot)
-            entries = offs_t[:, first // LIST_ROWS : end // LIST_ROWS]
-            nc.vector.tensor_copy(words[:], tab[a][:].bitcast(U32).indirect(entries))
-            v_words.setdefault(a, []).append((first, end, words))
+        def gather_words(a, slot):
+            v_words[a] = held([P, S], U32, slot)
+            nc.vector.tensor_copy(v_words[a][:], tab[a][:].bitcast(U32).indirect(offs_t[:]))
 
-        def parts_of_tile(b, t):
-            if (b, t) == (0, 0):
-                return [(0, BANK, 0), (BANK, LAST_CUT, 1), (LAST_CUT, S, 2 * PACK - 1)]
-            return [(0, BANK, 2 * t), (BANK, S, 2 * t + 1)]
+        def round_on_gpsimd_into(out_view, in_view):
+            nc.gpsimd.tensor_scalar(out_view, in_view, 1.0, 0.0, ALU.mult, ALU.add)
 
-        def runs_of_part(a, part_first, part_end):
-            for_bank = []
-            for first, end, words in v_words[a]:
-                lo, hi = max(first, part_first), min(end, part_end)
-                if lo < hi:
-                    for_bank.append((lo, hi, words[:, lo - first : hi - first]))
-            return for_bank
+        def grouped_tile(slot):
+            return held([P, PAIR_COLS * PACK], BF16, slot)
 
-        def codes_slot(a, b, d):
-            return "w1_codes_%d_%d_%d" % (a, b, d)
-
-        def planes_slot(a, b, d):
-            return "w1_planes_%d_%d_%d" % (a, b, d)
-
-        def quantise_w1(a, b, d, slot=None, copy=nc.scalar.copy, room=1):
-            if slot is not None:
-                grouped = held([P, room * PAIR_COLS * PACK], BF16, slot)[:, 0 : PAIR_COLS * PACK]
+        def round_first_pair(a, grouped, u=None):
+            src = w1_raw[a, 0][:].rearrange("p j (w u side) -> p u w j side", u=2, side=2)
+            if u is None:
+                nc.scalar.copy(grouped[:].rearrange("p (u side w j) -> p u w j side", u=2, side=2, j=PACK), src)
             else:
-                grouped = stage.tile([P, PAIR_COLS * PACK], BF16, name="grouped", align_bytes=ALIGN, bufs=4)[:]
-            if b == 0:
-                copy(
-                    grouped.rearrange("p (u side w j) -> p u w j side", u=2, side=2, j=PACK),
-                    w1_raw[a, d * PAIR_COLS][:].rearrange("p j (w u side) -> p u w j side", u=2, side=2),
-                )
-            else:
-                copy(
-                    grouped.rearrange("p (t w j) -> p w j t", t=2, j=PACK),
-                    w1_raw[a, PASS][:].rearrange("p j (w t) -> p w j t", t=PACK)[:, :, :, 2 * d : 2 * d + 2],
-                )
-            w1_codes[a, b, d] = held([P, PAIR_COLS], U32, codes_slot(a, b, d))
-            w1_planes[a, b, d] = held([P, PAIR_COLS], U8, planes_slot(a, b, d))
-            nc.vector.quantize_mx(out=w1_codes[a, b, d][:].bitcast(FP8X4), scales=w1_planes[a, b, d][:], in_=grouped)
+                nc.scalar.copy(grouped[:].rearrange("p (side w j) -> p w j side", side=2, j=PACK), src[:, u, :, :, :])
 
-        def quantise_first_tiles():
-            w1_codes[LAST, 0, 0] = held([P, PAIR_COLS], U32, codes_slot(LAST, 0, 0))
-            w1_planes[LAST, 0, 0] = held([P, PAIR_COLS], U8, planes_slot(LAST, 0, 0))
-            for u in range(2):
-                grouped = held([P, P * PACK], BF16, "grouped_tile%d" % u)
+        def round_second_pair(a, grouped, u=None, on_gpsimd=False):
+            raw = w1_raw[a, PAIR_COLS][:]
+            if u is None:
                 nc.scalar.copy(
-                    grouped[:].rearrange("p (side w j) -> p w j side", side=2, j=PACK),
-                    w1_raw[LAST, 0][:].rearrange("p j (w u side) -> p u w j side", u=2, side=2)[:, u, :, :, :],
+                    grouped[:].rearrange("p (u w side j) -> p u w j side", u=2, side=2, j=PACK),
+                    raw.rearrange("p j (w u side) -> p u w j side", u=2, side=2),
                 )
-                if u == 1:
-                    gather_words(LAST, LAST_CUT, S, raw_slot(LAST, 0))
-                cols = slice(u * P, (u + 1) * P)
-                nc.vector.quantize_mx(
-                    out=w1_codes[LAST, 0, 0][:, cols].bitcast(FP8X4), scales=w1_planes[LAST, 0, 0][:, cols], in_=grouped[:]
+            elif on_gpsimd:
+                round_on_gpsimd_into(
+                    grouped[:].rearrange("p (w side j) -> p w side j", side=2, j=PACK),
+                    raw.rearrange("p j (w u side) -> p u w side j", u=2, side=2)[:, u, :, :, :],
+                )
+            else:
+                nc.scalar.copy(
+                    grouped[:].rearrange("p (w side j) -> p w j side", side=2, j=PACK),
+                    raw.rearrange("p j (w u side) -> p u w j side", u=2, side=2)[:, u, :, :, :],
                 )
 
-        def h_pass(a, b, d):
-            for t in (2 * d, 2 * d + 1):
-                cols = slice((t % 2) * P, (t % 2 + 1) * P)
-                for first, end, index in parts_of_tile(b, t):
+        def round_late_pair(a, d, grouped, copy=nc.scalar.copy):
+            copy(
+                grouped[:].rearrange("p (t w j) -> p w j t", t=2, j=PACK),
+                w1_raw[a, PASS][:].rearrange("p j (w t) -> p w j t", t=PACK)[:, :, :, 2 * d : 2 * d + 2],
+            )
+
+        def quantise_w1(a, b, tiles, grouped, codes_slot=None):
+            width = P * len(tiles)
+            tag = "%d_%d_%d" % (a, b, tiles[0])
+            codes = held([P, width], U32, "w1_codes" + tag if codes_slot is None else codes_slot)
+            planes = held([P, width], U8, "w1_planes" + tag)
+            nc.vector.quantize_mx(out=codes[:].bitcast(FP8X4), scales=planes[:], in_=grouped[:, :])
+            for n, t in enumerate(tiles):
+                w1_codes[a, b, t] = codes[:, n * P : (n + 1) * P]
+                w1_planes[a, b, t] = planes[:, n * P : (n + 1) * P]
+
+        def h_pass(a, b, tiles):
+            for t in tiles:
+                for half in range(S // BANK):
                     if a == 0:
-                        h_acc[b, t, first] = bank(index)
-                    for lo, hi, words in runs_of_part(a, first, end):
-                        nc.tensor.matmul_mx(
-                            out=h_acc[b, t, first][:, lo - first : hi - first],
-                            lhsT=w1_codes[a, b, d][:, cols].bitcast(FP8X4),
-                            lhsT_scale=w1_planes[a, b, d][:, cols],
-                            rhs=words.bitcast(FP8X4),
-                            rhs_scale=v_planes[PLANE_ROWS * a : P, lo:hi],
-                            start=(a == 0),
-                            stop=(a == LAST and hi == end),
-                        )
+                        h_acc[b, t, half] = bank(2 * t + half)
+                    cols = slice(half * BANK, (half + 1) * BANK)
+                    nc.tensor.matmul_mx(
+                        out=h_acc[b, t, half][:],
+                        lhsT=w1_codes[a, b, t].bitcast(FP8X4),
+                        lhsT_scale=w1_planes[a, b, t],
+                        rhs=v_words[a][:, cols].bitcast(FP8X4),
+                        rhs_scale=v_planes[PLANE_ROWS * a : P, cols],
+                        start=(a == 0),
+                        stop=(a == LAST),
+                    )
 
-        def h_passes(b, d):
-            for a in range(K_PASSES):
-                h_pass(a, b, d)
+        def last_pass_by_tiles(b, tiles, grouped):
+            for n, t in enumerate(tiles):
+                quantise_w1(LAST, b, (t,), grouped[:, n * PASS : (n + 1) * PASS])
+                h_pass(LAST, b, (t,))
 
-        def relu(b, t, slot=None):
-            h[b, t] = held([P, S], F32, "h%d_%d" % (b, t) if slot is None else slot)
-            for first, end, index in parts_of_tile(b, t):
-                acc_part = h_acc[b, t, first][:, 0 : end - first]
-                nc.scalar.activation(h[b, t][:, first:end], acc_part, ACT.Relu, bias=bias_col[b, t])
+        def relu(b, t, slot=None, shared=False, banks=(0, 1)):
+            if banks[0] == 0:
+                h[b, t] = held([P, S], F32, "h%d_%d" % (b, t) if slot is None else slot)
+            for half in banks:
+                dst = h[b, t][:, half * BANK : (half + 1) * BANK]
+                if shared and half == 0:
+                    nc.vector.tensor_scalar(dst, h_acc[b, t, half][:], bias_col[b, t], 0.0, ALU.add, ALU.max)
+                else:
+                    nc.scalar.activation(dst, h_acc[b, t, half][:], ACT.Relu, bias=bias_col[b, t])
 
         z_early_slot = raw_slot(1, PAIR_COLS)
         z_early = held([P, PACK, M], F32, z_early_slot)
-        z_late_slots = (AT_RAW1, "tab2")
+        z_late_slots = (AT_RAW2, AT_RAW2 + H_BYTES)
         z_late_flat = [held([P, PACK * MH], F32, slot) for slot in z_late_slots]
         z_late = [flat[:].rearrange("p (j m) -> p j m", j=PACK) for flat in z_late_flat]
         halves = [slice(e * MH, (e + 1) * MH) for e in range(2)]
@@ -271,16 +260,11 @@ def tile_list_redline_pair_features_kernel(
 
         def move_early(t, z_tile):
             d, u = divmod(t, 2)
-            for side in range(1 - d, 2):
-                nc.sync.dma_start(
-                    z_early[SIDE * d : SIDE * (d + 1), 2 * u + side, :], z_tile[SIDE * side : SIDE * (side + 1), :]
-                )
-
-        def early_differences(t, z_tile):
-            old = held([P, M], F32, "old%d" % t)
-            nc.vector.tensor_copy(old[:], h[0, t][:].indirect(pos1_t[:]))
-            nc.vector.tensor_tensor(z_tile, h[0, t][:].indirect(pos2_t[:]), old[:], ALU.subtract)
-            move_early(t, z_tile)
+            if d == 0:
+                nc.sync.dma_start(z_early[0:SIDE, 2 * u + 1, :], z_tile[SIDE:P, :])
+            else:
+                for side in range(2):
+                    nc.sync.dma_start(z_early[SIDE:P, 2 * u + side, :], z_tile[side:P:2, :])
 
         def late_differences(t):
             differences_by_halves(1, t, [z_late[e][:, t, :] for e in range(2)])
@@ -299,9 +283,10 @@ def tile_list_redline_pair_features_kernel(
         for b in range(R_PASSES):
             z_codes[b] = held([P, M], U32, "z_codes%d" % b)
             z_planes[b] = held([P, M], U8, "z_planes%d" % b)
-        for b in range(R_PASSES):
-            wu_codes[b] = held([P, N], U32, old_slot(1, 1, 0) if b == 0 else z_late_slots[0])
-            wu_planes[b] = held([P, N], U8, "wu_planes%d" % b)
+        wu_slots = {(0, 0): old_slot(1, 1, 0), (0, 1): old_slot(1, 1, 1), (1, 0): "old_last2", (1, 1): z_late_slots[0]}
+        for (b, c), slot in wu_slots.items():
+            wu_codes[b, c] = held([P, NH], U32, slot)
+            wu_planes[b, c] = held([P, NH], U8, "wu_planes%d_%d" % (b, c))
 
         def quantise_z(b, changes, grouped):
             nc.vector.quantize_mx(out=z_codes[b][:, changes].bitcast(FP8X4), scales=z_planes[b][:, changes], in_=grouped)
@@ -315,41 +300,97 @@ def tile_list_redline_pair_features_kernel(
         def round_on_scalar(src, slot):
             return round_and_group(src, slot, nc.scalar.copy)
 
-        def quantise_wu(b, cols, slot, rounding):
-            grouped = rounding(wu_raw[b][:, :, cols], slot)
-            nc.vector.quantize_mx(out=wu_codes[b][:, cols].bitcast(FP8X4), scales=wu_planes[b][:, cols], in_=grouped)
+        def quantise_grouped_wu(b, cols, grouped):
+            c, first_col = divmod(cols.start, NH)
+            within = slice(first_col, first_col + cols.stop - cols.start)
+            nc.vector.quantize_mx(
+                out=wu_codes[b, c][:, within].bitcast(FP8X4), scales=wu_planes[b, c][:, within], in_=grouped
+            )
 
+        def quantise_wu(b, cols, slot, rounding):
+            quantise_grouped_wu(b, cols, rounding(wu_raw[b][:, :, cols], slot))
+
+        first, second, third, fourth = (0, 1), (2, 3), (0, 1), (2, 3)
         for a in range(K_PASSES):
-            gather_words(a, 0, LAST_CUT if a == LAST else S, "tab_planes" if a == 1 else "v%d" % a)
+            gather_words(a, "tab_planes" if a == 1 else "v%d" % a)
             if a == 0:
                 v_planes = held([P, S], U8, "v_planes")
                 nc.vector.tensor_copy(v_planes[:], tab_planes[:].indirect(offs_t[:]))
             if a < LAST:
-                quantise_w1(a, 0, 0)
-            else:
-                quantise_first_tiles()
-            h_pass(a, 0, 0)
+                grouped = grouped_tile("grouped_first%d" % a)
+                round_first_pair(a, grouped)
+                quantise_w1(a, 0, first, grouped)
+                h_pass(a, 0, first)
+        for u in range(2):
+            grouped = held([P, PASS], BF16, "grouped_tile%d" % u)
+            round_first_pair(LAST, grouped, u)
+            quantise_w1(LAST, 0, (u,), grouped)
+            h_pass(LAST, 0, (u,))
 
-        quantise_w1(0, 0, 1)
-        relu(0, 0)
-        quantise_w1(1, 0, 1, slot="grouped_second")
-        early_differences(0, z_early[:, 0, :])
-        quantise_w1(2, 0, 1, slot=planes_slot(LAST, 0, 0))
-        h_passes(0, 1)
-        relu(0, 1, slot=raw_slot(LAST, PAIR_COLS))
-        differences_by_halves(0, 1, [z_early[:, 2, changes] for changes in halves])
+        def second_tile_weights(a, u, slot):
+            grouped = held([P, PASS], BF16, slot)
+            round_second_pair(a, grouped, u, on_gpsimd=(u == 1))
+            return grouped
+
+        def second_tile_pass(a, u, grouped):
+            quantise_w1(a, 0, (2 + u,), grouped)
+            h_pass(a, 0, (2 + u,))
+
+        grouped = grouped_tile("grouped_second0")
+        round_second_pair(0, grouped)
+        relu(0, 0, shared=True)
+        quantise_w1(0, 0, second, grouped)
+        h_pass(0, 0, second)
+        pass1 = [second_tile_weights(1, 0, "w1_planes%d_0_0" % LAST), second_tile_weights(1, 1, "grouped_second0")]
+        old = held([P, M], F32, raw_slot(0, PAIR_COLS))
+        nc.vector.tensor_copy(old[:], h[0, 0][:].indirect(pos1_t[:]))
+        for u in range(2):
+            second_tile_pass(1, u, pass1[u])
+        nc.vector.tensor_tensor(z_early[:, 0, :], h[0, 0][:].indirect(pos2_t[:]), old[:], ALU.subtract)
+        move_early(0, z_early[:, 0, :])
+        relu(0, 1, banks=(0,))
+        grouped = grouped_tile("w1_planes%d_0_1" % LAST)
+        round_second_pair(LAST, grouped)
+        relu(0, 1, banks=(1,))
+        last_pass_by_tiles(0, second, grouped)
+        old = held([P, M], F32, raw_slot(LAST, PAIR_COLS))
+        for e in range(2):
+            pick_old(0, 1, e, old[:, halves[e]])
+        for e in range(2):
+            pick_new(0, 1, e, old[:, halves[e]], z_early[:, 2, halves[e]])
         move_early(1, z_early[:, 2, :])
-        quantise_w1(0, 1, 0)
-        relu(0, 2)
-        quantise_w1(1, 1, 0, slot=AT_THIRD_PASS1)
-        early_differences(2, held([P, M], F32, AT_THIRD_PASS1)[:])
-        quantise_w1(2, 1, 0)
-        h_passes(1, 0)
-        relu(0, 3, slot=AT_H3)
-        quantise_w1(0, 1, 1, slot=AT_FOURTH, room=2)
-        early_differences(3, held([P, M], F32, raw_slot(0, PASS))[:])
 
-        load_wu(1, "old%d" % (PACK - 1))
+        def late_weights(a, slot):
+            grouped = grouped_tile(slot)
+            round_late_pair(a, 0, grouped)
+            quantise_w1(a, 1, third, grouped)
+            h_pass(a, 1, third)
+
+        late_weights(0, "grouped_first1")
+        relu(0, 2)
+        z_tile = held([P, M], F32, "z_tile2")
+        differences_by_halves(0, 2, [z_tile[:, changes] for changes in halves])
+        move_early(2, z_tile[:])
+        late_weights(1, "w1_planes%d_0_2" % LAST)
+        relu(0, 3, slot=AT_H3)
+        old = held([P, M], F32, "old3")
+        nc.vector.tensor_copy(old[:], h[0, 3][:].indirect(pos1_t[:]))
+        grouped = held([P, PAIR_COLS * PACK], BF16, AT_THIRD2)
+        round_late_pair(LAST, 0, grouped)
+        last_pass_by_tiles(1, third, grouped)
+        g_fourth = [grouped_tile(slot) for slot in (AT_FOURTH0, "bias3", "w1_planes%d_1_0" % LAST)]
+        round_late_pair(0, 1, g_fourth[0], nc.vector.tensor_copy)
+        z_tile = held([P, M], F32, AT_Z3)
+        nc.vector.tensor_tensor(z_tile[:], h[0, 3][:].indirect(pos2_t[:]), old[:], ALU.subtract)
+        move_early(3, z_tile[:])
+        round_late_pair(1, 1, g_fourth[1])
+        for a in range(LAST):
+            quantise_w1(a, 1, fourth, g_fourth[a])
+            h_pass(a, 1, fourth)
+
+        wu_rows = wu[PASS : 2 * PASS, :].rearrange("(p j) c -> p j c", j=PACK)
+        wu_head = held([P, PACK, NH], F32, "old2_1")
+        nc.sync.dma_start(wu_head[:], wu_rows[:, :, 0:NH])
         wg_t = held([P, R_PASSES, 2 * N], U8, AT_H3)
         nc.sync.dma_start(wg_t[:].bitcast(I32), wg_words.rearrange("b p c -> p b c").bitcast(I32))
         for quad in range(P // QUADRANT):
@@ -357,33 +398,23 @@ def tile_list_redline_pair_features_kernel(
         pos3_t = load_list(pos3, "pos3_t")
         pos4_t = load_list(pos4, "pos4_t")
 
-        relu(1, 0, slot=AT_H4)
-        quantise_w1(1, 1, 1, slot=AT_FOURTH)
+        relu(1, 0)
         old = held([P, M], F32, "old_late0")
         nc.vector.tensor_copy(old[:], h[1, 0][:].indirect(pos1_t[:]))
+        round_late_pair(LAST, 1, g_fourth[LAST])
+        last_pass_by_tiles(1, fourth, g_fourth[LAST])
+        wu_tail = []
+        for e in range(2):
+            parked = z_late_flat[e][:, 2 * MH : PACK * MH].rearrange("p (j c) -> p j c", j=PACK)
+            nc.sync.dma_start(parked, wu_rows[:, :, NH + e * P : NH + (e + 1) * P])
+            wu_tail.append(parked)
         for e in range(2):
             pick_new(1, 0, e, old[:, halves[e]], z_late[e][:, 0, :])
-        quantise_w1(2, 1, 1, slot=AT_FOURTH + GROUPED_BYTES)
-        h_passes(1, 1)
-        relu(1, 1, slot=AT_RAW1 + H_BYTES)
+        relu(1, 1)
         late_differences(1)
-        quantise_wu(0, slice(0, P), AT_H3 + GROUPED_BYTES, round_on_gpsimd)
-        quantise_wu(0, slice(P, NH), AT_FOURTH + GROUPED_BYTES, round_on_gpsimd)
-        quantise_wu(0, slice(NH, N), AT_RAW2, round_on_scalar)
-
-        last_pair = (PACK - 2, PACK - 1)
-        old_last = {}
-        for t in last_pair:
-            relu(1, t)
-            old_last[t] = held([P, M], F32, "old_last%d" % t)
-            nc.vector.tensor_copy(old_last[t][:], h[1, t][:].indirect(pos1_t[:]))
-
-        def early_half_then_last_differences(e):
-            grouped = z_late_flat[e][:, last_pair[0] * MH : PACK * MH].bitcast(BF16)
-            quantise_z(0, halves[e], round_into(grouped, z_early[:, :, halves[e]], nc.scalar.copy))
-            second_pass(0, e, opens=True)
-            for t in last_pair:
-                pick_new(1, t, e, old_last[t][:, halves[e]], z_late[e][:, t, :])
+        quantise_wu(0, slice(0, P), "bias3", round_on_gpsimd)
+        quantise_wu(0, slice(P, NH), "old_late0", round_on_gpsimd)
+        quantise_wu(0, slice(NH, N), "w1_codes%d_1_1" % LAST, round_on_scalar)
 
         acc = {}
         gate_cols, lin_cols = slice(0, MH), slice(MH, 2 * MH)
@@ -392,36 +423,45 @@ def tile_list_redline_pair_features_kernel(
             for i in range(N_TILES):
                 if opens:
                     acc[e, i] = bank(N_TILES * e + i)
-                for c0 in range(0, MH, P):
-                    changes = slice(e * MH + c0, e * MH + c0 + P)
-                    nc.tensor.matmul_mx(
-                        out=acc[e, i][:, c0 : c0 + P],
-                        lhsT=wg_t[:, b, 2 * i * P : 2 * (i + 1) * P].bitcast(FP4X4),
-                        lhsT_scale=wg_planes[:, b * N + i * P : b * N + (i + 1) * P],
-                        rhs=z_codes[b][:, changes].bitcast(FP8X4),
-                        rhs_scale=z_planes[b][:, changes],
-                        start=(opens and c0 == 0),
-                        stop=False,
-                    )
-                cols = slice(i * P, (i + 1) * P)
+                nc.tensor.matmul_mx(
+                    out=acc[e, i][:, gate_cols],
+                    lhsT=wg_t[:, b, 2 * i * P : 2 * (i + 1) * P].bitcast(FP4X4),
+                    lhsT_scale=wg_planes[:, b * N + i * P : b * N + (i + 1) * P],
+                    rhs=z_codes[b][:, halves[e]].bitcast(FP8X4),
+                    rhs_scale=z_planes[b][:, halves[e]],
+                    start=opens,
+                    stop=False,
+                )
+                c, within = divmod(i, 2)
+                cols = slice(within * P, (within + 1) * P)
                 nc.tensor.matmul_mx(
                     out=acc[e, i][:, lin_cols],
-                    lhsT=wu_codes[b][:, cols].bitcast(FP8X4),
-                    lhsT_scale=wu_planes[b][:, cols],
+                    lhsT=wu_codes[b, c][:, cols].bitcast(FP8X4),
+                    lhsT_scale=wu_planes[b, c][:, cols],
                     rhs=z_codes[b][:, halves[e]].bitcast(FP8X4),
                     rhs_scale=z_planes[b][:, halves[e]],
                     start=False,
                     stop=not opens,
                 )
 
+        last_pair = (PACK - 2, PACK - 1)
+        old_last = {}
+        for e, t in enumerate(last_pair):
+            relu(1, t)
+            old_last[t] = held([P, M], F32, "old_last%d" % t)
+            nc.vector.tensor_copy(old_last[t][:], h[1, t][:].indirect(pos1_t[:]))
+            quantise_z(0, halves[e], round_on_scalar(z_early[:, :, halves[e]], "w1_planes%d_1_%d" % (LAST, t)))
+            second_pass(0, e, opens=True)
+        wu_last = held([P, NH * PACK], BF16, "w1_codes%d_1_%d" % (LAST, last_pair[1]))
         for e in range(2):
-            early_half_then_last_differences(e)
-        wu_first = round_on_gpsimd(wu_raw[1][:, :, 0:NH], AT_RAW2)
-        wu_last = round_on_scalar(wu_raw[1][:, :, NH:N], "v_planes")
+            round_into(wu_last[:, e * PASS : (e + 1) * PASS], wu_tail[e], nc.scalar.copy)
+            for t in last_pair:
+                pick_new(1, t, e, old_last[t][:, halves[e]], z_late[e][:, t, :])
+        wu_first = round_on_scalar(wu_head[:], "w1_codes%d_1_%d" % (LAST, last_pair[0]))
+        quantise_grouped_wu(1, slice(0, NH), wu_first)
         quantise_z(1, halves[0], round_on_scalar(z_late[0], "z_first_grouped"))
         z_last_grouped = round_on_scalar(z_late[1], "z_last_grouped")
-        for cols, grouped in ((slice(0, NH), wu_first), (slice(NH, N), wu_last)):
-            nc.vector.quantize_mx(out=wu_codes[1][:, cols].bitcast(FP8X4), scales=wu_planes[1][:, cols], in_=grouped)
+        quantise_grouped_wu(1, slice(NH, N), wu_last[:])
         second_pass(1, 0, opens=False)
         quantise_z(1, halves[1], z_last_grouped)
         second_pass(1, 1, opens=False)
@@ -437,7 +477,7 @@ def tile_list_redline_pair_features_kernel(
             nc.vector.tensor_tensor(y[i][:, halves[e]], acc[e, i][:, lin_cols], silu[e, i][:], ALU.mult)
 
         def make_y_on_gpsimd(e, i):
-            lin = held([P, MH], F32, "lin%d_%d" % (e, i))
+            lin = held([P, MH], F32, AT_LAST_LIN if i == N_TILES - 1 else "lin%d_%d" % (e, i))
             nc.scalar.copy(lin[:], acc[e, i][:, lin_cols])
             nc.gpsimd.tensor_tensor(y[i][:, halves[e]], lin[:], silu[e, i][:], ALU.mult)
 
@@ -462,6 +502,6 @@ def tile_list_redline_pair_features_kernel(
         for i in range(N_TILES):
             pick_first(i)
         last = N_TILES - 1
-        result_slots = ("silu1_%d" % last, "lin1_%d" % last, "result2", "result3")
+        result_slots = ("silu1_%d" % last, AT_LAST_LIN - M2 * 2, AT_LAST_LIN + M2 * 2, "result3")
         for i in range(N_TILES):
             add_second_and_store(i, result_slots[i])

@@ -42,6 +42,12 @@ AT_Z3 = AT_H3 + H_BYTES
 AT_THIRD2 = AT_Z3 + GROUPED_BYTES // 2
 AT_FOURTH0 = AT_THIRD2 + GROUPED_BYTES // 2
 AT_LAST_LIN = AT_FOURTH0 + 2 * GROUPED_BYTES
+AT_EARLY0 = AT_LAST_LIN + GROUPED_BYTES
+AT_LAST_PLANES = AT_EARLY0 + GROUPED_BYTES - ALIGN
+AT_EARLY1 = AT_LAST_PLANES + ALIGN
+AT_WU_LAST = AT_EARLY1 + GROUPED_BYTES
+AT_LAST_CODES = AT_WU_LAST + GROUPED_BYTES - PAIR_COLS
+AT_WU_FIRST = AT_LAST_CODES + PAIR_COLS
 
 
 def tile_list_redline_pair_features_kernel(
@@ -55,9 +61,12 @@ def tile_list_redline_pair_features_kernel(
         placed = ctx.enter_context(tc.tile_pool(name="placed", bufs=1))
         psum = ctx.enter_context(tc.psum_pool(name="psum", bufs=1))
 
+        placed_tiles = []
+
         def held(shape, dtype, slot):
             if isinstance(slot, int):
-                return placed.tile(shape, dtype, name="placed%d_%d_%d" % (slot, shape[1], len(shape)), align_bytes=ALIGN, offset=slot)
+                placed_tiles.append(slot)
+                return placed.tile(shape, dtype, name="placed%d" % len(placed_tiles), align_bytes=ALIGN, offset=slot)
             return keep.tile(shape, dtype, name=slot, align_bytes=ALIGN)
 
         def bank(index):
@@ -65,8 +74,6 @@ def tile_list_redline_pair_features_kernel(
 
         tab_planes = held([P, T], U8, "tab_planes")
         nc.vector.memset(tab_planes[:].bitcast(I32), 0)
-        wg_planes = held([P, R_PASSES * N], U8, "wg_planes")
-        nc.vector.memset(wg_planes[:].bitcast(I32), 0)
 
         tab, w1_raw, wu_raw, bias_col = {}, {}, {}, {}
 
@@ -191,11 +198,11 @@ def tile_list_redline_pair_features_kernel(
                 w1_raw[a, PASS][:].rearrange("p j (w t) -> p w j t", t=PACK)[:, :, :, 2 * d : 2 * d + 2],
             )
 
-        def quantise_w1(a, b, tiles, grouped, codes_slot=None):
+        def quantise_w1(a, b, tiles, grouped):
             width = P * len(tiles)
             tag = "%d_%d_%d" % (a, b, tiles[0])
-            codes = held([P, width], U32, "w1_codes" + tag if codes_slot is None else codes_slot)
-            planes = held([P, width], U8, "w1_planes" + tag)
+            codes = held([P, width], U32, AT_LAST_CODES if (a, b, tiles[0]) == (LAST, 1, 3) else "w1_codes" + tag)
+            planes = held([P, width], U8, AT_LAST_PLANES if (a, b, tiles[0]) == (LAST, 1, 3) else "w1_planes" + tag)
             nc.vector.quantize_mx(out=codes[:].bitcast(FP8X4), scales=planes[:], in_=grouped[:, :])
             for n, t in enumerate(tiles):
                 w1_codes[a, b, t] = codes[:, n * P : (n + 1) * P]
@@ -373,6 +380,8 @@ def tile_list_redline_pair_features_kernel(
         move_early(2, z_tile[:])
         late_weights(1, "w1_planes%d_0_2" % LAST)
         relu(0, 3, slot=AT_H3)
+        wg_planes = held([P, R_PASSES * N], U8, "w1_planes%d_0_2" % LAST)
+        nc.gpsimd.memset(wg_planes[:].bitcast(I32), 0)
         old = held([P, M], F32, "old3")
         nc.vector.tensor_copy(old[:], h[0, 3][:].indirect(pos1_t[:]))
         grouped = held([P, PAIR_COLS * PACK], BF16, AT_THIRD2)
@@ -389,10 +398,10 @@ def tile_list_redline_pair_features_kernel(
             h_pass(a, 1, fourth)
 
         wu_rows = wu[PASS : 2 * PASS, :].rearrange("(p j) c -> p j c", j=PACK)
-        wu_head = held([P, PACK, NH], F32, "old2_1")
-        nc.sync.dma_start(wu_head[:], wu_rows[:, :, 0:NH])
         wg_t = held([P, R_PASSES, 2 * N], U8, AT_H3)
         nc.sync.dma_start(wg_t[:].bitcast(I32), wg_words.rearrange("b p c -> p b c").bitcast(I32))
+        wu_head = held([P, PACK, NH], F32, "old3")
+        nc.sync.dma_start(wu_head[:], wu_rows[:, :, 0:NH])
         for quad in range(P // QUADRANT):
             load_wg_planes(quad)
         pos3_t = load_list(pos3, "pos3_t")
@@ -446,18 +455,19 @@ def tile_list_redline_pair_features_kernel(
 
         last_pair = (PACK - 2, PACK - 1)
         old_last = {}
-        for e, t in enumerate(last_pair):
+        for t in last_pair:
             relu(1, t)
             old_last[t] = held([P, M], F32, "old_last%d" % t)
             nc.vector.tensor_copy(old_last[t][:], h[1, t][:].indirect(pos1_t[:]))
-            quantise_z(0, halves[e], round_on_scalar(z_early[:, :, halves[e]], "w1_planes%d_1_%d" % (LAST, t)))
+        for e, t in enumerate(last_pair):
+            quantise_z(0, halves[e], round_on_scalar(z_early[:, :, halves[e]], (AT_EARLY0, AT_EARLY1)[e]))
             second_pass(0, e, opens=True)
-        wu_last = held([P, NH * PACK], BF16, "w1_codes%d_1_%d" % (LAST, last_pair[1]))
+        wu_last = held([P, NH * PACK], BF16, AT_WU_LAST)
         for e in range(2):
             round_into(wu_last[:, e * PASS : (e + 1) * PASS], wu_tail[e], nc.scalar.copy)
             for t in last_pair:
                 pick_new(1, t, e, old_last[t][:, halves[e]], z_late[e][:, t, :])
-        wu_first = round_on_scalar(wu_head[:], "w1_codes%d_1_%d" % (LAST, last_pair[0]))
+        wu_first = round_on_scalar(wu_head[:], AT_WU_FIRST)
         quantise_grouped_wu(1, slice(0, NH), wu_first)
         quantise_z(1, halves[0], round_on_scalar(z_late[0], "z_first_grouped"))
         z_last_grouped = round_on_scalar(z_late[1], "z_last_grouped")

@@ -35,19 +35,15 @@ NH = N // 2
 GROUPED_BYTES = PAIR_COLS * PACK * 2
 H_BYTES = S * 4
 RAW_BYTES = PACK * PASS * 4
-AT_RAW1 = 0
-AT_RAW2 = AT_RAW1 + RAW_BYTES
+AT_RAW1 = GROUPED_BYTES
+AT_RAW2 = AT_RAW1 + RAW_BYTES + H_BYTES
 AT_H3 = AT_RAW2 + RAW_BYTES
-AT_Z3 = AT_H3 + H_BYTES
-AT_THIRD2 = AT_Z3 + GROUPED_BYTES // 2
-AT_FOURTH0 = AT_THIRD2 + GROUPED_BYTES // 2
-AT_LAST_LIN = AT_FOURTH0 + 2 * GROUPED_BYTES
+AT_LAST_LIN = AT_H3 + H_BYTES + GROUPED_BYTES
 AT_EARLY0 = AT_LAST_LIN + GROUPED_BYTES
 AT_LAST_PLANES = AT_EARLY0 + GROUPED_BYTES - ALIGN
 AT_EARLY1 = AT_LAST_PLANES + ALIGN
 AT_WU_LAST = AT_EARLY1 + GROUPED_BYTES
 AT_LAST_CODES = AT_WU_LAST + GROUPED_BYTES - PAIR_COLS
-AT_WU_FIRST = AT_LAST_CODES + PAIR_COLS
 
 
 def tile_list_redline_pair_features_kernel(
@@ -74,6 +70,9 @@ def tile_list_redline_pair_features_kernel(
 
         tab_planes = held([P, T], U8, "tab_planes")
         nc.vector.memset(tab_planes[:].bitcast(I32), 0)
+
+        wg_planes = held([P, R_PASSES * N], U8, "wg_planes")
+        nc.vector.memset(wg_planes[:].bitcast(I32), 0)
 
         tab, w1_raw, wu_raw, bias_col = {}, {}, {}, {}
 
@@ -201,17 +200,17 @@ def tile_list_redline_pair_features_kernel(
         def quantise_w1(a, b, tiles, grouped):
             width = P * len(tiles)
             tag = "%d_%d_%d" % (a, b, tiles[0])
-            codes = held([P, width], U32, AT_LAST_CODES if (a, b, tiles[0]) == (LAST, 1, 3) else "w1_codes" + tag)
-            planes = held([P, width], U8, AT_LAST_PLANES if (a, b, tiles[0]) == (LAST, 1, 3) else "w1_planes" + tag)
+            codes = held([P, width], U32, AT_LAST_CODES if (a, b, tiles[0]) == (1, 1, 3) else "w1_codes" + tag)
+            planes = held([P, width], U8, AT_LAST_PLANES if (a, b, tiles[0]) == (1, 1, 3) else "w1_planes" + tag)
             nc.vector.quantize_mx(out=codes[:].bitcast(FP8X4), scales=planes[:], in_=grouped[:, :])
             for n, t in enumerate(tiles):
                 w1_codes[a, b, t] = codes[:, n * P : (n + 1) * P]
                 w1_planes[a, b, t] = planes[:, n * P : (n + 1) * P]
 
-        def h_pass(a, b, tiles):
+        def h_pass(a, b, tiles, opening=0, closing=LAST):
             for t in tiles:
                 for half in range(S // BANK):
-                    if a == 0:
+                    if a == opening:
                         h_acc[b, t, half] = bank(2 * t + half)
                     cols = slice(half * BANK, (half + 1) * BANK)
                     nc.tensor.matmul_mx(
@@ -220,14 +219,14 @@ def tile_list_redline_pair_features_kernel(
                         lhsT_scale=w1_planes[a, b, t],
                         rhs=v_words[a][:, cols].bitcast(FP8X4),
                         rhs_scale=v_planes[PLANE_ROWS * a : P, cols],
-                        start=(a == 0),
-                        stop=(a == LAST),
+                        start=(a == opening),
+                        stop=(a == closing),
                     )
 
-        def last_pass_by_tiles(b, tiles, grouped):
+        def last_pass_by_tiles(b, tiles, grouped, opening=0, closing=LAST):
             for n, t in enumerate(tiles):
-                quantise_w1(LAST, b, (t,), grouped[:, n * PASS : (n + 1) * PASS])
-                h_pass(LAST, b, (t,))
+                quantise_w1(closing, b, (t,), grouped[:, n * PASS : (n + 1) * PASS])
+                h_pass(closing, b, (t,), opening, closing)
 
         def relu(b, t, slot=None, shared=False, banks=(0, 1)):
             if banks[0] == 0:
@@ -241,7 +240,7 @@ def tile_list_redline_pair_features_kernel(
 
         z_early_slot = raw_slot(1, PAIR_COLS)
         z_early = held([P, PACK, M], F32, z_early_slot)
-        z_late_slots = (AT_RAW2, AT_RAW2 + H_BYTES)
+        z_late_slots = (AT_RAW1 + H_BYTES - ALIGN, AT_RAW1 + 2 * H_BYTES - ALIGN)
         z_late_flat = [held([P, PACK * MH], F32, slot) for slot in z_late_slots]
         z_late = [flat[:].rearrange("p (j m) -> p j m", j=PACK) for flat in z_late_flat]
         halves = [slice(e * MH, (e + 1) * MH) for e in range(2)]
@@ -373,29 +372,50 @@ def tile_list_redline_pair_features_kernel(
             quantise_w1(a, 1, third, grouped)
             h_pass(a, 1, third)
 
+
+        def round_fourth_piece(t, half, slot):
+            grouped = held([P, PAIR_COLS], BF16, slot)
+            words = slice(half * SIDE, (half + 1) * SIDE)
+            round_on_gpsimd_into(
+                grouped[:].rearrange("p (w j) -> p w j", j=PACK),
+                w1_raw[0, PASS][:].rearrange("p j (w t) -> p t w j", t=PACK)[:, t, words, :],
+            )
+            pieces[t, half] = grouped
+
+        def quantise_fourth_pieces(t, slot):
+            codes = held([P, P], U32, slot)
+            planes = held([P, P], U8, slot + GROUPED_BYTES)
+            for half in range(2):
+                cols = slice(half * SIDE, (half + 1) * SIDE)
+                nc.vector.quantize_mx(out=codes[:, cols].bitcast(FP8X4), scales=planes[:, cols], in_=pieces[t, half][:])
+            w1_codes[0, 1, t], w1_planes[0, 1, t] = codes[:], planes[:]
+            h_pass(0, 1, (t,), opening=LAST, closing=1)
+
+        pieces = {}
+        round_fourth_piece(2, 0, "w1_planes%d_0_1" % LAST)
         late_weights(0, "grouped_first1")
+        round_fourth_piece(2, 1, "grouped_first1")
         relu(0, 2)
         z_tile = held([P, M], F32, "z_tile2")
         differences_by_halves(0, 2, [z_tile[:, changes] for changes in halves])
         move_early(2, z_tile[:])
         late_weights(1, "w1_planes%d_0_2" % LAST)
         relu(0, 3, slot=AT_H3)
-        wg_planes = held([P, R_PASSES * N], U8, "w1_planes%d_0_2" % LAST)
-        nc.gpsimd.memset(wg_planes[:].bitcast(I32), 0)
+        round_fourth_piece(3, 0, "w1_planes%d_0_2" % LAST)
         old = held([P, M], F32, "old3")
         nc.vector.tensor_copy(old[:], h[0, 3][:].indirect(pos1_t[:]))
-        grouped = held([P, PAIR_COLS * PACK], BF16, AT_THIRD2)
+        grouped = grouped_tile("grouped_third2")
         round_late_pair(LAST, 0, grouped)
         last_pass_by_tiles(1, third, grouped)
-        g_fourth = [grouped_tile(slot) for slot in (AT_FOURTH0, "bias3", "w1_planes%d_1_0" % LAST)]
-        round_late_pair(0, 1, g_fourth[0], nc.vector.tensor_copy)
-        z_tile = held([P, M], F32, AT_Z3)
+        g_fourth = {1: grouped_tile("w1_planes%d_1_0" % LAST), LAST: grouped_tile("grouped_fourth2")}
+        z_tile = held([P, M], F32, "grouped_third2")
         nc.vector.tensor_tensor(z_tile[:], h[0, 3][:].indirect(pos2_t[:]), old[:], ALU.subtract)
         move_early(3, z_tile[:])
-        round_late_pair(1, 1, g_fourth[1])
-        for a in range(LAST):
-            quantise_w1(a, 1, fourth, g_fourth[a])
-            h_pass(a, 1, fourth)
+        round_late_pair(LAST, 1, g_fourth[LAST])
+        quantise_w1(LAST, 1, fourth, g_fourth[LAST])
+        h_pass(LAST, 1, fourth, opening=LAST, closing=1)
+        quantise_fourth_pieces(2, AT_RAW2)
+        round_fourth_piece(3, 1, "grouped_first1")
 
         wu_rows = wu[PASS : 2 * PASS, :].rearrange("(p j) c -> p j c", j=PACK)
         wg_t = held([P, R_PASSES, 2 * N], U8, AT_H3)
@@ -410,8 +430,9 @@ def tile_list_redline_pair_features_kernel(
         relu(1, 0)
         old = held([P, M], F32, "old_late0")
         nc.vector.tensor_copy(old[:], h[1, 0][:].indirect(pos1_t[:]))
-        round_late_pair(LAST, 1, g_fourth[LAST])
-        last_pass_by_tiles(1, fourth, g_fourth[LAST])
+        round_late_pair(1, 1, g_fourth[1])
+        quantise_fourth_pieces(3, AT_RAW1 - PAIR_COLS)
+        last_pass_by_tiles(1, fourth, g_fourth[1], opening=LAST, closing=1)
         wu_tail = []
         for e in range(2):
             parked = z_late_flat[e][:, 2 * MH : PACK * MH].rearrange("p (j c) -> p j c", j=PACK)
@@ -421,8 +442,8 @@ def tile_list_redline_pair_features_kernel(
             pick_new(1, 0, e, old[:, halves[e]], z_late[e][:, 0, :])
         relu(1, 1)
         late_differences(1)
-        quantise_wu(0, slice(0, P), "bias3", round_on_gpsimd)
-        quantise_wu(0, slice(P, NH), "old_late0", round_on_gpsimd)
+        quantise_wu(0, slice(0, P), "old_late0", round_on_gpsimd)
+        quantise_wu(0, slice(P, NH), "w1_planes%d_1_1" % LAST, round_on_scalar)
         quantise_wu(0, slice(NH, N), "w1_codes%d_1_1" % LAST, round_on_scalar)
 
         acc = {}
@@ -459,15 +480,14 @@ def tile_list_redline_pair_features_kernel(
             relu(1, t)
             old_last[t] = held([P, M], F32, "old_last%d" % t)
             nc.vector.tensor_copy(old_last[t][:], h[1, t][:].indirect(pos1_t[:]))
-        for e, t in enumerate(last_pair):
-            quantise_z(0, halves[e], round_on_scalar(z_early[:, :, halves[e]], (AT_EARLY0, AT_EARLY1)[e]))
-            second_pass(0, e, opens=True)
+        wu_first = round_on_gpsimd(wu_head[:], "w1_codes%d_1_1" % LAST)
         wu_last = held([P, NH * PACK], BF16, AT_WU_LAST)
         for e in range(2):
+            quantise_z(0, halves[e], round_on_scalar(z_early[:, :, halves[e]], (AT_EARLY0, AT_EARLY1)[e]))
+            second_pass(0, e, opens=True)
             round_into(wu_last[:, e * PASS : (e + 1) * PASS], wu_tail[e], nc.scalar.copy)
             for t in last_pair:
                 pick_new(1, t, e, old_last[t][:, halves[e]], z_late[e][:, t, :])
-        wu_first = round_on_scalar(wu_head[:], AT_WU_FIRST)
         quantise_grouped_wu(1, slice(0, NH), wu_first)
         quantise_z(1, halves[0], round_on_scalar(z_late[0], "z_first_grouped"))
         z_last_grouped = round_on_scalar(z_late[1], "z_last_grouped")

@@ -35,7 +35,7 @@ NH = N // 2
 GROUPED_BYTES = PAIR_COLS * PACK * 2
 H_BYTES = S * 4
 RAW_BYTES = PACK * PASS * 4
-AT_RAW1 = GROUPED_BYTES
+AT_RAW1 = 0
 AT_RAW2 = AT_RAW1 + RAW_BYTES + H_BYTES
 AT_H3 = AT_RAW2 + RAW_BYTES
 AT_LAST_LIN = AT_H3 + H_BYTES + GROUPED_BYTES
@@ -44,6 +44,8 @@ AT_LAST_PLANES = AT_EARLY0 + GROUPED_BYTES - ALIGN
 AT_EARLY1 = AT_LAST_PLANES + ALIGN
 AT_WU_LAST = AT_EARLY1 + GROUPED_BYTES
 AT_LAST_CODES = AT_WU_LAST + GROUPED_BYTES - PAIR_COLS
+AT_WU_FIRST = AT_LAST_CODES + PAIR_COLS
+AT_OLD5 = AT_WU_FIRST + GROUPED_BYTES
 
 
 def tile_list_redline_pair_features_kernel(
@@ -249,6 +251,8 @@ def tile_list_redline_pair_features_kernel(
             return offsets[:, e * MH // LIST_ROWS : (e + 1) * MH // LIST_ROWS]
 
         def old_slot(b, t, e):
+            if (b, t, e) == (1, 1, 0):
+                return AT_OLD5
             return ("old%d_%d" if b == 0 else "old_late%d_%d") % (t, e)
 
         def pick_old(b, t, e, old):
@@ -289,10 +293,6 @@ def tile_list_redline_pair_features_kernel(
         for b in range(R_PASSES):
             z_codes[b] = held([P, M], U32, "z_codes%d" % b)
             z_planes[b] = held([P, M], U8, "z_planes%d" % b)
-        wu_slots = {(0, 0): old_slot(1, 1, 0), (0, 1): old_slot(1, 1, 1), (1, 0): "old_last2", (1, 1): z_late_slots[0]}
-        for (b, c), slot in wu_slots.items():
-            wu_codes[b, c] = held([P, NH], U32, slot)
-            wu_planes[b, c] = held([P, NH], U8, "wu_planes%d_%d" % (b, c))
 
         def quantise_z(b, changes, grouped):
             nc.vector.quantize_mx(out=z_codes[b][:, changes].bitcast(FP8X4), scales=z_planes[b][:, changes], in_=grouped)
@@ -306,15 +306,14 @@ def tile_list_redline_pair_features_kernel(
         def round_on_scalar(src, slot):
             return round_and_group(src, slot, nc.scalar.copy)
 
-        def quantise_grouped_wu(b, cols, grouped):
-            c, first_col = divmod(cols.start, NH)
-            within = slice(first_col, first_col + cols.stop - cols.start)
-            nc.vector.quantize_mx(
-                out=wu_codes[b, c][:, within].bitcast(FP8X4), scales=wu_planes[b, c][:, within], in_=grouped
-            )
-
-        def quantise_wu(b, cols, slot, rounding):
-            quantise_grouped_wu(b, cols, rounding(wu_raw[b][:, :, cols], slot))
+        def quantise_wu(b, first_tile, grouped, codes_slot, planes_slot=None):
+            width = grouped.shape[1] // PACK
+            codes = held([P, width], U32, codes_slot)
+            planes = held([P, width], U8, planes_slot or "wu_planes%d_%d" % (b, first_tile))
+            nc.vector.quantize_mx(out=codes[:].bitcast(FP8X4), scales=planes[:], in_=grouped)
+            for n in range(width // P):
+                wu_codes[b, first_tile + n] = codes[:, n * P : (n + 1) * P]
+                wu_planes[b, first_tile + n] = planes[:, n * P : (n + 1) * P]
 
         first, second, third, fourth = (0, 1), (2, 3), (0, 1), (2, 3)
         for a in range(K_PASSES):
@@ -431,7 +430,7 @@ def tile_list_redline_pair_features_kernel(
         old = held([P, M], F32, "old_late0")
         nc.vector.tensor_copy(old[:], h[1, 0][:].indirect(pos1_t[:]))
         round_late_pair(1, 1, g_fourth[1])
-        quantise_fourth_pieces(3, AT_RAW1 - PAIR_COLS)
+        quantise_fourth_pieces(3, AT_RAW1 + PASS)
         last_pass_by_tiles(1, fourth, g_fourth[1], opening=LAST, closing=1)
         wu_tail = []
         for e in range(2):
@@ -442,9 +441,9 @@ def tile_list_redline_pair_features_kernel(
             pick_new(1, 0, e, old[:, halves[e]], z_late[e][:, 0, :])
         relu(1, 1)
         late_differences(1)
-        quantise_wu(0, slice(0, P), "old_late0", round_on_gpsimd)
-        quantise_wu(0, slice(P, NH), "w1_planes%d_1_1" % LAST, round_on_scalar)
-        quantise_wu(0, slice(NH, N), "w1_codes%d_1_1" % LAST, round_on_scalar)
+        quantise_wu(0, 0, round_on_gpsimd(wu_raw[0][:, :, 0:P], "old_late0"), old_slot(1, 1, 0))
+        quantise_wu(0, 3, round_on_scalar(wu_raw[0][:, :, 3 * P : N], "w1_codes%d_1_1" % LAST), AT_OLD5 + PASS)
+        wu_middle = round_on_gpsimd(wu_raw[0][:, :, P : 3 * P], "w1_codes%d_1_1" % LAST)
 
         acc = {}
         gate_cols, lin_cols = slice(0, MH), slice(MH, 2 * MH)
@@ -462,12 +461,10 @@ def tile_list_redline_pair_features_kernel(
                     start=opens,
                     stop=False,
                 )
-                c, within = divmod(i, 2)
-                cols = slice(within * P, (within + 1) * P)
                 nc.tensor.matmul_mx(
                     out=acc[e, i][:, lin_cols],
-                    lhsT=wu_codes[b, c][:, cols].bitcast(FP8X4),
-                    lhsT_scale=wu_planes[b, c][:, cols],
+                    lhsT=wu_codes[b, i].bitcast(FP8X4),
+                    lhsT_scale=wu_planes[b, i],
                     rhs=z_codes[b][:, halves[e]].bitcast(FP8X4),
                     rhs_scale=z_planes[b][:, halves[e]],
                     start=False,
@@ -478,20 +475,21 @@ def tile_list_redline_pair_features_kernel(
         old_last = {}
         for t in last_pair:
             relu(1, t)
-            old_last[t] = held([P, M], F32, "old_last%d" % t)
+            old_last[t] = held([P, M], F32, old_slot(1, 1, 1) if t == last_pair[0] else "old_last")
             nc.vector.tensor_copy(old_last[t][:], h[1, t][:].indirect(pos1_t[:]))
-        wu_first = round_on_gpsimd(wu_head[:], "w1_codes%d_1_1" % LAST)
+        quantise_wu(0, 1, wu_middle, "wu_codes0_1", "bias_late")
         wu_last = held([P, NH * PACK], BF16, AT_WU_LAST)
         for e in range(2):
             quantise_z(0, halves[e], round_on_scalar(z_early[:, :, halves[e]], (AT_EARLY0, AT_EARLY1)[e]))
             second_pass(0, e, opens=True)
+        for e in range(2):
             round_into(wu_last[:, e * PASS : (e + 1) * PASS], wu_tail[e], nc.scalar.copy)
             for t in last_pair:
                 pick_new(1, t, e, old_last[t][:, halves[e]], z_late[e][:, t, :])
-        quantise_grouped_wu(1, slice(0, NH), wu_first)
+        quantise_wu(1, 0, round_on_scalar(wu_head[:], AT_WU_FIRST), old_slot(1, 1, 1))
         quantise_z(1, halves[0], round_on_scalar(z_late[0], "z_first_grouped"))
         z_last_grouped = round_on_scalar(z_late[1], "z_last_grouped")
-        quantise_grouped_wu(1, slice(NH, N), wu_last[:])
+        quantise_wu(1, 2, wu_last[:], z_late_slots[0])
         second_pass(1, 0, opens=False)
         quantise_z(1, halves[1], z_last_grouped)
         second_pass(1, 1, opens=False)

@@ -32,6 +32,7 @@ PAIR_COLS = 2 * P
 MH = M // 2
 N_TILES = N // P
 NH = N // 2
+BIAS_RUN = 3
 GROUPED_BYTES = PAIR_COLS * PACK * 2
 H_BYTES = S * 4
 RAW_BYTES = PACK * PASS * 4
@@ -55,7 +56,6 @@ def tile_list_redline_pair_features_kernel(
 
     with ExitStack() as ctx:
         keep = ctx.enter_context(tc.tile_pool(name="keep", bufs=1))
-        stage = ctx.enter_context(tc.tile_pool(name="stage", bufs=3))
         placed = ctx.enter_context(tc.tile_pool(name="placed", bufs=1))
         psum = ctx.enter_context(tc.psum_pool(name="psum", bufs=1))
 
@@ -109,16 +109,18 @@ def tile_list_redline_pair_features_kernel(
 
         b1_early = b1[0:PASS].rearrange("(d w x) -> w d x", d=2, x=PACK)
 
-        def load_bias_of_tile(t, slot, width):
-            d, u = divmod(t, 2)
-            cols = held([P, width], F32, slot)
-            if d == 0:
-                for side in range(2):
-                    x = 2 * u + side
-                    nc.sync.dma_start(cols[SIDE * side : SIDE * (side + 1), 0:1], b1_early[:, d, x : x + 1])
-            else:
-                nc.sync.dma_start(cols[:, 0:1], b1_early[:, d, 2 * u : 2 * u + 2])
-            bias_col[0, t] = cols[:, 0:1]
+        def load_bias_of_first_pair():
+            runs = held([P, BIAS_RUN], F32, "bias_first")
+            for side in range(2):
+                nc.sync.dma_start(runs[SIDE * side : SIDE * (side + 1), :], b1_early[:, 0, side : side + BIAS_RUN])
+            for u in range(2):
+                bias_col[0, u] = runs[:, 2 * u : 2 * u + 1]
+
+        def load_bias_of_tile(t):
+            u = t - 2
+            col = held([P, 1], F32, "bias%d" % t)
+            nc.sync.dma_start(col[:], b1_early[:, 1, 2 * u : 2 * u + 2])
+            bias_col[0, t] = col[:]
 
         for quad in range(P // QUADRANT):
             queue = nc.sync if quad % 2 == 0 else nc.scalar
@@ -137,17 +139,16 @@ def tile_list_redline_pair_features_kernel(
             load_tab(a)
             load_w1(a, 0, PAIR_COLS)
             if a == 1:
-                load_bias_of_tile(0, "bias0", 1)
-                load_bias_of_tile(1, "bias1", 1)
+                load_bias_of_first_pair()
         load_w1(0, PAIR_COLS, PAIR_COLS)
         pos1_t = load_list(pos1, "pos1_t")
         load_w1(1, PAIR_COLS, PAIR_COLS)
         pos2_t = load_list(pos2, "pos2_t")
         load_w1(2, PAIR_COLS, PAIR_COLS)
         load_w1(0, PASS, PASS)
-        load_bias_of_tile(2, "bias2", 1)
+        load_bias_of_tile(2)
         load_w1(1, PASS, PASS, slot=AT_RAW1)
-        load_bias_of_tile(3, "bias3", 1)
+        load_bias_of_tile(3)
         load_w1(2, PASS, PASS, slot=AT_RAW2)
         b1_late = b1[PASS : 2 * PASS].rearrange("(p t) -> p t", t=PACK)
         bias_late = held([P, PACK], F32, "bias_late")
@@ -193,8 +194,8 @@ def tile_list_redline_pair_features_kernel(
                     raw.rearrange("p j (w u side) -> p u w j side", u=2, side=2)[:, u, :, :, :],
                 )
 
-        def round_late_pair(a, d, grouped, copy=nc.scalar.copy):
-            copy(
+        def round_late_pair(a, d, grouped):
+            nc.scalar.copy(
                 grouped[:].rearrange("p (t w j) -> p w j t", t=2, j=PACK),
                 w1_raw[a, PASS][:].rearrange("p j (w t) -> p w j t", t=PACK)[:, :, :, 2 * d : 2 * d + 2],
             )
@@ -202,8 +203,8 @@ def tile_list_redline_pair_features_kernel(
         def quantise_w1(a, b, tiles, grouped):
             width = P * len(tiles)
             tag = "%d_%d_%d" % (a, b, tiles[0])
-            codes = held([P, width], U32, AT_LAST_CODES if (a, b, tiles[0]) == (1, 1, 3) else "w1_codes" + tag)
-            planes = held([P, width], U8, AT_LAST_PLANES if (a, b, tiles[0]) == (1, 1, 3) else "w1_planes" + tag)
+            codes = held([P, width], U32, "w1_codes" + tag)
+            planes = held([P, width], U8, "w1_planes" + tag)
             nc.vector.quantize_mx(out=codes[:].bitcast(FP8X4), scales=planes[:], in_=grouped[:, :])
             for n, t in enumerate(tiles):
                 w1_codes[a, b, t] = codes[:, n * P : (n + 1) * P]
@@ -225,10 +226,10 @@ def tile_list_redline_pair_features_kernel(
                         stop=(a == closing),
                     )
 
-        def last_pass_by_tiles(b, tiles, grouped, opening=0, closing=LAST):
+        def last_pass_by_tiles(b, tiles, grouped):
             for n, t in enumerate(tiles):
-                quantise_w1(closing, b, (t,), grouped[:, n * PASS : (n + 1) * PASS])
-                h_pass(closing, b, (t,), opening, closing)
+                quantise_w1(LAST, b, (t,), grouped[:, n * PASS : (n + 1) * PASS])
+                h_pass(LAST, b, (t,))
 
         def relu(b, t, slot=None, shared=False, banks=(0, 1)):
             if banks[0] == 0:
@@ -251,6 +252,8 @@ def tile_list_redline_pair_features_kernel(
             return offsets[:, e * MH // LIST_ROWS : (e + 1) * MH // LIST_ROWS]
 
         def old_slot(b, t, e):
+            if (b, t, e) == (1, 0, 0):
+                return AT_LAST_CODES
             if (b, t, e) == (1, 1, 0):
                 return AT_OLD5
             return ("old%d_%d" if b == 0 else "old_late%d_%d") % (t, e)
@@ -279,15 +282,12 @@ def tile_list_redline_pair_features_kernel(
         def late_differences(t):
             differences_by_halves(1, t, [z_late[e][:, t, :] for e in range(2)])
 
-        def round_into(grouped, src, copy):
-            copy(
+        def round_into(grouped, src):
+            nc.scalar.copy(
                 grouped.rearrange("p (c x j) -> p c j x", x=2, j=PACK),
                 src.rearrange("p j (c x) -> p c j x", x=2),
             )
             return grouped
-
-        def round_and_group(src, slot, copy):
-            return round_into(held([P, src.shape[2] * PACK], BF16, slot)[:], src, copy)
 
         z_codes, z_planes, wu_codes, wu_planes = {}, {}, {}, {}
         for b in range(R_PASSES):
@@ -304,7 +304,7 @@ def tile_list_redline_pair_features_kernel(
             return grouped
 
         def round_on_scalar(src, slot):
-            return round_and_group(src, slot, nc.scalar.copy)
+            return round_into(held([P, src.shape[2] * PACK], BF16, slot)[:], src)
 
         def quantise_wu(b, first_tile, grouped, codes_slot, planes_slot=None):
             width = grouped.shape[1] // PACK
@@ -371,7 +371,6 @@ def tile_list_redline_pair_features_kernel(
             quantise_w1(a, 1, third, grouped)
             h_pass(a, 1, third)
 
-
         def round_fourth_piece(t, half, slot):
             grouped = held([P, PAIR_COLS], BF16, slot)
             words = slice(half * SIDE, (half + 1) * SIDE)
@@ -381,16 +380,17 @@ def tile_list_redline_pair_features_kernel(
             )
             pieces[t, half] = grouped
 
-        def quantise_fourth_pieces(t, slot):
-            codes = held([P, P], U32, slot)
-            planes = held([P, P], U8, slot + GROUPED_BYTES)
+        def quantise_fourth_pieces(t, codes_slot, planes_slot):
+            codes = held([P, P], U32, codes_slot)
+            planes = held([P, P], U8, planes_slot)
             for half in range(2):
                 cols = slice(half * SIDE, (half + 1) * SIDE)
                 nc.vector.quantize_mx(out=codes[:, cols].bitcast(FP8X4), scales=planes[:, cols], in_=pieces[t, half][:])
             w1_codes[0, 1, t], w1_planes[0, 1, t] = codes[:], planes[:]
-            h_pass(0, 1, (t,), opening=LAST, closing=1)
+            h_pass(0, 1, (t,), opening=LAST, closing=closing_pass[t])
 
         pieces = {}
+        closing_pass = {2: 1, 3: 0}
         round_fourth_piece(2, 0, "w1_planes%d_0_1" % LAST)
         late_weights(0, "grouped_first1")
         round_fourth_piece(2, 1, "grouped_first1")
@@ -413,7 +413,7 @@ def tile_list_redline_pair_features_kernel(
         round_late_pair(LAST, 1, g_fourth[LAST])
         quantise_w1(LAST, 1, fourth, g_fourth[LAST])
         h_pass(LAST, 1, fourth, opening=LAST, closing=1)
-        quantise_fourth_pieces(2, AT_RAW2)
+        quantise_fourth_pieces(2, AT_RAW2, "w1_planes0_1_2")
         round_fourth_piece(3, 1, "grouped_first1")
 
         wu_rows = wu[PASS : 2 * PASS, :].rearrange("(p j) c -> p j c", j=PACK)
@@ -427,21 +427,24 @@ def tile_list_redline_pair_features_kernel(
         pos4_t = load_list(pos4, "pos4_t")
 
         relu(1, 0)
-        old = held([P, M], F32, "old_late0")
-        nc.vector.tensor_copy(old[:], h[1, 0][:].indirect(pos1_t[:]))
+        old = [held([P, MH], F32, old_slot(1, 0, e)) for e in range(2)]
+        for e in range(2):
+            pick_old(1, 0, e, old[e][:])
         round_late_pair(1, 1, g_fourth[1])
-        quantise_fourth_pieces(3, AT_RAW1 + PASS)
-        last_pass_by_tiles(1, fourth, g_fourth[1], opening=LAST, closing=1)
+        quantise_w1(1, 1, fourth, g_fourth[1])
+        for t in fourth:
+            h_pass(1, 1, (t,), opening=LAST, closing=closing_pass[t])
         wu_tail = []
         for e in range(2):
             parked = z_late_flat[e][:, 2 * MH : PACK * MH].rearrange("p (j c) -> p j c", j=PACK)
             nc.sync.dma_start(parked, wu_rows[:, :, NH + e * P : NH + (e + 1) * P])
             wu_tail.append(parked)
         for e in range(2):
-            pick_new(1, 0, e, old[:, halves[e]], z_late[e][:, 0, :])
+            pick_new(1, 0, e, old[e][:], z_late[e][:, 0, :])
+        quantise_fourth_pieces(3, AT_LAST_CODES, AT_LAST_PLANES)
         relu(1, 1)
         late_differences(1)
-        quantise_wu(0, 0, round_on_gpsimd(wu_raw[0][:, :, 0:P], "old_late0"), old_slot(1, 1, 0))
+        quantise_wu(0, 0, round_on_gpsimd(wu_raw[0][:, :, 0:P], "grouped_first1"), old_slot(1, 1, 0))
         quantise_wu(0, 3, round_on_scalar(wu_raw[0][:, :, 3 * P : N], "w1_codes%d_1_1" % LAST), AT_OLD5 + PASS)
         wu_middle = round_on_gpsimd(wu_raw[0][:, :, P : 3 * P], "w1_codes%d_1_1" % LAST)
 
@@ -483,7 +486,7 @@ def tile_list_redline_pair_features_kernel(
             quantise_z(0, halves[e], round_on_scalar(z_early[:, :, halves[e]], (AT_EARLY0, AT_EARLY1)[e]))
             second_pass(0, e, opens=True)
         for e in range(2):
-            round_into(wu_last[:, e * PASS : (e + 1) * PASS], wu_tail[e], nc.scalar.copy)
+            round_into(wu_last[:, e * PASS : (e + 1) * PASS], wu_tail[e])
             for t in last_pair:
                 pick_new(1, t, e, old_last[t][:, halves[e]], z_late[e][:, t, :])
         quantise_wu(1, 0, round_on_scalar(wu_head[:], AT_WU_FIRST), old_slot(1, 1, 1))

@@ -25,6 +25,8 @@ PASS = P * PACK
 BANK = 512
 LIST_ROWS = 16
 ALIGN = 64
+DMA_ALIGN = 256
+LOAD_SLOTS = ("tab", "w1_raw", "old3")
 K_PASSES = K // PASS
 R_PASSES = H // PASS
 LAST = K_PASSES - 1
@@ -64,8 +66,10 @@ def tile_list_redline_pair_features_kernel(
         def held(shape, dtype, slot):
             if isinstance(slot, int):
                 placed_tiles.append(slot)
-                return placed.tile(shape, dtype, name="placed%d" % len(placed_tiles), align_bytes=ALIGN, offset=slot)
-            return keep.tile(shape, dtype, name=slot, align_bytes=ALIGN)
+                align = DMA_ALIGN if slot % DMA_ALIGN == 0 else ALIGN
+                return placed.tile(shape, dtype, name="placed%d" % len(placed_tiles), align_bytes=align, offset=slot)
+            align = DMA_ALIGN if slot.startswith(LOAD_SLOTS) else ALIGN
+            return keep.tile(shape, dtype, name=slot, align_bytes=align)
 
         def bank(index):
             return psum.tile([P, BANK], F32, name="bank%d" % index)

from contextlib import ExitStack

import concourse.mybir as mybir

K, H, N, T, S, M, M2 = 1536, 1024, 512, 2048, 1024, 512, 256
FLOPS = 2 * K * H * S + 2 * 2 * H * N * M

F32 = mybir.dt.float32
BF16 = mybir.dt.bfloat16
I32 = mybir.dt.int32
U32 = mybir.dt.uint32
U16 = mybir.dt.uint16
U8 = mybir.dt.uint8
FP8X4 = mybir.dt.float8_e4m3fn_x4
FP4X4 = mybir.dt.float4_e2m1fn_x4
ACT = mybir.ActivationFunctionType
ALU = mybir.AluOpType

P = 128
SIDE = P // 2
QUADRANT = 32
PLANE_ROWS = 4
PACK = 4
PASS = P * PACK
BANK = 512
LIST_ROWS = 16
ALIGN = 64
DMA_ALIGN = 256
LOAD_SLOTS = ("tab", "w1_raw", "old3")
K_PASSES = K // PASS
R_PASSES = H // PASS
LAST = K_PASSES - 1
PAIR_COLS = 2 * P
MH = M // 2
N_TILES = N // P
NH = N // 2
BIAS_RUN = 3
GROUPED_BYTES = PAIR_COLS * PACK * 2
H_BYTES = S * 4
RAW_BYTES = PACK * PASS * 4
AT_RAW1 = 0
AT_RAW2 = AT_RAW1 + RAW_BYTES + H_BYTES
AT_H3 = AT_RAW2 + RAW_BYTES
AT_LAST_LIN = AT_H3 + H_BYTES + GROUPED_BYTES
AT_EARLY0 = AT_LAST_LIN + GROUPED_BYTES
AT_LAST_PLANES = AT_EARLY0 + GROUPED_BYTES - ALIGN
AT_EARLY1 = AT_LAST_PLANES + ALIGN
AT_WU_LAST = AT_EARLY1 + GROUPED_BYTES
AT_LAST_CODES = AT_WU_LAST + GROUPED_BYTES - PAIR_COLS
AT_WU_FIRST = AT_LAST_CODES + PAIR_COLS
AT_OLD5 = AT_WU_FIRST + GROUPED_BYTES


def tile_list_redline_pair_features_kernel(
    tc, tab_words, tab_scales, offs, pos1, pos2, pos3, pos4, w1, b1, wg_words, wg_scales, wu, out
):
    nc = tc.nc

    with ExitStack() as ctx:
        keep = ctx.enter_context(tc.tile_pool(name="keep", bufs=1))
        placed = ctx.enter_context(tc.tile_pool(name="placed", bufs=1))
        psum = ctx.enter_context(tc.psum_pool(name="psum", bufs=1))

        placed_tiles = []

        def held(shape, dtype, slot):
            if isinstance(slot, int):
                placed_tiles.append(slot)
                align = DMA_ALIGN if slot % DMA_ALIGN == 0 else ALIGN
                return placed.tile(shape, dtype, name="placed%d" % len(placed_tiles), align_bytes=align, offset=slot)
            align = DMA_ALIGN if slot.startswith(LOAD_SLOTS) else ALIGN
            return keep.tile(shape, dtype, name=slot, align_bytes=align)

        def bank(index):
            return psum.tile([P, BANK], F32, name="bank%d" % index)

        tab_planes = held([P, T], U8, "tab_planes")
        nc.vector.memset(tab_planes[:].bitcast(I32), 0)

        wg_planes = held([P, R_PASSES * N], U8, "wg_planes")
        nc.vector.memset(wg_planes[:].bitcast(I32), 0)

        tab, w1_raw, wu_raw, bias_col = {}, {}, {}, {}

        def load_list(src, name):
            offsets = keep.tile(list(src.shape), U16, name=name)
            nc.sync.dma_start(offsets[:], src)
            return offsets

        def load_tab(a):
            tab[a] = held([P, T], I32, "tab%d" % a)
            nc.sync.dma_start(tab[a][:], tab_words[a].rearrange("p c j -> p (c j)").bitcast(I32))

        def raw_slot(a, first_col):
            return "w1_raw_%d_%d" % (a, first_col)

        def load_w1(a, first_col, width, slot=None):
            raw = held([P, PACK, width], F32, raw_slot(a, first_col) if slot is None else slot)
            rows = w1[a * PASS : (a + 1) * PASS, first_col : first_col + width]
            nc.sync.dma_start(raw[:], rows.rearrange("(p j) c -> p j c", j=PACK))
            w1_raw[a, first_col] = raw

        def load_wu(b, slot):
            wu_raw[b] = held([P, PACK, N], F32, slot)
            nc.sync.dma_start(wu_raw[b][:], wu[b * PASS : (b + 1) * PASS, :].rearrange("(p j) c -> p j c", j=PACK))

        def load_wg_planes(quad):
            rows = wg_planes[QUADRANT * quad : QUADRANT * quad + PLANE_ROWS, :]
            nc.sync.dma_start(
                rows.bitcast(I32).rearrange("s (b c) -> s b c", b=R_PASSES),
                wg_scales[:, PLANE_ROWS * quad : PLANE_ROWS * (quad + 1), :].rearrange("b s c -> s b c").bitcast(I32),
            )

        b1_early = b1[0:PASS].rearrange("(d w x) -> w d x", d=2, x=PACK)

        def load_bias_of_first_pair():
            runs = held([P, BIAS_RUN], F32, "bias_first")
            for side in range(2):
                nc.sync.dma_start(runs[SIDE * side : SIDE * (side + 1), :], b1_early[:, 0, side : side + BIAS_RUN])
            for u in range(2):
                bias_col[0, u] = runs[:, 2 * u : 2 * u + 1]

        def load_bias_of_tile(t):
            u = t - 2
            col = held([P, 1], F32, "bias%d" % t)
            nc.sync.dma_start(col[:], b1_early[:, 1, 2 * u : 2 * u + 2])
            bias_col[0, t] = col[:]

        for quad in range(P // QUADRANT):
            queue = nc.sync if quad % 2 == 0 else nc.scalar
            queue.dma_start(
                tab_planes[QUADRANT * quad : QUADRANT * quad + PLANE_ROWS * K_PASSES, :].bitcast(I32),
                tab_scales[:, PLANE_ROWS * quad : PLANE_ROWS * (quad + 1), :].bitcast(I32),
            )

        warm_in = held([P, 1], F32, "warm_in")
        nc.vector.memset(warm_in[:], 0.0)
        warm_out = held([P, 1], F32, "warm_out")
        nc.scalar.activation(warm_out[:], warm_in[:], ACT.Silu)

        offs_t = load_list(offs, "offs_t")
        for a in range(K_PASSES):
            load_tab(a)
            load_w1(a, 0, PAIR_COLS)
            if a == 1:
                load_bias_of_first_pair()
        load_w1(0, PAIR_COLS, PAIR_COLS)
        pos1_t = load_list(pos1, "pos1_t")
        load_w1(1, PAIR_COLS, PAIR_COLS)
        pos2_t = load_list(pos2, "pos2_t")
        load_w1(2, PAIR_COLS, PAIR_COLS)
        load_w1(0, PASS, PASS)
        load_bias_of_tile(2)
        load_w1(1, PASS, PASS, slot=AT_RAW1)
        load_bias_of_tile(3)
        load_w1(2, PASS, PASS, slot=AT_RAW2)
        b1_late = b1[PASS : 2 * PASS].rearrange("(p t) -> p t", t=PACK)
        bias_late = held([P, PACK], F32, "bias_late")
        nc.sync.dma_start(bias_late[:], b1_late)
        for t in range(PACK):
            bias_col[1, t] = bias_late[:, t : t + 1]
        load_wu(0, "tab0")

        v_words, w1_codes, w1_planes, h_acc, h = {}, {}, {}, {}, {}

        def gather_words(a, slot):
            v_words[a] = held([P, S], U32, slot)
            nc.vector.tensor_copy(v_words[a][:], tab[a][:].bitcast(U32).indirect(offs_t[:]))

        def round_on_gpsimd_into(out_view, in_view):
            nc.gpsimd.tensor_scalar(out_view, in_view, 1.0, 0.0, ALU.mult, ALU.add)

        def grouped_tile(slot):
            return held([P, PAIR_COLS * PACK], BF16, slot)

        def round_first_pair(a, grouped, u=None):
            src = w1_raw[a, 0][:].rearrange("p j (w u side) -> p u w j side", u=2, side=2)
            if u is None:
                nc.scalar.copy(grouped[:].rearrange("p (u side w j) -> p u w j side", u=2, side=2, j=PACK), src)
            else:
                nc.scalar.copy(grouped[:].rearrange("p (side w j) -> p w j side", side=2, j=PACK), src[:, u, :, :, :])

        def round_second_pair(a, grouped, u=None, on_gpsimd=False):
            raw = w1_raw[a, PAIR_COLS][:]
            if u is None:
                nc.scalar.copy(
                    grouped[:].rearrange("p (u w side j) -> p u w j side", u=2, side=2, j=PACK),
                    raw.rearrange("p j (w u side) -> p u w j side", u=2, side=2),
                )
            elif on_gpsimd:
                round_on_gpsimd_into(
                    grouped[:].rearrange("p (w side j) -> p w side j", side=2, j=PACK),
                    raw.rearrange("p j (w u side) -> p u w side j", u=2, side=2)[:, u, :, :, :],
                )
            else:
                nc.scalar.copy(
                    grouped[:].rearrange("p (w side j) -> p w j side", side=2, j=PACK),
                    raw.rearrange("p j (w u side) -> p u w j side", u=2, side=2)[:, u, :, :, :],
                )

        def round_late_pair(a, d, grouped):
            nc.scalar.copy(
                grouped[:].rearrange("p (t w j) -> p w j t", t=2, j=PACK),
                w1_raw[a, PASS][:].rearrange("p j (w t) -> p w j t", t=PACK)[:, :, :, 2 * d : 2 * d + 2],
            )

        def quantise_w1(a, b, tiles, grouped):
            width = P * len(tiles)
            tag = "%d_%d_%d" % (a, b, tiles[0])
            codes = held([P, width], U32, "w1_codes" + tag)
            planes = held([P, width], U8, "w1_planes" + tag)
            nc.vector.quantize_mx(out=codes[:].bitcast(FP8X4), scales=planes[:], in_=grouped[:, :])
            for n, t in enumerate(tiles):
                w1_codes[a, b, t] = codes[:, n * P : (n + 1) * P]
                w1_planes[a, b, t] = planes[:, n * P : (n + 1) * P]

        def h_pass(a, b, tiles, opening=0, closing=LAST):
            for t in tiles:
                for half in range(S // BANK):
                    if a == opening:
                        h_acc[b, t, half] = bank(2 * t + half)
                    cols = slice(half * BANK, (half + 1) * BANK)
                    nc.tensor.matmul_mx(
                        out=h_acc[b, t, half][:],
                        lhsT=w1_codes[a, b, t].bitcast(FP8X4),
                        lhsT_scale=w1_planes[a, b, t],
                        rhs=v_words[a][:, cols].bitcast(FP8X4),
                        rhs_scale=v_planes[PLANE_ROWS * a : P, cols],
                        start=(a == opening),
                        stop=(a == closing),
                    )

        def last_pass_by_tiles(b, tiles, grouped):
            for n, t in enumerate(tiles):
                quantise_w1(LAST, b, (t,), grouped[:, n * PASS : (n + 1) * PASS])
                h_pass(LAST, b, (t,))

        def relu(b, t, slot=None, shared=False, banks=(0, 1)):
            if banks[0] == 0:
                h[b, t] = held([P, S], F32, "h%d_%d" % (b, t) if slot is None else slot)
            for half in banks:
                dst = h[b, t][:, half * BANK : (half + 1) * BANK]
                if shared and half == 0:
                    nc.vector.tensor_scalar(dst, h_acc[b, t, half][:], bias_col[b, t], 0.0, ALU.add, ALU.max)
                else:
                    nc.scalar.activation(dst, h_acc[b, t, half][:], ACT.Relu, bias=bias_col[b, t])

        z_early_slot = raw_slot(1, PAIR_COLS)
        z_early = held([P, PACK, M], F32, z_early_slot)
        z_late_slots = (AT_RAW1 + H_BYTES - ALIGN, AT_RAW1 + 2 * H_BYTES - ALIGN)
        z_late_flat = [held([P, PACK * MH], F32, slot) for slot in z_late_slots]
        z_late = [flat[:].rearrange("p (j m) -> p j m", j=PACK) for flat in z_late_flat]
        halves = [slice(e * MH, (e + 1) * MH) for e in range(2)]

        def half_list(offsets, e):
            return offsets[:, e * MH // LIST_ROWS : (e + 1) * MH // LIST_ROWS]

        def old_slot(b, t, e):
            if (b, t, e) == (1, 0, 0):
                return AT_LAST_CODES
            if (b, t, e) == (1, 1, 0):
                return AT_OLD5
            return ("old%d_%d" if b == 0 else "old_late%d_%d") % (t, e)

        def pick_old(b, t, e, old):
            nc.vector.tensor_copy(old, h[b, t][:].indirect(half_list(pos1_t, e)))

        def pick_new(b, t, e, old, dst):
            nc.vector.tensor_tensor(dst, h[b, t][:].indirect(half_list(pos2_t, e)), old, ALU.subtract)

        def differences_by_halves(b, t, dst):
            old = [held([P, MH], F32, old_slot(b, t, e)) for e in range(2)]
            for e in range(2):
                pick_old(b, t, e, old[e][:])
            for e in range(2):
                pick_new(b, t, e, old[e][:], dst[e])

        def move_early(t, z_tile):
            d, u = divmod(t, 2)
            if d == 0:
                nc.sync.dma_start(z_early[0:SIDE, 2 * u + 1, :], z_tile[SIDE:P, :])
            else:
                for side in range(2):
                    nc.sync.dma_start(z_early[SIDE:P, 2 * u + side, :], z_tile[side:P:2, :])

        def late_differences(t):
            differences_by_halves(1, t, [z_late[e][:, t, :] for e in range(2)])

        def round_into(grouped, src):
            nc.scalar.copy(
                grouped.rearrange("p (c x j) -> p c j x", x=2, j=PACK),
                src.rearrange("p j (c x) -> p c j x", x=2),
            )
            return grouped

        z_codes, z_planes, wu_codes, wu_planes = {}, {}, {}, {}
        for b in range(R_PASSES):
            z_codes[b] = held([P, M], U32, "z_codes%d" % b)
            z_planes[b] = held([P, M], U8, "z_planes%d" % b)

        def quantise_z(b, changes, grouped):
            nc.vector.quantize_mx(out=z_codes[b][:, changes].bitcast(FP8X4), scales=z_planes[b][:, changes], in_=grouped)

        def round_on_gpsimd(src, slot):
            grouped = held([P, src.shape[2] * PACK], BF16, slot)[:]
            by_column = grouped.rearrange("p (c j) -> p c j", j=PACK)
            nc.gpsimd.tensor_scalar(by_column, src.rearrange("p j c -> p c j"), 1.0, 0.0, ALU.mult, ALU.add)
            return grouped

        def round_on_scalar(src, slot):
            return round_into(held([P, src.shape[2] * PACK], BF16, slot)[:], src)

        def quantise_wu(b, first_tile, grouped, codes_slot, planes_slot=None):
            width = grouped.shape[1] // PACK
            codes = held([P, width], U32, codes_slot)
            planes = held([P, width], U8, planes_slot or "wu_planes%d_%d" % (b, first_tile))
            nc.vector.quantize_mx(out=codes[:].bitcast(FP8X4), scales=planes[:], in_=grouped)
            for n in range(width // P):
                wu_codes[b, first_tile + n] = codes[:, n * P : (n + 1) * P]
                wu_planes[b, first_tile + n] = planes[:, n * P : (n + 1) * P]

        first, second, third, fourth = (0, 1), (2, 3), (0, 1), (2, 3)
        for a in range(K_PASSES):
            gather_words(a, "tab_planes" if a == 1 else "v%d" % a)
            if a == 0:
                v_planes = held([P, S], U8, "v_planes")
                nc.vector.tensor_copy(v_planes[:], tab_planes[:].indirect(offs_t[:]))
            if a < LAST:
                grouped = grouped_tile("grouped_first%d" % a)
                round_first_pair(a, grouped)
                quantise_w1(a, 0, first, grouped)
                h_pass(a, 0, first)
        for u in range(2):
            grouped = held([P, PASS], BF16, "grouped_tile%d" % u)
            round_first_pair(LAST, grouped, u)
            quantise_w1(LAST, 0, (u,), grouped)
            h_pass(LAST, 0, (u,))

        def second_tile_weights(a, u, slot):
            grouped = held([P, PASS], BF16, slot)
            round_second_pair(a, grouped, u, on_gpsimd=(u == 1))
            return grouped

        def second_tile_pass(a, u, grouped):
            quantise_w1(a, 0, (2 + u,), grouped)
            h_pass(a, 0, (2 + u,))

        grouped = grouped_tile("grouped_second0")
        round_second_pair(0, grouped)
        relu(0, 0, shared=True)
        quantise_w1(0, 0, second, grouped)
        h_pass(0, 0, second)
        pass1 = [second_tile_weights(1, 0, "w1_planes%d_0_0" % LAST), second_tile_weights(1, 1, "grouped_second0")]
        old = held([P, M], F32, raw_slot(0, PAIR_COLS))
        nc.vector.tensor_copy(old[:], h[0, 0][:].indirect(pos1_t[:]))
        for u in range(2):
            second_tile_pass(1, u, pass1[u])
        nc.vector.tensor_tensor(z_early[:, 0, :], h[0, 0][:].indirect(pos2_t[:]), old[:], ALU.subtract)
        move_early(0, z_early[:, 0, :])
        relu(0, 1, banks=(0,))
        grouped = grouped_tile("w1_planes%d_0_1" % LAST)
        round_second_pair(LAST, grouped)
        relu(0, 1, banks=(1,))
        last_pass_by_tiles(0, second, grouped)
        old = held([P, M], F32, raw_slot(LAST, PAIR_COLS))
        for e in range(2):
            pick_old(0, 1, e, old[:, halves[e]])
        for e in range(2):
            pick_new(0, 1, e, old[:, halves[e]], z_early[:, 2, halves[e]])
        move_early(1, z_early[:, 2, :])

        def late_weights(a, slot):
            grouped = grouped_tile(slot)
            round_late_pair(a, 0, grouped)
            quantise_w1(a, 1, third, grouped)
            h_pass(a, 1, third)

        def round_fourth_piece(t, half, slot):
            grouped = held([P, PAIR_COLS], BF16, slot)
            words = slice(half * SIDE, (half + 1) * SIDE)
            round_on_gpsimd_into(
                grouped[:].rearrange("p (w j) -> p w j", j=PACK),
                w1_raw[0, PASS][:].rearrange("p j (w t) -> p t w j", t=PACK)[:, t, words, :],
            )
            pieces[t, half] = grouped

        def quantise_fourth_pieces(t, codes_slot, planes_slot):
            codes = held([P, P], U32, codes_slot)
            planes = held([P, P], U8, planes_slot)
            for half in range(2):
                cols = slice(half * SIDE, (half + 1) * SIDE)
                nc.vector.quantize_mx(out=codes[:, cols].bitcast(FP8X4), scales=planes[:, cols], in_=pieces[t, half][:])
            w1_codes[0, 1, t], w1_planes[0, 1, t] = codes[:], planes[:]
            h_pass(0, 1, (t,), opening=LAST, closing=closing_pass[t])

        pieces = {}
        closing_pass = {2: 1, 3: 0}
        round_fourth_piece(2, 0, "w1_planes%d_0_1" % LAST)
        late_weights(0, "grouped_first1")
        round_fourth_piece(2, 1, "grouped_first1")
        relu(0, 2)
        z_tile = held([P, M], F32, "z_tile2")
        differences_by_halves(0, 2, [z_tile[:, changes] for changes in halves])
        move_early(2, z_tile[:])
        late_weights(1, "w1_planes%d_0_2" % LAST)
        relu(0, 3, slot=AT_H3)
        round_fourth_piece(3, 0, "w1_planes%d_0_2" % LAST)
        old = held([P, M], F32, "old3")
        nc.vector.tensor_copy(old[:], h[0, 3][:].indirect(pos1_t[:]))
        grouped = grouped_tile("grouped_third2")
        round_late_pair(LAST, 0, grouped)
        last_pass_by_tiles(1, third, grouped)
        g_fourth = {1: grouped_tile("w1_planes%d_1_0" % LAST), LAST: grouped_tile("grouped_fourth2")}
        z_tile = held([P, M], F32, "grouped_third2")
        nc.vector.tensor_tensor(z_tile[:], h[0, 3][:].indirect(pos2_t[:]), old[:], ALU.subtract)
        move_early(3, z_tile[:])
        round_late_pair(LAST, 1, g_fourth[LAST])
        quantise_w1(LAST, 1, fourth, g_fourth[LAST])
        h_pass(LAST, 1, fourth, opening=LAST, closing=1)
        quantise_fourth_pieces(2, AT_RAW2, "w1_planes0_1_2")
        round_fourth_piece(3, 1, "grouped_first1")

        wu_rows = wu[PASS : 2 * PASS, :].rearrange("(p j) c -> p j c", j=PACK)
        wg_t = held([P, R_PASSES, 2 * N], U8, AT_H3)
        nc.sync.dma_start(wg_t[:].bitcast(I32), wg_words.rearrange("b p c -> p b c").bitcast(I32))
        wu_head = held([P, PACK, NH], F32, "old3")
        nc.sync.dma_start(wu_head[:], wu_rows[:, :, 0:NH])
        for quad in range(P // QUADRANT):
            load_wg_planes(quad)
        pos3_t = load_list(pos3, "pos3_t")
        pos4_t = load_list(pos4, "pos4_t")

        relu(1, 0)
        old = [held([P, MH], F32, old_slot(1, 0, e)) for e in range(2)]
        for e in range(2):
            pick_old(1, 0, e, old[e][:])
        round_late_pair(1, 1, g_fourth[1])
        quantise_w1(1, 1, fourth, g_fourth[1])
        for t in fourth:
            h_pass(1, 1, (t,), opening=LAST, closing=closing_pass[t])
        wu_tail = []
        for e in range(2):
            parked = z_late_flat[e][:, 2 * MH : PACK * MH].rearrange("p (j c) -> p j c", j=PACK)
            nc.sync.dma_start(parked, wu_rows[:, :, NH + e * P : NH + (e + 1) * P])
            wu_tail.append(parked)
        for e in range(2):
            pick_new(1, 0, e, old[e][:], z_late[e][:, 0, :])
        quantise_fourth_pieces(3, AT_LAST_CODES, AT_LAST_PLANES)
        relu(1, 1)
        late_differences(1)
        quantise_wu(0, 0, round_on_gpsimd(wu_raw[0][:, :, 0:P], "grouped_first1"), old_slot(1, 1, 0))
        quantise_wu(0, 3, round_on_scalar(wu_raw[0][:, :, 3 * P : N], "w1_codes%d_1_1" % LAST), AT_OLD5 + PASS)
        wu_middle = round_on_gpsimd(wu_raw[0][:, :, P : 3 * P], "w1_codes%d_1_1" % LAST)

        acc = {}
        gate_cols, lin_cols = slice(0, MH), slice(MH, 2 * MH)

        def second_pass(b, e, opens):
            for i in range(N_TILES):
                if opens:
                    acc[e, i] = bank(N_TILES * e + i)
                nc.tensor.matmul_mx(
                    out=acc[e, i][:, gate_cols],
                    lhsT=wg_t[:, b, 2 * i * P : 2 * (i + 1) * P].bitcast(FP4X4),
                    lhsT_scale=wg_planes[:, b * N + i * P : b * N + (i + 1) * P],
                    rhs=z_codes[b][:, halves[e]].bitcast(FP8X4),
                    rhs_scale=z_planes[b][:, halves[e]],
                    start=opens,
                    stop=False,
                )
                nc.tensor.matmul_mx(
                    out=acc[e, i][:, lin_cols],
                    lhsT=wu_codes[b, i].bitcast(FP8X4),
                    lhsT_scale=wu_planes[b, i],
                    rhs=z_codes[b][:, halves[e]].bitcast(FP8X4),
                    rhs_scale=z_planes[b][:, halves[e]],
                    start=False,
                    stop=not opens,
                )

        last_pair = (PACK - 2, PACK - 1)
        old_last = {}
        for t in last_pair:
            relu(1, t)
            old_last[t] = held([P, M], F32, old_slot(1, 1, 1) if t == last_pair[0] else "old_last")
            nc.vector.tensor_copy(old_last[t][:], h[1, t][:].indirect(pos1_t[:]))
        quantise_wu(0, 1, wu_middle, "wu_codes0_1", "bias_late")
        wu_last = held([P, NH * PACK], BF16, AT_WU_LAST)
        for e in range(2):
            quantise_z(0, halves[e], round_on_scalar(z_early[:, :, halves[e]], (AT_EARLY0, AT_EARLY1)[e]))
            second_pass(0, e, opens=True)
        for e in range(2):
            round_into(wu_last[:, e * PASS : (e + 1) * PASS], wu_tail[e])
            for t in last_pair:
                pick_new(1, t, e, old_last[t][:, halves[e]], z_late[e][:, t, :])
        quantise_wu(1, 0, round_on_scalar(wu_head[:], AT_WU_FIRST), old_slot(1, 1, 1))
        quantise_z(1, halves[0], round_on_scalar(z_late[0], "z_first_grouped"))
        z_last_grouped = round_on_scalar(z_late[1], "z_last_grouped")
        quantise_wu(1, 2, wu_last[:], z_late_slots[0])
        second_pass(1, 0, opens=False)
        quantise_z(1, halves[1], z_last_grouped)
        second_pass(1, 1, opens=False)

        y = [held([P, M], F32, "y%d" % i) for i in range(N_TILES)]
        silu, first = {}, {}

        def make_silu(e, i):
            silu[e, i] = held([P, MH], F32, "silu%d_%d" % (e, i))
            nc.scalar.activation(silu[e, i][:], acc[e, i][:, gate_cols], ACT.Silu)

        def make_y(e, i):
            nc.vector.tensor_tensor(y[i][:, halves[e]], acc[e, i][:, lin_cols], silu[e, i][:], ALU.mult)

        def make_y_on_gpsimd(e, i):
            lin = held([P, MH], F32, AT_LAST_LIN if i == N_TILES - 1 else "lin%d_%d" % (e, i))
            nc.scalar.copy(lin[:], acc[e, i][:, lin_cols])
            nc.gpsimd.tensor_tensor(y[i][:, halves[e]], lin[:], silu[e, i][:], ALU.mult)

        def pick_first(i):
            first[i] = held([P, M2], F32, "first%d" % i)
            nc.vector.tensor_copy(first[i][:], y[i][:].indirect(pos3_t[:]))

        def add_second_and_store(i, slot):
            result = held([P, M2], F32, slot)
            nc.vector.tensor_tensor(result[:], y[i][:].indirect(pos4_t[:]), first[i][:], ALU.add)
            nc.sync.dma_start(out[i * P : (i + 1) * P, :], result[:])

        for i in range(N_TILES):
            make_silu(0, i)
            make_y(0, i)
        for i in range(N_TILES):
            make_silu(1, i)
            if i < N_TILES // 2:
                make_y(1, i)
            else:
                make_y_on_gpsimd(1, i)
        for i in range(N_TILES):
            pick_first(i)
        last = N_TILES - 1
        result_slots = ("silu1_%d" % last, AT_LAST_LIN - M2 * 2, AT_LAST_LIN + M2 * 2, "result3")
        for i in range(N_TILES):
            add_second_and_store(i, result_slots[i])
